import numpy as np
import ml_dtypes


def mxq(x, axis, fmt="e4m3"):
    dtype, down = {"e4m3": (ml_dtypes.float8_e4m3fn, 7), "e5m2": (ml_dtypes.float8_e5m2, 14)}[fmt]
    v = np.moveaxis(np.asarray(x, np.float32).astype(ml_dtypes.bfloat16).astype(np.float64), axis, -1)
    blocks = v.reshape(v.shape[:-1] + (-1, 32))
    amax = np.abs(blocks).max(-1, keepdims=True)
    byte = np.maximum(np.where(amax > 0, np.frexp(amax)[1] - 1 + 127, 0) - down, 1)
    scale = np.exp2(byte - 127.0)
    codes = (blocks / scale).astype(np.float32).astype(dtype).astype(np.float64)
    return np.moveaxis((codes * scale).reshape(v.shape), -1, axis)


WIDE = False


def mx_kscale(k):
    if not WIDE:
        return np.ones(k)
    levels = np.array([10, -10, 5, -5, 0])
    if k % 512:
        return np.exp2(np.random.permutation(np.resize(levels, k // 32))).repeat(32)
    a = np.empty((k // 512, 16))
    for p in range(k // 512):
        a[p, :8] = np.random.permutation(np.resize(levels, 8))
        for g in range(8):
            far = levels[np.abs(levels - a[p, g]) >= 10]
            a[p, g + 8] = far[np.random.randint(len(far))]
    return np.exp2(a.ravel()).repeat(32)


def f64(x):
    return np.asarray(x).astype(np.float64)


def striped(idx):
    return np.tile(idx.reshape(-1, 16).T, (8, 1)).astype(np.uint16)


def unstriped(offs):
    return offs[:16].T.reshape(-1).astype(np.int64)


E2M1 = np.array([0.0, 0.5, 1.0, 1.5, 2.0, 3.0, 4.0, 6.0, -0.0, -0.5, -1.0, -1.5, -2.0, -3.0, -4.0, -6.0])


def pack_weight(w, fmt):
    k, n = w.shape
    w = f64(np.asarray(w, np.float32).astype(ml_dtypes.bfloat16)).reshape(k // 32, 32, n)
    amax = np.abs(w).max(1)
    if fmt == "e4m3":
        byte = np.frexp(amax)[1] - 1 + 127 - 7
    else:
        mant, ex = np.frexp(amax / 6.0)
        byte = np.where(mant > 0.5, ex, ex - 1) + 127
    byte = np.clip(np.where(amax > 0, byte, 1), 1, 254)
    scaled = (w * np.exp2(127.0 - byte)[:, None, :]).reshape(k, n).astype(np.float32)
    by_word = np.ascontiguousarray(scaled.reshape(k // 512, 128, 4, n).transpose(0, 1, 3, 2))
    if fmt == "e4m3":
        words = by_word.astype(ml_dtypes.float8_e4m3fn).view(np.uint8)
    else:
        c = by_word.astype(ml_dtypes.float4_e2m1fn).view(np.uint8) & 0xF
        words = (c[..., 0::2] | (c[..., 1::2] << 4)).reshape(k // 512, 128, 2 * n)
    return np.ascontiguousarray(words), np.ascontiguousarray(byte.astype(np.uint8).reshape(k // 512, 16, n))


def unpack_weight(words, scales, fmt):
    g, _, n = scales.shape
    words = np.ascontiguousarray(words).reshape(g, 128, n, -1)
    if fmt == "e4m3":
        vals = words.view(ml_dtypes.float8_e4m3fn).astype(np.float64)
    else:
        nib = np.empty((g, 128, n, 4), np.uint8)
        nib[..., 0::2] = words & 0xF
        nib[..., 1::2] = words >> 4
        vals = E2M1[nib]
    vals = vals * np.repeat(np.exp2(scales.astype(np.float64) - 127.0), 8, axis=1)[..., None]
    return vals.transpose(0, 1, 3, 2).reshape(g * 512, n)


def gelu(v):
    return 0.5 * v * (1.0 + np.tanh(np.sqrt(2.0 / np.pi) * (v + 0.044715 * v**3)))


def striped8(idx):
    return np.concatenate([v.reshape(-1, 16).T for v in idx]).astype(np.uint16)


def unstriped8(offs):
    return np.stack([offs[16 * g:16 * g + 16].T.reshape(-1) for g in range(8)]).astype(np.int64)


def runs(v, idx8):
    k = np.arange(v.shape[0])
    return v[k[:, None], idx8[k % 512 // 64]]


K, K2, T, S, H, N = 1024, 512, 2048, 1024, 512, 256

def setup_inputs():
    n = np.random.standard_normal
    s = mx_kscale(K)[:, None]
    s2 = mx_kscale(K2)[:, None]
    u = mx_kscale(H)[:, None]
    tab_words, tab_scales = pack_weight(n((K, T)) * s, "e4m3")
    tab2_words, tab2_scales = pack_weight(n((K2, T)) * s2, "e4m3")
    w4_words, w4_scales = pack_weight(0.35 * n((K, H)) / np.sqrt(K) / s, "e2m1")
    w8_words, w8_scales = pack_weight(0.35 * n((K2, H)) / np.sqrt(K2) / s2, "e4m3")
    return {
        "tab_words": tab_words, "tab_scales": tab_scales,
        "tab2_words": tab2_words, "tab2_scales": tab2_scales,
        "offs": striped8(np.stack([np.random.permutation(T)[:S] for _ in range(8)])),
        "offs2": striped(np.random.permutation(T)[:S]),
        "w4_words": w4_words, "w4_scales": w4_scales,
        "w8_words": w8_words, "w8_scales": w8_scales,
        "wd": (0.35 * n((K2, H)) / np.sqrt(K2) / s2).astype(np.float32),
        "wr": (0.35 * n((K, H)) / np.sqrt(K) / s).astype(np.float32),
        "gain": (2.0 * np.exp(0.3 * n(H)) * u[:, 0]).astype(np.float32),
        "w2": (n((H, N)) / np.sqrt(H) / u).astype(np.float32),
        "shift": (0.5 * n(N)).astype(np.float32),
    }

def reference(tab_words, tab_scales, tab2_words, tab2_scales, offs, offs2, w4_words, w4_scales,
              w8_words, w8_scales, wd, wr, gain, w2, shift):
    v = runs(unpack_weight(tab_words, tab_scales, "e4m3"), unstriped8(offs))
    v2 = unpack_weight(tab2_words, tab2_scales, "e4m3")[:, unstriped(offs2)]
    w4 = unpack_weight(w4_words, w4_scales, "e2m1")
    w8 = unpack_weight(w8_words, w8_scales, "e4m3")
    total = w4.T @ v + mxq(f64(wd), 0, "e4m3").T @ v2
    diff = (mxq(f64(wr), 0, "e4m3").T @ v) - (w8.T @ v2)
    h = np.sin(total) * np.cos(diff) * f64(gain)[:, None]
    y = mxq(f64(w2), 0, "e4m3").T @ mxq(h, 0, "e4m3")
    return y + f64(shift)[:, None]

@@ -1,0 +1,223 @@
+import math
+from contextlib import ExitStack
+
+import concourse.mybir as mybir
+
+K, K2, T, S, H, N = 1024, 512, 2048, 1024, 512, 256
+FLOPS = 2 * S * H * (2 * K + 2 * K2) + 2 * S * H * N
+
+F32 = mybir.dt.float32
+BF16 = mybir.dt.bfloat16
+I32 = mybir.dt.int32
+U32 = mybir.dt.uint32
+U16 = mybir.dt.uint16
+U8 = mybir.dt.uint8
+FP8X4 = mybir.dt.float8_e4m3fn_x4
+FP4X4 = mybir.dt.float4_e2m1fn_x4
+ACT = mybir.ActivationFunctionType
+ALU = mybir.AluOpType
+
+P = 128
+HALF = 512
+TAB_AT, W4_AT, TAB2_AT, W8_AT, STAGED = 0, S, S + H, 2 * S + H, 2 * S + 2 * H
+
+
+def tile_list_coldchain_spoilage_scores_kernel(
+    tc, tab_words, tab_scales, tab2_words, tab2_scales, offs, offs2,
+    w4_words, w4_scales, w8_words, w8_scales, wd, wr, gain, w2, shift, out,
+):
+    nc = tc.nc
+    with ExitStack() as ctx:
+        keep = ctx.enter_context(tc.tile_pool(name="keep", bufs=1))
+        ring = ctx.enter_context(tc.tile_pool(name="ring", bufs=4))
+        psum = ctx.enter_context(tc.psum_pool(name="psum", bufs=2))
+
+        def held(name, shape, dtype):
+            return keep.tile(shape, dtype, name=name, align_bytes=64)
+
+        lists = held("lists", [P, S // 16], U16)
+        list2 = held("list2", [P, S // 16], U16)
+        nc.sync.dma_start(lists[:], offs)
+        nc.sync.dma_start(list2[:], offs2)
+
+        warm = held("warm", [P, 2], F32)
+        nc.vector.memset(warm[:, 0:1], 0.0)
+        nc.scalar.activation(warm[:, 1:2], warm[:, 0:1], ACT.Sin)
+
+        tab_rows = held("tab_rows", [P, T], U8)
+        tab2_rows = held("tab2_rows", [P, T], U8)
+        w4_rows = held("w4_rows", [P, H], U8)
+        w8_rows = held("w8_rows", [P, H], U8)
+        planes = held("planes", [P, 2, STAGED], U8)
+        for tile in (tab_rows, tab2_rows, w4_rows, w8_rows):
+            nc.vector.memset(tile[:].bitcast(I32), 0)
+        nc.vector.memset(planes[:].rearrange("p a c -> p (a c)").bitcast(I32), 0)
+        nc.scalar.dma_start(tab_rows[0:P:4, :].bitcast(I32), tab_scales.bitcast(I32).rearrange("a q t -> q a t"))
+        nc.scalar.dma_start(tab2_rows[0:P:8, :].bitcast(I32), tab2_scales[0].bitcast(I32))
+        nc.scalar.dma_start(w4_rows[0:P:4, :].bitcast(I32), w4_scales.bitcast(I32).rearrange("a q c -> q a c"))
+        nc.scalar.dma_start(w8_rows[0:P:8, :].bitcast(I32), w8_scales[0].bitcast(I32))
+
+        def load_rows(name, rows):
+            raw = held(name, [P, 4, H], F32)
+            nc.sync.dma_start(raw[:], rows.rearrange("(p j) c -> p j c", j=4))
+            return raw
+
+        def load_words(name, words):
+            tile = held(name, [P, words.shape[1]], I32)
+            nc.sync.dma_start(tile[:], words.rearrange("p n i -> p (n i)").bitcast(I32))
+            return tile
+
+        wr0_raw = load_rows("wr0_raw", wr[0:512, :])
+        w8_raw = load_words("w8_raw", w8_words[0])
+        w4_raw = held("w4_raw", [P, 2, H // 2], I32)
+        nc.sync.dma_start(w4_raw[:], w4_words.bitcast(I32).rearrange("a p c -> p a c"))
+        wd_raw = load_rows("wd_raw", wd)
+        tab2_tile = load_words("tab2_tile", tab2_words[0])
+        wr1_raw = load_rows("wr1_raw", wr[512:1024, :])
+        tab_tiles = [load_words("tab_tile%d" % a, tab_words[a]) for a in range(2)]
+        w2_raw = held("w2_raw", [P, 4, N], F32)
+        w2_by_slot = w2.rearrange("(q t i) n -> t q i n", t=4, i=8)
+        for t in range(4):
+            nc.sync.dma_start(w2_raw[:, t, :], w2_by_slot[t])
+        gains = held("gains", [P, 4, 8], F32)
+        shifts = held("shifts", [P, N // P], F32)
+        with nc.allow_non_contiguous_dma(reason="one value a partition"):
+            for t in range(4):
+                nc.sync.dma_start(gains[:, t, 0:1], gain.rearrange("(q t i o) -> t q i o", t=4, i=8, o=1)[t])
+            nc.sync.dma_start(shifts[:], shift.rearrange("(c p) -> p c", p=P))
+
+        tab_picked = held("tab_picked", [P, S], U8)
+        tab2_picked = held("tab2_picked", [P, S], U8)
+        staged = held("staged", [P, STAGED], U8)
+        nc.vector.tensor_copy(tab_picked[:], tab_rows[:].indirect(lists[:]))
+        nc.vector.tensor_copy(tab2_picked[:], tab2_rows[:].indirect(list2[:]))
+        nc.vector.tensor_copy(staged[:, TAB_AT : TAB_AT + S].bitcast(I32), tab_picked[:].bitcast(I32))
+        for rows, at in ((w4_rows, W4_AT), (w8_rows, W8_AT)):
+            nc.vector.tensor_copy(
+                staged[:, at : at + H].bitcast(I32).rearrange("p (t q w) -> p t q w", t=4, w=2),
+                rows[:].bitcast(I32).rearrange("p (q t w) -> p t q w", t=4, w=2),
+            )
+        nc.vector.tensor_copy(staged[:, TAB2_AT : TAB2_AT + S].bitcast(I32), tab2_picked[:].bitcast(I32))
+        for d in range(4):
+            nc.gpsimd.dma_start(
+                planes[32 * d : 32 * d + 4, :, :].bitcast(I32),
+                staged[32 * d : 32 * d + 32 : 4, :].bitcast(I32),
+            )
+
+        w8_codes = held("w8_codes", [P, H], I32)
+        nc.vector.tensor_copy(
+            w8_codes[:].rearrange("p (t q w) -> p t q w", t=4, w=8),
+            w8_raw[:].rearrange("p (q t w) -> p t q w", t=4, w=8),
+        )
+        w4_codes = held("w4_codes", [P, 2, H // 2], I32)
+        nc.vector.tensor_copy(
+            w4_codes[:].rearrange("p a (t q w) -> p a t q w", t=4, w=4),
+            w4_raw[:].rearrange("p a (q t w) -> p a t q w", t=4, w=4),
+        )
+
+        def quantise_weight(name, raw):
+            grouped = held(name + "_bf16", [P, 4 * H], BF16)
+            nc.scalar.copy(
+                grouped[:].rearrange("p (t q i j) -> p t q i j", t=4, i=8, j=4),
+                raw[:].rearrange("p j (q t i) -> p t q i j", t=4, i=8),
+            )
+            codes = held(name + "_codes", [P, H], U32)
+            scales = held(name + "_scales", [P, H], U8)
+            nc.vector.quantize_mx(out=codes[:].bitcast(FP8X4), scales=scales[:], in_=grouped[:])
+            return codes, scales
+
+        def pick_words(name, table, offsets, half):
+            picked = held(name, [P, HALF], U32)
+            cols = slice(half * HALF // 16, (half + 1) * HALF // 16)
+            nc.vector.tensor_copy(picked[:], table[:].bitcast(U32).indirect(offsets[:, cols]))
+            return picked
+
+        wr_q = [quantise_weight("wr0", wr0_raw)]
+        wd_q = quantise_weight("wd", wd_raw)
+        v2 = [pick_words("v2_%d" % half, tab2_tile, list2, half) for half in range(2)]
+        wr_q.append(quantise_weight("wr1", wr1_raw))
+
+        def v_scales(a, half):
+            return planes[:, a, TAB_AT + half * HALF : TAB_AT + (half + 1) * HALF]
+
+        def v2_scales(half):
+            return planes[:, 0, TAB2_AT + half * HALF : TAB2_AT + (half + 1) * HALF]
+
+        depot = {}
+        for half in range(2):
+            for t in range(4):
+                cols = slice(t * P, (t + 1) * P)
+                bank = psum.tile([P, HALF], F32, name="depot_bank")
+                nc.tensor.matmul_mx(
+                    out=bank[:], lhsT=w8_codes[:, cols].bitcast(FP8X4),
+                    lhsT_scale=planes[:, 0, W8_AT + t * P : W8_AT + (t + 1) * P],
+                    rhs=v2[half][:].bitcast(FP8X4), rhs_scale=v2_scales(half), start=True, stop=True,
+                )
+                depot[half, t] = held("depot%d_%d" % (half, t), [P, HALF], F32)
+                nc.scalar.copy(depot[half, t][:], bank[:])
+
+        v = {}
+        for a in range(2):
+            for half in range(2):
+                v[a, half] = pick_words("v%d_%d" % (a, half), tab_tiles[a], lists, half)
+
+        w2_grouped = held("w2_bf16", [P, N, 4], BF16)
+        nc.scalar.copy(w2_grouped[:], w2_raw[:].rearrange("p t n -> p n t"))
+        w2_codes = held("w2_codes", [P, N], U32)
+        w2_scales = held("w2_scales", [P, N], U8)
+        nc.vector.quantize_mx(
+            out=w2_codes[:].bitcast(FP8X4), scales=w2_scales[:], in_=w2_grouped[:].rearrange("p n t -> p (n t)")
+        )
+
+        for half in range(2):
+            h_rows = held("h_rows%d" % half, [P, 4, HALF], BF16)
+            for t in range(4):
+                cols = slice(t * P, (t + 1) * P)
+                route = psum.tile([P, HALF], F32, name="route_bank")
+                for a in range(2):
+                    nc.tensor.matmul_mx(
+                        out=route[:], lhsT=wr_q[a][0][:, cols].bitcast(FP8X4), lhsT_scale=wr_q[a][1][:, cols],
+                        rhs=v[a, half][:].bitcast(FP8X4), rhs_scale=v_scales(a, half), start=(a == 0), stop=(a == 1),
+                    )
+                total = psum.tile([P, HALF], F32, name="total_bank")
+                nc.tensor.matmul_mx(
+                    out=total[:], lhsT=wd_q[0][:, cols].bitcast(FP8X4), lhsT_scale=wd_q[1][:, cols],
+                    rhs=v2[half][:].bitcast(FP8X4), rhs_scale=v2_scales(half), start=True, stop=False,
+                )
+                for a in range(2):
+                    nc.tensor.matmul_mx(
+                        out=total[:], lhsT=w4_codes[:, a, t * P // 2 : (t + 1) * P // 2].bitcast(FP4X4),
+                        lhsT_scale=planes[:, a, W4_AT + t * P : W4_AT + (t + 1) * P],
+                        rhs=v[a, half][:].bitcast(FP8X4), rhs_scale=v_scales(a, half), start=False, stop=(a == 1),
+                    )
+                diff = ring.tile([P, HALF], F32, name="diff")
+                nc.vector.tensor_tensor(diff[:], route[:], depot[half, t][:], ALU.subtract)
+                size = ring.tile([P, HALF], F32, name="size")
+                nc.scalar.activation(size[:], diff[:], ACT.Abs)
+                sine = ring.tile([P, HALF], F32, name="sine")
+                nc.scalar.activation(sine[:], total[:], ACT.Sin)
+                cosine = ring.tile([P, HALF], F32, name="cosine")
+                nc.scalar.activation(cosine[:], size[:], ACT.Sin, bias=math.pi / 2, scale=-1.0)
+                nc.vector.scalar_tensor_tensor(
+                    h_rows[:, t, :], cosine[:], gains[:, t, 0:1], sine[:], ALU.mult, ALU.mult
+                )
+            h_grouped = held("h_grouped%d" % half, [P, HALF, 4], BF16)
+            nc.vector.tensor_copy(h_grouped[:], h_rows[:].rearrange("p t j -> p j t"))
+            h_codes = held("h_codes%d" % half, [P, HALF], U32)
+            h_scales = held("h_scales%d" % half, [P, HALF], U8)
+            nc.vector.quantize_mx(
+                out=h_codes[:].bitcast(FP8X4), scales=h_scales[:], in_=h_grouped[:].rearrange("p j t -> p (j t)")
+            )
+            for c in range(N // P):
+                cols = slice(c * P, (c + 1) * P)
+                scores = psum.tile([P, HALF], F32, name="score_bank")
+                nc.tensor.matmul_mx(
+                    out=scores[:], lhsT=w2_codes[:, cols].bitcast(FP8X4), lhsT_scale=w2_scales[:, cols],
+                    rhs=h_codes[:].bitcast(FP8X4), rhs_scale=h_scales[:], start=True, stop=True,
+                )
+                result = ring.tile([P, HALF], F32, name="result")
+                if c == 0:
+                    nc.scalar.activation(result[:], scores[:], ACT.Identity, bias=shifts[:, c : c + 1])
+                else:
+                    nc.vector.tensor_scalar_add(result[:], scores[:], shifts[:, c : c + 1])
+                nc.sync.dma_start(out[cols, half * HALF : (half + 1) * HALF], result[:])

@@ -19,7 +19,7 @@ ALU = mybir.AluOpType
 
 P = 128
 HALF = 512
-TAB_AT, W4_AT, TAB2_AT, W8_AT, STAGED = 0, S, S + H, 2 * S + H, 2 * S + 2 * H
+CHUNKS = (((0, 512, 1),), ((0, 256, 2), (256, 128, 4), (384, 128, 4)))
 
 
 def tile_list_coldchain_spoilage_scores_kernel(
@@ -29,33 +29,27 @@ def tile_list_coldchain_spoilage_scores_kernel(
     nc = tc.nc
     with ExitStack() as ctx:
         keep = ctx.enter_context(tc.tile_pool(name="keep", bufs=1))
-        ring = ctx.enter_context(tc.tile_pool(name="ring", bufs=4))
-        psum = ctx.enter_context(tc.psum_pool(name="psum", bufs=2))
+        psum = ctx.enter_context(tc.psum_pool(name="psum", bufs=1))
 
         def held(name, shape, dtype):
             return keep.tile(shape, dtype, name=name, align_bytes=64)
 
         lists = held("lists", [P, S // 16], U16)
         list2 = held("list2", [P, S // 16], U16)
-        nc.sync.dma_start(lists[:], offs)
-        nc.sync.dma_start(list2[:], offs2)
-
-        warm = held("warm", [P, 2], F32)
-        nc.vector.memset(warm[:, 0:1], 0.0)
-        nc.scalar.activation(warm[:, 1:2], warm[:, 0:1], ACT.Sin)
-
         tab_rows = held("tab_rows", [P, T], U8)
         tab2_rows = held("tab2_rows", [P, T], U8)
         w4_rows = held("w4_rows", [P, H], U8)
         w8_rows = held("w8_rows", [P, H], U8)
-        planes = held("planes", [P, 2, STAGED], U8)
-        for tile in (tab_rows, tab2_rows, w4_rows, w8_rows):
-            nc.vector.memset(tile[:].bitcast(I32), 0)
+        planes = held("planes", [P, 2, S + H], U8)
+        for rows in (tab_rows, tab2_rows):
+            nc.vector.memset(rows[:, 0 : T // 2].bitcast(I32), 0)
+            nc.gpsimd.memset(rows[:, T // 2 : T].bitcast(I32), 0)
+        for rows in (w4_rows, w8_rows):
+            nc.vector.memset(rows[:].bitcast(I32), 0)
+        warm = held("warm", [P, 2], F32)
+        nc.vector.memset(warm[:, 0:1], 0.0)
+        nc.scalar.activation(warm[:, 1:2], warm[:, 0:1], ACT.Sin)
         nc.vector.memset(planes[:].rearrange("p a c -> p (a c)").bitcast(I32), 0)
-        nc.scalar.dma_start(tab_rows[0:P:4, :].bitcast(I32), tab_scales.bitcast(I32).rearrange("a q t -> q a t"))
-        nc.scalar.dma_start(tab2_rows[0:P:8, :].bitcast(I32), tab2_scales[0].bitcast(I32))
-        nc.scalar.dma_start(w4_rows[0:P:4, :].bitcast(I32), w4_scales.bitcast(I32).rearrange("a q c -> q a c"))
-        nc.scalar.dma_start(w8_rows[0:P:8, :].bitcast(I32), w8_scales[0].bitcast(I32))
 
         def load_rows(name, rows):
             raw = held(name, [P, 4, H], F32)
@@ -67,18 +61,51 @@ def tile_list_coldchain_spoilage_scores_kernel(
             nc.sync.dma_start(tile[:], words.rearrange("p n i -> p (n i)").bitcast(I32))
             return tile
 
-        wr0_raw = load_rows("wr0_raw", wr[0:512, :])
+        def load_plane(rows, scales, quadrants):
+            for d in quadrants:
+                nc.sync.dma_start(rows[32 * d : 32 * d + 4, :].bitcast(I32), scales[4 * d : 4 * d + 4, :].bitcast(I32))
+
+        def move_planes():
+            for d in range(4):
+                nc.sync.dma_start(
+                    planes[32 * d : 32 * d + 4, :, :].bitcast(I32),
+                    staged[32 * d : 32 * d + 32 : 4, :].bitcast(I32),
+                )
+
+        def permute(dst, src, words):
+            nc.vector.tensor_copy(
+                dst.rearrange("p (t q w) -> p t q w", t=4, w=words),
+                src.rearrange("p (q t w) -> p t q w", t=4, w=words),
+            )
+
+        nc.sync.dma_start(lists[:], offs)
+        nc.sync.dma_start(list2[:], offs2)
+        nc.sync.dma_start(tab_rows[0:P:4, :].bitcast(I32), tab_scales.bitcast(I32).rearrange("a q t -> q a t"))
+        raw = {}
+        tab_picked = held("tab_picked", [P, S], U8)
+        tab2_plane = held("tab2_plane", [P, S], U8)
+        staged = held("staged", [P, S + H], U8)
+        nc.vector.tensor_copy(tab_picked[:], tab_rows[:].indirect(lists[:]))
+        load_plane(tab2_rows, tab2_scales[0], (0, 1))
+        raw["wr0"] = load_rows("wr0_raw", wr[0:512, :])
+        load_plane(tab2_rows, tab2_scales[0], (2, 3))
+        raw["wr1"] = load_rows("wr1_raw", wr[512:1024, :])
+        nc.sync.dma_start(w4_rows[0:P:4, :].bitcast(I32), w4_scales.bitcast(I32).rearrange("a q c -> q a c"))
+        load_plane(w8_rows, w8_scales[0], (0, 1))
+        load_plane(w8_rows, w8_scales[0], (2, 3))
         w8_raw = load_words("w8_raw", w8_words[0])
+        tab2_tile = load_words("tab2_tile", tab2_words[0])
+        tab0_tile = load_words("tab0_tile", tab_words[0])
+        nc.vector.tensor_copy(staged[:, 0:S].bitcast(I32), tab_picked[:].bitcast(I32))
+        permute(staged[:, S : S + H].bitcast(I32), w4_rows[:].bitcast(I32), 2)
+        move_planes()
+        tab1_tile = load_words("tab1_tile", tab_words[1])
         w4_raw = held("w4_raw", [P, 2, H // 2], I32)
         nc.sync.dma_start(w4_raw[:], w4_words.bitcast(I32).rearrange("a p c -> p a c"))
-        wd_raw = load_rows("wd_raw", wd)
-        tab2_tile = load_words("tab2_tile", tab2_words[0])
-        wr1_raw = load_rows("wr1_raw", wr[512:1024, :])
-        tab_tiles = [load_words("tab_tile%d" % a, tab_words[a]) for a in range(2)]
+        raw["wd"] = load_rows("wd_raw", wd)
         w2_raw = held("w2_raw", [P, 4, N], F32)
-        w2_by_slot = w2.rearrange("(q t i) n -> t q i n", t=4, i=8)
         for t in range(4):
-            nc.sync.dma_start(w2_raw[:, t, :], w2_by_slot[t])
+            nc.sync.dma_start(w2_raw[:, t, :], w2.rearrange("(q t i) n -> t q i n", t=4, i=8)[t])
         gains = held("gains", [P, 4, 8], F32)
         shifts = held("shifts", [P, N // P], F32)
         with nc.allow_non_contiguous_dma(reason="one value a partition"):
@@ -86,45 +113,20 @@ def tile_list_coldchain_spoilage_scores_kernel(
                 nc.sync.dma_start(gains[:, t, 0:1], gain.rearrange("(q t i o) -> t q i o", t=4, i=8, o=1)[t])
             nc.sync.dma_start(shifts[:], shift.rearrange("(c p) -> p c", p=P))
 
-        tab_picked = held("tab_picked", [P, S], U8)
-        tab2_picked = held("tab2_picked", [P, S], U8)
-        staged = held("staged", [P, STAGED], U8)
-        nc.vector.tensor_copy(tab_picked[:], tab_rows[:].indirect(lists[:]))
-        nc.vector.tensor_copy(tab2_picked[:], tab2_rows[:].indirect(list2[:]))
-        nc.vector.tensor_copy(staged[:, TAB_AT : TAB_AT + S].bitcast(I32), tab_picked[:].bitcast(I32))
-        for rows, at in ((w4_rows, W4_AT), (w8_rows, W8_AT)):
-            nc.vector.tensor_copy(
-                staged[:, at : at + H].bitcast(I32).rearrange("p (t q w) -> p t q w", t=4, w=2),
-                rows[:].bitcast(I32).rearrange("p (q t w) -> p t q w", t=4, w=2),
-            )
-        nc.vector.tensor_copy(staged[:, TAB2_AT : TAB2_AT + S].bitcast(I32), tab2_picked[:].bitcast(I32))
-        for d in range(4):
-            nc.gpsimd.dma_start(
-                planes[32 * d : 32 * d + 4, :, :].bitcast(I32),
-                staged[32 * d : 32 * d + 32 : 4, :].bitcast(I32),
-            )
-
-        w8_codes = held("w8_codes", [P, H], I32)
-        nc.vector.tensor_copy(
-            w8_codes[:].rearrange("p (t q w) -> p t q w", t=4, w=8),
-            w8_raw[:].rearrange("p (q t w) -> p t q w", t=4, w=8),
-        )
-        w4_codes = held("w4_codes", [P, 2, H // 2], I32)
-        nc.vector.tensor_copy(
-            w4_codes[:].rearrange("p a (t q w) -> p a t q w", t=4, w=4),
-            w4_raw[:].rearrange("p a (q t w) -> p a t q w", t=4, w=4),
-        )
-
-        def quantise_weight(name, raw):
-            grouped = held(name + "_bf16", [P, 4 * H], BF16)
-            nc.scalar.copy(
-                grouped[:].rearrange("p (t q i j) -> p t q i j", t=4, i=8, j=4),
-                raw[:].rearrange("p j (q t i) -> p t q i j", t=4, i=8),
-            )
-            codes = held(name + "_codes", [P, H], U32)
-            scales = held(name + "_scales", [P, H], U8)
+        def quantise_weight(name, slots, copy):
+            width = len(slots) * P
+            label = "%s_%d" % (name, slots[0])
+            grouped = held(label + "_bf16", [P, 4 * width], BF16)
+            for n, t in enumerate(slots):
+                copy(
+                    grouped[:, n * 4 * P : (n + 1) * 4 * P].rearrange("p (q u i j) -> p q u j i", u=2, i=4, j=4),
+                    raw[name][:].rearrange("p j (q t u i) -> p t q u j i", t=4, u=2, i=4)[:, t],
+                )
+            codes = held(label + "_codes", [P, width], U32)
+            scales = held(label + "_scales", [P, width], U8)
             nc.vector.quantize_mx(out=codes[:].bitcast(FP8X4), scales=scales[:], in_=grouped[:])
-            return codes, scales
+            for n, t in enumerate(slots):
+                made[name, t] = (codes[:, n * P : (n + 1) * P], scales[:, n * P : (n + 1) * P])
 
         def pick_words(name, table, offsets, half):
             picked = held(name, [P, HALF], U32)
@@ -132,92 +134,160 @@ def tile_list_coldchain_spoilage_scores_kernel(
             nc.vector.tensor_copy(picked[:], table[:].bitcast(U32).indirect(offsets[:, cols]))
             return picked
 
-        wr_q = [quantise_weight("wr0", wr0_raw)]
-        wd_q = quantise_weight("wd", wd_raw)
+        def bank(tag, bufs):
+            return psum.tile([P, HALF], F32, name=tag, bufs=bufs)
+
+        on_scalar, on_vector = nc.scalar.copy, nc.vector.tensor_copy
+        made = {}
+        nc.vector.tensor_copy(tab2_plane[:], tab2_rows[:].indirect(list2[:]))
+        w8_plane = held("w8_plane", [P, H], U8)
+        permute(w8_plane[:].bitcast(I32), w8_rows[:].bitcast(I32), 2)
+        w8_codes = held("w8_codes", [P, H], I32)
+        permute(w8_codes[:], w8_raw[:], 8)
+        quantise_weight("wr0", (0, 1, 2, 3), on_scalar)
+        quantise_weight("wr1", (0, 1), on_vector)
+        quantise_weight("wr1", (2, 3), on_scalar)
         v2 = [pick_words("v2_%d" % half, tab2_tile, list2, half) for half in range(2)]
-        wr_q.append(quantise_weight("wr1", wr1_raw))
-
-        def v_scales(a, half):
-            return planes[:, a, TAB_AT + half * HALF : TAB_AT + (half + 1) * HALF]
-
-        def v2_scales(half):
-            return planes[:, 0, TAB2_AT + half * HALF : TAB2_AT + (half + 1) * HALF]
 
         depot = {}
         for half in range(2):
             for t in range(4):
                 cols = slice(t * P, (t + 1) * P)
-                bank = psum.tile([P, HALF], F32, name="depot_bank")
+                product = bank(("lone", "total")[half], 4)
                 nc.tensor.matmul_mx(
-                    out=bank[:], lhsT=w8_codes[:, cols].bitcast(FP8X4),
-                    lhsT_scale=planes[:, 0, W8_AT + t * P : W8_AT + (t + 1) * P],
-                    rhs=v2[half][:].bitcast(FP8X4), rhs_scale=v2_scales(half), start=True, stop=True,
+                    out=product[:], lhsT=w8_codes[:, cols].bitcast(FP8X4), lhsT_scale=w8_plane[:, cols],
+                    rhs=v2[half][:].bitcast(FP8X4), rhs_scale=tab2_plane[:, half * HALF : (half + 1) * HALF],
+                    start=True, stop=True,
                 )
                 depot[half, t] = held("depot%d_%d" % (half, t), [P, HALF], F32)
-                nc.scalar.copy(depot[half, t][:], bank[:])
+                nc.scalar.copy(depot[half, t][:], product[:])
 
         v = {}
-        for a in range(2):
-            for half in range(2):
-                v[a, half] = pick_words("v%d_%d" % (a, half), tab_tiles[a], lists, half)
+        for half in range(2):
+            v[0, half] = pick_words("v0_%d" % half, tab0_tile, lists, half)
 
-        w2_grouped = held("w2_bf16", [P, N, 4], BF16)
-        nc.scalar.copy(w2_grouped[:], w2_raw[:].rearrange("p t n -> p n t"))
+        v[1, 0] = pick_words("v1_0", tab1_tile, lists, 0)
+        w4_codes = held("w4_codes", [P, 2, H // 2], I32)
+        nc.vector.tensor_copy(
+            w4_codes[:].rearrange("p a (t q w) -> p a t q w", t=4, w=4),
+            w4_raw[:].rearrange("p a (q t w) -> p a t q w", t=4, w=4),
+        )
+        v[1, 1] = pick_words("v1_1", tab1_tile, lists, 1)
+
+        def quantise_w2():
+            w2_grouped = held("w2_bf16", [P, 4 * N], BF16)
+            on_scalar(
+                w2_grouped[:].rearrange("p (u i t) -> p u t i", i=4, t=4),
+                w2_raw[:].rearrange("p t (u i) -> p u t i", i=4),
+            )
+            nc.vector.quantize_mx(out=w2_codes[:].bitcast(FP8X4), scales=w2_scales[:], in_=w2_grouped[:])
+
         w2_codes = held("w2_codes", [P, N], U32)
         w2_scales = held("w2_scales", [P, N], U8)
-        nc.vector.quantize_mx(
-            out=w2_codes[:].bitcast(FP8X4), scales=w2_scales[:], in_=w2_grouped[:].rearrange("p n t -> p (n t)")
-        )
 
-        for half in range(2):
-            h_rows = held("h_rows%d" % half, [P, 4, HALF], BF16)
-            for t in range(4):
-                cols = slice(t * P, (t + 1) * P)
-                route = psum.tile([P, HALF], F32, name="route_bank")
-                for a in range(2):
-                    nc.tensor.matmul_mx(
-                        out=route[:], lhsT=wr_q[a][0][:, cols].bitcast(FP8X4), lhsT_scale=wr_q[a][1][:, cols],
-                        rhs=v[a, half][:].bitcast(FP8X4), rhs_scale=v_scales(a, half), start=(a == 0), stop=(a == 1),
-                    )
-                total = psum.tile([P, HALF], F32, name="total_bank")
+        out_view = out.rearrange("(c p) j -> p c j", p=P)
+        totals, diffs = {}, {}
+
+        def route_product(half, t):
+            route = bank("lone", 4)
+            for a in range(2):
+                codes, scales = made["wr%d" % a, t]
                 nc.tensor.matmul_mx(
-                    out=total[:], lhsT=wd_q[0][:, cols].bitcast(FP8X4), lhsT_scale=wd_q[1][:, cols],
-                    rhs=v2[half][:].bitcast(FP8X4), rhs_scale=v2_scales(half), start=True, stop=False,
+                    out=route[:], lhsT=codes.bitcast(FP8X4), lhsT_scale=scales, rhs=v[a, half][:].bitcast(FP8X4),
+                    rhs_scale=planes[:, a, half * HALF : (half + 1) * HALF], start=(a == 0), stop=(a == 1),
                 )
-                for a in range(2):
-                    nc.tensor.matmul_mx(
-                        out=total[:], lhsT=w4_codes[:, a, t * P // 2 : (t + 1) * P // 2].bitcast(FP4X4),
-                        lhsT_scale=planes[:, a, W4_AT + t * P : W4_AT + (t + 1) * P],
-                        rhs=v[a, half][:].bitcast(FP8X4), rhs_scale=v_scales(a, half), start=False, stop=(a == 1),
-                    )
-                diff = ring.tile([P, HALF], F32, name="diff")
-                nc.vector.tensor_tensor(diff[:], route[:], depot[half, t][:], ALU.subtract)
-                size = ring.tile([P, HALF], F32, name="size")
-                nc.scalar.activation(size[:], diff[:], ACT.Abs)
-                sine = ring.tile([P, HALF], F32, name="sine")
-                nc.scalar.activation(sine[:], total[:], ACT.Sin)
-                cosine = ring.tile([P, HALF], F32, name="cosine")
-                nc.scalar.activation(cosine[:], size[:], ACT.Sin, bias=math.pi / 2, scale=-1.0)
-                nc.vector.scalar_tensor_tensor(
-                    h_rows[:, t, :], cosine[:], gains[:, t, 0:1], sine[:], ALU.mult, ALU.mult
-                )
-            h_grouped = held("h_grouped%d" % half, [P, HALF, 4], BF16)
-            nc.vector.tensor_copy(h_grouped[:], h_rows[:].rearrange("p t j -> p j t"))
-            h_codes = held("h_codes%d" % half, [P, HALF], U32)
-            h_scales = held("h_scales%d" % half, [P, HALF], U8)
-            nc.vector.quantize_mx(
-                out=h_codes[:].bitcast(FP8X4), scales=h_scales[:], in_=h_grouped[:].rearrange("p j t -> p (j t)")
+            nc.vector.tensor_tensor(diffs[half][:, t, :], route[:], depot[half, t][:], ALU.subtract)
+
+        def total_product(half, t):
+            total = bank("total", 4)
+            codes, scales = made["wd", t]
+            nc.tensor.matmul_mx(
+                out=total[:], lhsT=codes.bitcast(FP8X4), lhsT_scale=scales, rhs=v2[half][:].bitcast(FP8X4),
+                rhs_scale=tab2_plane[:, half * HALF : (half + 1) * HALF], start=True, stop=False,
             )
-            for c in range(N // P):
-                cols = slice(c * P, (c + 1) * P)
-                scores = psum.tile([P, HALF], F32, name="score_bank")
+            for a in range(2):
                 nc.tensor.matmul_mx(
-                    out=scores[:], lhsT=w2_codes[:, cols].bitcast(FP8X4), lhsT_scale=w2_scales[:, cols],
+                    out=total[:], lhsT=w4_codes[:, a, t * P // 2 : (t + 1) * P // 2].bitcast(FP4X4),
+                    lhsT_scale=planes[:, a, S + t * P : S + (t + 1) * P], rhs=v[a, half][:].bitcast(FP8X4),
+                    rhs_scale=planes[:, a, half * HALF : (half + 1) * HALF], start=False, stop=(a == 1),
+                )
+            totals[half, t] = total
+
+        def differences(half):
+            diffs[half] = held("diff%d" % half, [P, 4, HALF], F32)
+            for t in range(4):
+                route_product(half, t)
+
+        def cosines(half, first, width, slots):
+            cols = slice(first, first + width)
+            size = keep.tile([P, len(slots), width], F32, name="size", bufs=2)
+            nc.scalar.activation(size[:], diffs[half][:, slots[0] : slots[-1] + 1, cols], ACT.Abs)
+            cosine = held("cosine%d_%d_%d" % (half, first, slots[0]), [P, len(slots), width], F32)
+            nc.scalar.activation(cosine[:], size[:], ACT.Sin, bias=math.pi / 2, scale=-1.0)
+            for n, t in enumerate(slots):
+                cos_of[half, first, t] = cosine[:, n, :]
+
+        def sines(half, first, width, slots):
+            for t in slots:
+                sine = held("sine%d_%d_%d" % (half, first, t), [P, width], F32)
+                nc.scalar.activation(sine[:], totals[half, t][:, first : first + width], ACT.Sin)
+                sin_of[half, first, t] = sine
+
+        def quantise_h(half, first, width):
+            name = "%d_%d" % (half, first)
+            h_rows = held("h_rows" + name, [P, 4, width], BF16)
+            for t in range(4):
+                nc.vector.scalar_tensor_tensor(
+                    h_rows[:, t, :], cos_of[half, first, t], gains[:, t, 0:1], sin_of[half, first, t][:],
+                    ALU.mult, ALU.mult,
+                )
+            h_grouped = held("h_grouped" + name, [P, 4 * width], BF16)
+            nc.vector.tensor_copy(
+                h_grouped[:].rearrange("p (u i t) -> p u t i", i=4, t=4),
+                h_rows[:].rearrange("p t (u i) -> p u t i", i=4),
+            )
+            h_codes = held("h_codes" + name, [P, width], U32)
+            h_scales = held("h_scales" + name, [P, width], U8)
+            nc.vector.quantize_mx(out=h_codes[:].bitcast(FP8X4), scales=h_scales[:], in_=h_grouped[:])
+            h_of[half, first] = (h_codes, h_scales)
+
+        def scores_of(half, first, width, on_vector_rows):
+            h_codes, h_scales = h_of[half, first]
+            result = held("result%d_%d" % (half, first), [P, N // P, width], F32)
+            for c in range(N // P):
+                rows = slice(c * P, (c + 1) * P)
+                scores = bank("lone", 4)
+                nc.tensor.matmul_mx(
+                    out=scores[:, 0:width], lhsT=w2_codes[:, rows].bitcast(FP8X4), lhsT_scale=w2_scales[:, rows],
                     rhs=h_codes[:].bitcast(FP8X4), rhs_scale=h_scales[:], start=True, stop=True,
                 )
-                result = ring.tile([P, HALF], F32, name="result")
-                if c == 0:
-                    nc.scalar.activation(result[:], scores[:], ACT.Identity, bias=shifts[:, c : c + 1])
+                if c in on_vector_rows:
+                    nc.vector.tensor_scalar_add(result[:, c, :], scores[:, 0:width], shifts[:, c : c + 1])
                 else:
-                    nc.vector.tensor_scalar_add(result[:], scores[:], shifts[:, c : c + 1])
-                nc.sync.dma_start(out[cols, half * HALF : (half + 1) * HALF], result[:])
+                    nc.scalar.activation(result[:, c, :], scores[:, 0:width], ACT.Identity, bias=shifts[:, c : c + 1])
+            at = half * HALF + first
+            nc.sync.dma_start(out_view[:, :, at : at + width], result[:])
+
+        cos_of, sin_of, h_of = {}, {}, {}
+        differences(0)
+        quantise_weight("wd", (0, 1), on_vector)
+        quantise_weight("wd", (2, 3), on_vector)
+        for t in range(4):
+            total_product(0, t)
+        for t in range(4):
+            cosines(0, 0, HALF, (t,))
+        differences(1)
+        quantise_w2()
+        sines(0, 0, HALF, range(4))
+        for t in range(4):
+            total_product(1, t)
+        quantise_h(0, 0, HALF)
+        pieces = ((0, 256), (256, 128), (384, 128))
+        for first, width in pieces:
+            cosines(1, first, width, (0, 1, 2, 3))
+            sines(1, first, width, range(4))
+        for first, width in pieces:
+            quantise_h(1, first, width)
+        scores_of(0, 0, HALF, ())
+        for first, width in pieces:
+            scores_of(1, first, width, (1,) if first + width == HALF else ())

@@ -46,9 +46,6 @@ def tile_list_coldchain_spoilage_scores_kernel(
             nc.gpsimd.memset(rows[:, T // 2 : T].bitcast(I32), 0)
         for rows in (w4_rows, w8_rows):
             nc.vector.memset(rows[:].bitcast(I32), 0)
-        warm = held("warm", [P, 2], F32)
-        nc.vector.memset(warm[:, 0:1], 0.0)
-        nc.scalar.activation(warm[:, 1:2], warm[:, 0:1], ACT.Sin)
         nc.vector.memset(planes[:].rearrange("p a c -> p (a c)").bitcast(I32), 0)
 
         def load_rows(name, rows):
@@ -87,22 +84,22 @@ def tile_list_coldchain_spoilage_scores_kernel(
         staged = held("staged", [P, S + H], U8)
         nc.vector.tensor_copy(tab_picked[:], tab_rows[:].indirect(lists[:]))
         load_plane(tab2_rows, tab2_scales[0], (0, 1))
-        raw["wr0"] = load_rows("wr0_raw", wr[0:512, :])
         load_plane(tab2_rows, tab2_scales[0], (2, 3))
-        raw["wr1"] = load_rows("wr1_raw", wr[512:1024, :])
-        nc.sync.dma_start(w4_rows[0:P:4, :].bitcast(I32), w4_scales.bitcast(I32).rearrange("a q c -> q a c"))
+        raw["wr0"] = load_rows("wr0_raw", wr[0:512, :])
         load_plane(w8_rows, w8_scales[0], (0, 1))
+        raw["wr1"] = load_rows("wr1_raw", wr[512:1024, :])
         load_plane(w8_rows, w8_scales[0], (2, 3))
+        nc.sync.dma_start(w4_rows[0:P:4, :].bitcast(I32), w4_scales.bitcast(I32).rearrange("a q c -> q a c"))
         w8_raw = load_words("w8_raw", w8_words[0])
         tab2_tile = load_words("tab2_tile", tab2_words[0])
         tab0_tile = load_words("tab0_tile", tab_words[0])
+        tab1_tile = load_words("tab1_tile", tab_words[1])
         nc.vector.tensor_copy(staged[:, 0:S].bitcast(I32), tab_picked[:].bitcast(I32))
         permute(staged[:, S : S + H].bitcast(I32), w4_rows[:].bitcast(I32), 2)
         move_planes()
-        tab1_tile = load_words("tab1_tile", tab_words[1])
+        raw["wd"] = load_rows("wd_raw", wd)
         w4_raw = held("w4_raw", [P, 2, H // 2], I32)
         nc.sync.dma_start(w4_raw[:], w4_words.bitcast(I32).rearrange("a p c -> p a c"))
-        raw["wd"] = load_rows("wd_raw", wd)
         w2_raw = held("w2_raw", [P, 4, N], F32)
         for t in range(4):
             nc.sync.dma_start(w2_raw[:, t, :], w2.rearrange("(q t i) n -> t q i n", t=4, i=8)[t])
@@ -127,6 +124,23 @@ def tile_list_coldchain_spoilage_scores_kernel(
             nc.vector.quantize_mx(out=codes[:].bitcast(FP8X4), scales=scales[:], in_=grouped[:])
             for n, t in enumerate(slots):
                 made[name, t] = (codes[:, n * P : (n + 1) * P], scales[:, n * P : (n + 1) * P])
+
+        def quantise_wd(slots):
+            width = len(slots) * P
+            grouped = held("wd_bf16_%d" % slots[0], [P, len(slots), 4 * P], BF16)
+            for n, t in enumerate(slots):
+                nc.gpsimd.tensor_scalar(
+                    grouped[:, n, :].rearrange("p (q i j) -> p q i j", i=8, j=4),
+                    raw["wd"][:].rearrange("p j (q t i) -> p t q i j", t=4, i=8)[:, t],
+                    1.0, 0.0, ALU.mult, ALU.add,
+                )
+            codes = held("wd_codes_%d" % slots[0], [P, width], U32)
+            scales = held("wd_scales_%d" % slots[0], [P, width], U8)
+            nc.vector.quantize_mx(
+                out=codes[:].bitcast(FP8X4), scales=scales[:], in_=grouped[:].rearrange("p t c -> p (t c)")
+            )
+            for n, t in enumerate(slots):
+                made["wd", t] = (codes[:, n * P : (n + 1) * P], scales[:, n * P : (n + 1) * P])
 
         def pick_words(name, table, offsets, half):
             picked = held(name, [P, HALF], U32)
@@ -176,10 +190,12 @@ def tile_list_coldchain_spoilage_scores_kernel(
 
         def quantise_w2():
             w2_grouped = held("w2_bf16", [P, 4 * N], BF16)
-            on_scalar(
-                w2_grouped[:].rearrange("p (u i t) -> p u t i", i=4, t=4),
-                w2_raw[:].rearrange("p t (u i) -> p u t i", i=4),
-            )
+            for c in range(N // P):
+                nc.gpsimd.tensor_scalar(
+                    w2_grouped[:, 4 * P * c : 4 * P * (c + 1)].rearrange("p (n t) -> p n t", t=4),
+                    w2_raw[:, :, P * c : P * (c + 1)].rearrange("p t n -> p n t"),
+                    1.0, 0.0, ALU.mult, ALU.add,
+                )
             nc.vector.quantize_mx(out=w2_codes[:].bitcast(FP8X4), scales=w2_scales[:], in_=w2_grouped[:])
 
         w2_codes = held("w2_codes", [P, N], U32)
@@ -227,6 +243,17 @@ def tile_list_coldchain_spoilage_scores_kernel(
             for n, t in enumerate(slots):
                 cos_of[half, first, t] = cosine[:, n, :]
 
+        def half_angle_term():
+            half_sine = held("half_sine", [P, HALF], F32)
+            nc.scalar.activation(half_sine[:], diffs[0][:, 0, :], ACT.Sin, scale=0.5)
+            gain_times_minus_two = held("gain_times_minus_two", [P, 1], F32)
+            nc.vector.tensor_scalar(gain_times_minus_two[:], gains[:, 0, 0:1], -2.0, 0.0, ALU.mult, ALU.add)
+            term = held("half_angle_term", [P, HALF], F32)
+            nc.vector.scalar_tensor_tensor(
+                term[:], half_sine[:], gain_times_minus_two[:], half_sine[:], ALU.mult, ALU.mult
+            )
+            cos_of[0, 0, 0] = term[:]
+
         def sines(half, first, width, slots):
             for t in slots:
                 sine = held("sine%d_%d_%d" % (half, first, t), [P, width], F32)
@@ -239,7 +266,7 @@ def tile_list_coldchain_spoilage_scores_kernel(
             for t in range(4):
                 nc.vector.scalar_tensor_tensor(
                     h_rows[:, t, :], cos_of[half, first, t], gains[:, t, 0:1], sin_of[half, first, t][:],
-                    ALU.mult, ALU.mult,
+                    ALU.add if (half, t) == (0, 0) else ALU.mult, ALU.mult,
                 )
             h_grouped = held("h_grouped" + name, [P, 4 * width], BF16)
             nc.vector.tensor_copy(
@@ -270,11 +297,12 @@ def tile_list_coldchain_spoilage_scores_kernel(
 
         cos_of, sin_of, h_of = {}, {}, {}
         differences(0)
-        quantise_weight("wd", (0, 1), on_vector)
-        quantise_weight("wd", (2, 3), on_vector)
+        quantise_wd((0, 1))
+        quantise_wd((2, 3))
         for t in range(4):
             total_product(0, t)
-        for t in range(4):
+        half_angle_term()
+        for t in range(1, 4):
             cosines(0, 0, HALF, (t,))
         differences(1)
         quantise_w2()

@@ -19,7 +19,6 @@ ALU = mybir.AluOpType
 
 P = 128
 HALF = 512
-CHUNKS = (((0, 512, 1),), ((0, 256, 2), (256, 128, 4), (384, 128, 4)))
 
 
 def tile_list_coldchain_spoilage_scores_kernel(
@@ -29,10 +28,11 @@ def tile_list_coldchain_spoilage_scores_kernel(
     nc = tc.nc
     with ExitStack() as ctx:
         keep = ctx.enter_context(tc.tile_pool(name="keep", bufs=1))
+        reused = ctx.enter_context(tc.tile_pool(name="reused", bufs=1))
         psum = ctx.enter_context(tc.psum_pool(name="psum", bufs=1))
 
-        def held(name, shape, dtype):
-            return keep.tile(shape, dtype, name=name, align_bytes=64)
+        def held(name, shape, dtype, after=None):
+            return keep.tile(shape, dtype, name=name, tag=after or name, align_bytes=64)
 
         lists = held("lists", [P, S // 16], U16)
         list2 = held("list2", [P, S // 16], U16)
@@ -41,15 +41,18 @@ def tile_list_coldchain_spoilage_scores_kernel(
         w4_rows = held("w4_rows", [P, H], U8)
         w8_rows = held("w8_rows", [P, H], U8)
         planes = held("planes", [P, 2, S + H], U8)
-        for rows in (tab_rows, tab2_rows):
-            nc.vector.memset(rows[:, 0 : T // 2].bitcast(I32), 0)
-            nc.gpsimd.memset(rows[:, T // 2 : T].bitcast(I32), 0)
-        for rows in (w4_rows, w8_rows):
+        nc.vector.memset(tab_rows[:, 0 : T // 2].bitcast(I32), 0)
+        nc.gpsimd.memset(tab_rows[:, T // 2 : T].bitcast(I32), 0)
+        for rows in (tab2_rows, w4_rows, w8_rows):
             nc.vector.memset(rows[:].bitcast(I32), 0)
         nc.vector.memset(planes[:].rearrange("p a c -> p (a c)").bitcast(I32), 0)
+        warm = held("warm", [P, 8], F32)
+        nc.gpsimd.memset(warm[:], 0.0)
+        warmed = held("warmed", [P, 8], F32)
+        nc.scalar.activation(warmed[:], warm[:], ACT.Sin)
 
-        def load_rows(name, rows):
-            raw = held(name, [P, 4, H], F32)
+        def load_rows(name, rows, raw=None):
+            raw = held(name, [P, 4, H], F32) if raw is None else raw
             nc.sync.dma_start(raw[:], rows.rearrange("(p j) c -> p j c", j=4))
             return raw
 
@@ -70,36 +73,34 @@ def tile_list_coldchain_spoilage_scores_kernel(
                 )
 
         def permute(dst, src, words):
-            nc.vector.tensor_copy(
+            nc.gpsimd.tensor_copy(
                 dst.rearrange("p (t q w) -> p t q w", t=4, w=words),
                 src.rearrange("p (q t w) -> p t q w", t=4, w=words),
             )
 
+        w8_raw = load_words("w8_raw", w8_words[0])
         nc.sync.dma_start(lists[:], offs)
-        nc.sync.dma_start(list2[:], offs2)
         nc.sync.dma_start(tab_rows[0:P:4, :].bitcast(I32), tab_scales.bitcast(I32).rearrange("a q t -> q a t"))
         raw = {}
+        raw["wr0"] = load_rows("wr0_raw", wr[0:512, :])
+        nc.sync.dma_start(list2[:], offs2)
         tab_picked = held("tab_picked", [P, S], U8)
         tab2_plane = held("tab2_plane", [P, S], U8)
         staged = held("staged", [P, S + H], U8)
         nc.vector.tensor_copy(tab_picked[:], tab_rows[:].indirect(lists[:]))
-        load_plane(tab2_rows, tab2_scales[0], (0, 1))
-        load_plane(tab2_rows, tab2_scales[0], (2, 3))
-        raw["wr0"] = load_rows("wr0_raw", wr[0:512, :])
-        load_plane(w8_rows, w8_scales[0], (0, 1))
-        raw["wr1"] = load_rows("wr1_raw", wr[512:1024, :])
-        load_plane(w8_rows, w8_scales[0], (2, 3))
-        nc.sync.dma_start(w4_rows[0:P:4, :].bitcast(I32), w4_scales.bitcast(I32).rearrange("a q c -> q a c"))
-        w8_raw = load_words("w8_raw", w8_words[0])
+        load_plane(tab2_rows, tab2_scales[0], range(4))
         tab2_tile = load_words("tab2_tile", tab2_words[0])
+        nc.sync.dma_start(w4_rows[0:P:4, :].bitcast(I32), w4_scales.bitcast(I32).rearrange("a q c -> q a c"))
+        load_plane(w8_rows, w8_scales[0], range(4))
         tab0_tile = load_words("tab0_tile", tab_words[0])
+        raw["wr1"] = load_rows("wr1_raw", wr[512:1024, :], reused.tile([P, 4, H], F32, name="wr1_raw", offset=0))
         tab1_tile = load_words("tab1_tile", tab_words[1])
         nc.vector.tensor_copy(staged[:, 0:S].bitcast(I32), tab_picked[:].bitcast(I32))
         permute(staged[:, S : S + H].bitcast(I32), w4_rows[:].bitcast(I32), 2)
         move_planes()
-        raw["wd"] = load_rows("wd_raw", wd)
         w4_raw = held("w4_raw", [P, 2, H // 2], I32)
         nc.sync.dma_start(w4_raw[:], w4_words.bitcast(I32).rearrange("a p c -> p a c"))
+        raw["wd"] = load_rows("wd_raw", wd)
         w2_raw = held("w2_raw", [P, 4, N], F32)
         for t in range(4):
             nc.sync.dma_start(w2_raw[:, t, :], w2.rearrange("(q t i) n -> t q i n", t=4, i=8)[t])
@@ -107,10 +108,10 @@ def tile_list_coldchain_spoilage_scores_kernel(
         shifts = held("shifts", [P, N // P], F32)
         with nc.allow_non_contiguous_dma(reason="one value a partition"):
             for t in range(4):
-                nc.sync.dma_start(gains[:, t, 0:1], gain.rearrange("(q t i o) -> t q i o", t=4, i=8, o=1)[t])
-            nc.sync.dma_start(shifts[:], shift.rearrange("(c p) -> p c", p=P))
+                nc.gpsimd.dma_start(gains[:, t, 0:1], gain.rearrange("(q t i o) -> t q i o", t=4, i=8, o=1)[t])
+            nc.gpsimd.dma_start(shifts[:], shift.rearrange("(c p) -> p c", p=P))
 
-        def quantise_weight(name, slots, copy):
+        def quantise_weight(name, slots, copy, after=None):
             width = len(slots) * P
             label = "%s_%d" % (name, slots[0])
             grouped = held(label + "_bf16", [P, 4 * width], BF16)
@@ -119,37 +120,36 @@ def tile_list_coldchain_spoilage_scores_kernel(
                     grouped[:, n * 4 * P : (n + 1) * 4 * P].rearrange("p (q u i j) -> p q u j i", u=2, i=4, j=4),
                     raw[name][:].rearrange("p j (q t u i) -> p t q u j i", t=4, u=2, i=4)[:, t],
                 )
-            codes = held(label + "_codes", [P, width], U32)
+            codes = held(label + "_codes", [P, width], U32, after)
             scales = held(label + "_scales", [P, width], U8)
             nc.vector.quantize_mx(out=codes[:].bitcast(FP8X4), scales=scales[:], in_=grouped[:])
             for n, t in enumerate(slots):
                 made[name, t] = (codes[:, n * P : (n + 1) * P], scales[:, n * P : (n + 1) * P])
 
-        def quantise_wd(slots):
+        def quantise_from_gpsimd(name, slots, codes):
             width = len(slots) * P
-            grouped = held("wd_bf16_%d" % slots[0], [P, len(slots), 4 * P], BF16)
+            grouped = held("%s_%d_bf16" % (name, slots[0]), [P, len(slots), 4 * P], BF16)
             for n, t in enumerate(slots):
                 nc.gpsimd.tensor_scalar(
                     grouped[:, n, :].rearrange("p (q i j) -> p q i j", i=8, j=4),
-                    raw["wd"][:].rearrange("p j (q t i) -> p t q i j", t=4, i=8)[:, t],
+                    raw[name][:].rearrange("p j (q t i) -> p t q i j", t=4, i=8)[:, t],
                     1.0, 0.0, ALU.mult, ALU.add,
                 )
-            codes = held("wd_codes_%d" % slots[0], [P, width], U32)
-            scales = held("wd_scales_%d" % slots[0], [P, width], U8)
+            scales = held("%s_%d_scales" % (name, slots[0]), [P, width], U8)
             nc.vector.quantize_mx(
                 out=codes[:].bitcast(FP8X4), scales=scales[:], in_=grouped[:].rearrange("p t c -> p (t c)")
             )
             for n, t in enumerate(slots):
-                made["wd", t] = (codes[:, n * P : (n + 1) * P], scales[:, n * P : (n + 1) * P])
+                made[name, t] = (codes[:, n * P : (n + 1) * P], scales[:, n * P : (n + 1) * P])
 
-        def pick_words(name, table, offsets, half):
-            picked = held(name, [P, HALF], U32)
+        def pick_words(name, table, offsets, half, after=None):
+            picked = held(name, [P, HALF], U32, after)
             cols = slice(half * HALF // 16, (half + 1) * HALF // 16)
             nc.vector.tensor_copy(picked[:], table[:].bitcast(U32).indirect(offsets[:, cols]))
             return picked
 
-        def bank(tag, bufs):
-            return psum.tile([P, HALF], F32, name=tag, bufs=bufs)
+        def bank(number):
+            return psum.tile([P, HALF], F32, name="bank%d" % number)
 
         on_scalar, on_vector = nc.scalar.copy, nc.vector.tensor_copy
         made = {}
@@ -158,35 +158,36 @@ def tile_list_coldchain_spoilage_scores_kernel(
         permute(w8_plane[:].bitcast(I32), w8_rows[:].bitcast(I32), 2)
         w8_codes = held("w8_codes", [P, H], I32)
         permute(w8_codes[:], w8_raw[:], 8)
-        quantise_weight("wr0", (0, 1, 2, 3), on_scalar)
-        quantise_weight("wr1", (0, 1), on_vector)
-        quantise_weight("wr1", (2, 3), on_scalar)
-        v2 = [pick_words("v2_%d" % half, tab2_tile, list2, half) for half in range(2)]
+        v2 = [pick_words("v2_0", tab2_tile, list2, 0), pick_words("v2_1", tab2_tile, list2, 1, "w8_rows")]
+        quantise_weight("wr0", (0, 1, 2, 3), on_scalar, "tab2_tile")
 
         depot = {}
-        for half in range(2):
+
+        def depot_products(half, tiles):
             for t in range(4):
                 cols = slice(t * P, (t + 1) * P)
-                product = bank(("lone", "total")[half], 4)
+                product = bank(4 * half + t)
                 nc.tensor.matmul_mx(
                     out=product[:], lhsT=w8_codes[:, cols].bitcast(FP8X4), lhsT_scale=w8_plane[:, cols],
                     rhs=v2[half][:].bitcast(FP8X4), rhs_scale=tab2_plane[:, half * HALF : (half + 1) * HALF],
                     start=True, stop=True,
                 )
-                depot[half, t] = held("depot%d_%d" % (half, t), [P, HALF], F32)
-                nc.scalar.copy(depot[half, t][:], product[:])
+                depot[half, t] = tiles[t]
+                nc.scalar.copy(tiles[t], product[:])
 
+        depot_products(0, [held("depot0_%d" % t, [P, HALF], F32)[:] for t in range(4)])
         v = {}
         for half in range(2):
             v[0, half] = pick_words("v0_%d" % half, tab0_tile, lists, half)
-
+        quantise_weight("wr1", (0, 1), on_scalar)
         v[1, 0] = pick_words("v1_0", tab1_tile, lists, 0)
+        quantise_from_gpsimd("wr1", (2, 3), held("wr1_2_codes", [P, 2 * P], U32))
+        depot_products(1, [reused.tile([P, HALF], F32, name="depot1_%d" % t, offset=t * 4 * HALF)[:] for t in range(4)])
         w4_codes = held("w4_codes", [P, 2, H // 2], I32)
-        nc.vector.tensor_copy(
+        nc.gpsimd.tensor_copy(
             w4_codes[:].rearrange("p a (t q w) -> p a t q w", t=4, w=4),
             w4_raw[:].rearrange("p a (q t w) -> p a t q w", t=4, w=4),
         )
-        v[1, 1] = pick_words("v1_1", tab1_tile, lists, 1)
 
         def quantise_w2():
             w2_grouped = held("w2_bf16", [P, 4 * N], BF16)
@@ -198,41 +199,67 @@ def tile_list_coldchain_spoilage_scores_kernel(
                 )
             nc.vector.quantize_mx(out=w2_codes[:].bitcast(FP8X4), scales=w2_scales[:], in_=w2_grouped[:])
 
-        w2_codes = held("w2_codes", [P, N], U32)
         w2_scales = held("w2_scales", [P, N], U8)
 
         out_view = out.rearrange("(c p) j -> p c j", p=P)
         totals, diffs = {}, {}
 
-        def route_product(half, t):
-            route = bank("lone", 4)
-            for a in range(2):
-                codes, scales = made["wr%d" % a, t]
-                nc.tensor.matmul_mx(
-                    out=route[:], lhsT=codes.bitcast(FP8X4), lhsT_scale=scales, rhs=v[a, half][:].bitcast(FP8X4),
-                    rhs_scale=planes[:, a, half * HALF : (half + 1) * HALF], start=(a == 0), stop=(a == 1),
-                )
-            nc.vector.tensor_tensor(diffs[half][:, t, :], route[:], depot[half, t][:], ALU.subtract)
-
-        def total_product(half, t):
-            total = bank("total", 4)
-            codes, scales = made["wd", t]
+        def route_pass(route, half, t, a):
+            codes, scales = made["wr%d" % a, t]
             nc.tensor.matmul_mx(
-                out=total[:], lhsT=codes.bitcast(FP8X4), lhsT_scale=scales, rhs=v2[half][:].bitcast(FP8X4),
-                rhs_scale=tab2_plane[:, half * HALF : (half + 1) * HALF], start=True, stop=False,
+                out=route[:], lhsT=codes.bitcast(FP8X4), lhsT_scale=scales, rhs=v[a, half][:].bitcast(FP8X4),
+                rhs_scale=planes[:, a, half * HALF : (half + 1) * HALF], start=(a == 0), stop=(a == 1),
             )
+
+        def open_total(half, t, number):
+            total = totals[half, t] = bank(number)
             for a in range(2):
                 nc.tensor.matmul_mx(
                     out=total[:], lhsT=w4_codes[:, a, t * P // 2 : (t + 1) * P // 2].bitcast(FP4X4),
                     lhsT_scale=planes[:, a, S + t * P : S + (t + 1) * P], rhs=v[a, half][:].bitcast(FP8X4),
-                    rhs_scale=planes[:, a, half * HALF : (half + 1) * HALF], start=False, stop=(a == 1),
+                    rhs_scale=planes[:, a, half * HALF : (half + 1) * HALF], start=(a == 0), stop=False,
                 )
-            totals[half, t] = total
 
-        def differences(half):
-            diffs[half] = held("diff%d" % half, [P, 4, HALF], F32)
+        def close_total(half, t):
+            codes, scales = made["wd", t]
+            nc.tensor.matmul_mx(
+                out=totals[half, t][:], lhsT=codes.bitcast(FP8X4), lhsT_scale=scales, rhs=v2[half][:].bitcast(FP8X4),
+                rhs_scale=tab2_plane[:, half * HALF : (half + 1) * HALF], start=False, stop=True,
+            )
+
+        def total_piece(first, number):
+            total = totals[1, first] = bank(number)
+            at = HALF + first
             for t in range(4):
-                route_product(half, t)
+                cols = slice(t * P, (t + 1) * P)
+                for a in range(2):
+                    nc.tensor.matmul_mx(
+                        out=total[:, cols], lhsT=w4_codes[:, a, t * P // 2 : (t + 1) * P // 2].bitcast(FP4X4),
+                        lhsT_scale=planes[:, a, S + t * P : S + (t + 1) * P],
+                        rhs=v[a, 1][:, first : first + P].bitcast(FP8X4), rhs_scale=planes[:, a, at : at + P],
+                        start=(a == 0), stop=False,
+                    )
+                codes, scales = made["wd", t]
+                nc.tensor.matmul_mx(
+                    out=total[:, cols], lhsT=codes.bitcast(FP8X4), lhsT_scale=scales,
+                    rhs=v2[1][:, first : first + P].bitcast(FP8X4), rhs_scale=tab2_plane[:, at : at + P],
+                    start=False, stop=True,
+                )
+
+        def piece_sines(first, width):
+            sine = held("sine1_%d" % first, [P, 4, width], F32)
+            for at in range(first, first + width, P):
+                step = min(P, width)
+                nc.scalar.activation(
+                    sine[:, :, at - first : at - first + step],
+                    totals[1, at - at % P][:].rearrange("p (t c) -> p t c", t=4)[:, :, at % P : at % P + step],
+                    ACT.Sin,
+                )
+            for t in range(4):
+                sin_of[1, first, t] = sine[:, t, :]
+
+        def subtract(route, half, t):
+            nc.vector.tensor_tensor(diffs[half][:, t, :], route[:], depot[half, t], ALU.subtract)
 
         def cosines(half, first, width, slots):
             cols = slice(first, first + width)
@@ -243,47 +270,39 @@ def tile_list_coldchain_spoilage_scores_kernel(
             for n, t in enumerate(slots):
                 cos_of[half, first, t] = cosine[:, n, :]
 
-        def half_angle_term():
-            half_sine = held("half_sine", [P, HALF], F32)
-            nc.scalar.activation(half_sine[:], diffs[0][:, 0, :], ACT.Sin, scale=0.5)
-            gain_times_minus_two = held("gain_times_minus_two", [P, 1], F32)
-            nc.vector.tensor_scalar(gain_times_minus_two[:], gains[:, 0, 0:1], -2.0, 0.0, ALU.mult, ALU.add)
-            term = held("half_angle_term", [P, HALF], F32)
-            nc.vector.scalar_tensor_tensor(
-                term[:], half_sine[:], gain_times_minus_two[:], half_sine[:], ALU.mult, ALU.mult
-            )
-            cos_of[0, 0, 0] = term[:]
-
         def sines(half, first, width, slots):
             for t in slots:
                 sine = held("sine%d_%d_%d" % (half, first, t), [P, width], F32)
                 nc.scalar.activation(sine[:], totals[half, t][:, first : first + width], ACT.Sin)
-                sin_of[half, first, t] = sine
+                sin_of[half, first, t] = sine[:]
 
-        def quantise_h(half, first, width):
-            name = "%d_%d" % (half, first)
-            h_rows = held("h_rows" + name, [P, 4, width], BF16)
+        def products(half, first, width):
+            h_rows = rows_of[half, first] = held("h_rows%d_%d" % (half, first), [P, 4, width], BF16)
             for t in range(4):
                 nc.vector.scalar_tensor_tensor(
-                    h_rows[:, t, :], cos_of[half, first, t], gains[:, t, 0:1], sin_of[half, first, t][:],
-                    ALU.add if (half, t) == (0, 0) else ALU.mult, ALU.mult,
+                    h_rows[:, t, :], cos_of[half, first, t], gains[:, t, 0:1], sin_of[half, first, t],
+                    ALU.mult, ALU.mult,
                 )
-            h_grouped = held("h_grouped" + name, [P, 4 * width], BF16)
+
+        def interleave(half, first, width):
+            h_grouped = grouped_of[half, first] = held("h_grouped%d_%d" % (half, first), [P, 4 * width], BF16)
             nc.vector.tensor_copy(
                 h_grouped[:].rearrange("p (u i t) -> p u t i", i=4, t=4),
-                h_rows[:].rearrange("p t (u i) -> p u t i", i=4),
+                rows_of[half, first][:].rearrange("p t (u i) -> p u t i", i=4),
             )
-            h_codes = held("h_codes" + name, [P, width], U32)
-            h_scales = held("h_scales" + name, [P, width], U8)
-            nc.vector.quantize_mx(out=h_codes[:].bitcast(FP8X4), scales=h_scales[:], in_=h_grouped[:])
+
+        def quantise_h(half, first, width):
+            h_codes = held("h_codes%d_%d" % (half, first), [P, width], U32)
+            h_scales = held("h_scales%d_%d" % (half, first), [P, width], U8)
+            nc.vector.quantize_mx(out=h_codes[:].bitcast(FP8X4), scales=h_scales[:], in_=grouped_of[half, first][:])
             h_of[half, first] = (h_codes, h_scales)
 
-        def scores_of(half, first, width, on_vector_rows):
+        def scores_of(half, first, width, on_vector_rows, numbers):
             h_codes, h_scales = h_of[half, first]
             result = held("result%d_%d" % (half, first), [P, N // P, width], F32)
             for c in range(N // P):
                 rows = slice(c * P, (c + 1) * P)
-                scores = bank("lone", 4)
+                scores = bank(numbers[c])
                 nc.tensor.matmul_mx(
                     out=scores[:, 0:width], lhsT=w2_codes[:, rows].bitcast(FP8X4), lhsT_scale=w2_scales[:, rows],
                     rhs=h_codes[:].bitcast(FP8X4), rhs_scale=h_scales[:], start=True, stop=True,
@@ -295,27 +314,57 @@ def tile_list_coldchain_spoilage_scores_kernel(
             at = half * HALF + first
             nc.sync.dma_start(out_view[:, :, at : at + width], result[:])
 
-        cos_of, sin_of, h_of = {}, {}, {}
-        differences(0)
-        quantise_wd((0, 1))
-        quantise_wd((2, 3))
+        cos_of, sin_of, rows_of, grouped_of, h_of = {}, {}, {}, {}, {}
+        for half in range(2):
+            diffs[half] = held("diff%d" % half, [P, 4, HALF], F32)
+        routes = [bank(t) for t in range(4)]
+        for a in range(2):
+            for t in range(4):
+                route_pass(routes[t], 0, t, a)
         for t in range(4):
-            total_product(0, t)
-        half_angle_term()
-        for t in range(1, 4):
+            subtract(routes[t], 0, t)
+            if t == 1:
+                v[1, 1] = pick_words("v1_1", tab1_tile, lists, 1, "depot0_0")
+        for t in range(4):
             cosines(0, 0, HALF, (t,))
-        differences(1)
-        quantise_w2()
+            open_total(0, t, 4 + t)
+        def difference(t, number):
+            route = bank(number)
+            for a in range(2):
+                route_pass(route, 1, t, a)
+            subtract(route, 1, t)
+
+        quantise_from_gpsimd("wd", (0, 1), held("wd_codes_0", [P, 2 * P], U32, "depot0_2"))
+        difference(0, 0)
+        difference(1, 1)
+        close_total(0, 0)
+        close_total(0, 1)
+        quantise_from_gpsimd("wd", (2, 3), reused.tile([P, 2 * P], U32, name="wd_codes_2", offset=0, align_bytes=64))
+        difference(2, 2)
+        close_total(0, 2)
+        close_total(0, 3)
         sines(0, 0, HALF, range(4))
-        for t in range(4):
-            total_product(1, t)
-        quantise_h(0, 0, HALF)
+        difference(3, 4)
+        for n, number in enumerate((3, 5, 6, 7)):
+            total_piece(n * P, number)
+        products(0, 0, HALF)
+        w2_codes = held("w2_codes", [P, N], U32, "cosine0_0_2")
+        quantise_w2()
+        interleave(0, 0, HALF)
         pieces = ((0, 256), (256, 128), (384, 128))
         for first, width in pieces:
             cosines(1, first, width, (0, 1, 2, 3))
-            sines(1, first, width, range(4))
-        for first, width in pieces:
-            quantise_h(1, first, width)
-        scores_of(0, 0, HALF, ())
-        for first, width in pieces:
-            scores_of(1, first, width, (1,) if first + width == HALF else ())
+            piece_sines(first, width)
+        quantise_h(0, 0, HALF)
+        products(1, *pieces[0])
+        interleave(1, *pieces[0])
+        products(1, *pieces[1])
+        quantise_h(1, *pieces[0])
+        interleave(1, *pieces[1])
+        products(1, *pieces[2])
+        quantise_h(1, *pieces[1])
+        interleave(1, *pieces[2])
+        quantise_h(1, *pieces[2])
+        scores_of(0, 0, HALF, (), (0, 1))
+        for (first, width), numbers in zip(pieces, ((2, 4), (0, 1), (2, 4))):
+            scores_of(1, first, width, (1,) if first + width == HALF else (), numbers)

@@ -39,7 +39,7 @@ def tile_list_coldchain_spoilage_scores_kernel(
         tab_rows = held("tab_rows", [P, T], U8)
         tab2_rows = held("tab2_rows", [P, T], U8)
         w4_rows = held("w4_rows", [P, H], U8)
-        w8_rows = held("w8_rows", [P, H], U8)
+        w8_rows = reused.tile([P, H], U8, name="w8_rows", offset=16 * HALF + S + H // 2, align_bytes=64)
         planes = held("planes", [P, 2, S + H], U8)
         nc.vector.memset(tab_rows[:, 0 : T // 2].bitcast(I32), 0)
         nc.gpsimd.memset(tab_rows[:, T // 2 : T].bitcast(I32), 0)
@@ -73,10 +73,15 @@ def tile_list_coldchain_spoilage_scores_kernel(
                 )
 
         def permute(dst, src, words):
-            nc.gpsimd.tensor_copy(
+            nc.vector.tensor_copy(
                 dst.rearrange("p (t q w) -> p t q w", t=4, w=words),
                 src.rearrange("p (q t w) -> p t q w", t=4, w=words),
             )
+
+        def pick_words(picked, table, offsets, half):
+            cols = slice(half * HALF // 16, (half + 1) * HALF // 16)
+            nc.vector.tensor_copy(picked[:], table[:].bitcast(U32).indirect(offsets[:, cols]))
+            return picked
 
         w8_raw = load_words("w8_raw", w8_words[0])
         nc.sync.dma_start(lists[:], offs)
@@ -86,7 +91,6 @@ def tile_list_coldchain_spoilage_scores_kernel(
         nc.sync.dma_start(list2[:], offs2)
         tab_picked = held("tab_picked", [P, S], U8)
         tab2_plane = held("tab2_plane", [P, S], U8)
-        staged = held("staged", [P, S + H], U8)
         nc.vector.tensor_copy(tab_picked[:], tab_rows[:].indirect(lists[:]))
         load_plane(tab2_rows, tab2_scales[0], range(4))
         tab2_tile = load_words("tab2_tile", tab2_words[0])
@@ -95,6 +99,15 @@ def tile_list_coldchain_spoilage_scores_kernel(
         tab0_tile = load_words("tab0_tile", tab_words[0])
         raw["wr1"] = load_rows("wr1_raw", wr[512:1024, :], reused.tile([P, 4, H], F32, name="wr1_raw", offset=0))
         tab1_tile = load_words("tab1_tile", tab_words[1])
+        nc.vector.tensor_copy(tab2_plane[:], tab2_rows[:].indirect(list2[:]))
+        w8_codes = held("w8_codes", [P, H], I32)
+        permute(w8_codes[:], w8_raw[:], 8)
+        v2 = [pick_words(held("v2_0", [P, HALF], U32), tab2_tile, list2, 0)]
+        w8_plane = held("w8_plane", [P, H], U8)
+        permute(w8_plane[:].bitcast(I32), w8_rows[:].bitcast(I32), 2)
+        v2_second = reused.tile([P, HALF], U32, name="v2_1", offset=16 * HALF + S + H, align_bytes=64)
+        v2.append(pick_words(v2_second, tab2_tile, list2, 1))
+        staged = reused.tile([P, S + H], U8, name="staged", offset=16 * HALF, align_bytes=64)
         nc.vector.tensor_copy(staged[:, 0:S].bitcast(I32), tab_picked[:].bitcast(I32))
         permute(staged[:, S : S + H].bitcast(I32), w4_rows[:].bitcast(I32), 2)
         move_planes()
@@ -108,8 +121,8 @@ def tile_list_coldchain_spoilage_scores_kernel(
         shifts = held("shifts", [P, N // P], F32)
         with nc.allow_non_contiguous_dma(reason="one value a partition"):
             for t in range(4):
-                nc.gpsimd.dma_start(gains[:, t, 0:1], gain.rearrange("(q t i o) -> t q i o", t=4, i=8, o=1)[t])
-            nc.gpsimd.dma_start(shifts[:], shift.rearrange("(c p) -> p c", p=P))
+                nc.sync.dma_start(gains[:, t, 0:1], gain.rearrange("(q t i o) -> t q i o", t=4, i=8, o=1)[t])
+            nc.sync.dma_start(shifts[:], shift.rearrange("(c p) -> p c", p=P))
 
         def quantise_weight(name, slots, copy, after=None):
             width = len(slots) * P
@@ -142,23 +155,11 @@ def tile_list_coldchain_spoilage_scores_kernel(
             for n, t in enumerate(slots):
                 made[name, t] = (codes[:, n * P : (n + 1) * P], scales[:, n * P : (n + 1) * P])
 
-        def pick_words(name, table, offsets, half, after=None):
-            picked = held(name, [P, HALF], U32, after)
-            cols = slice(half * HALF // 16, (half + 1) * HALF // 16)
-            nc.vector.tensor_copy(picked[:], table[:].bitcast(U32).indirect(offsets[:, cols]))
-            return picked
-
         def bank(number):
             return psum.tile([P, HALF], F32, name="bank%d" % number)
 
         on_scalar, on_vector = nc.scalar.copy, nc.vector.tensor_copy
         made = {}
-        nc.vector.tensor_copy(tab2_plane[:], tab2_rows[:].indirect(list2[:]))
-        w8_plane = held("w8_plane", [P, H], U8)
-        permute(w8_plane[:].bitcast(I32), w8_rows[:].bitcast(I32), 2)
-        w8_codes = held("w8_codes", [P, H], I32)
-        permute(w8_codes[:], w8_raw[:], 8)
-        v2 = [pick_words("v2_0", tab2_tile, list2, 0), pick_words("v2_1", tab2_tile, list2, 1, "w8_rows")]
         quantise_weight("wr0", (0, 1, 2, 3), on_scalar, "tab2_tile")
 
         depot = {}
@@ -178,25 +179,26 @@ def tile_list_coldchain_spoilage_scores_kernel(
         depot_products(0, [held("depot0_%d" % t, [P, HALF], F32)[:] for t in range(4)])
         v = {}
         for half in range(2):
-            v[0, half] = pick_words("v0_%d" % half, tab0_tile, lists, half)
+            v[0, half] = pick_words(held("v0_%d" % half, [P, HALF], U32), tab0_tile, lists, half)
         quantise_weight("wr1", (0, 1), on_scalar)
-        v[1, 0] = pick_words("v1_0", tab1_tile, lists, 0)
-        quantise_from_gpsimd("wr1", (2, 3), held("wr1_2_codes", [P, 2 * P], U32))
+        v[1, 0] = pick_words(held("v1_0", [P, HALF], U32), tab1_tile, lists, 0)
+        quantise_weight("wr1", (2, 3), on_scalar)
         depot_products(1, [reused.tile([P, HALF], F32, name="depot1_%d" % t, offset=t * 4 * HALF)[:] for t in range(4)])
         w4_codes = held("w4_codes", [P, 2, H // 2], I32)
-        nc.gpsimd.tensor_copy(
+        nc.vector.tensor_copy(
             w4_codes[:].rearrange("p a (t q w) -> p a t q w", t=4, w=4),
             w4_raw[:].rearrange("p a (q t w) -> p a t q w", t=4, w=4),
         )
 
+        w2_grouped = held("w2_bf16", [P, 4 * N], BF16)
+
+        def round_w2():
+            nc.vector.tensor_copy(
+                w2_grouped[:].rearrange("p (u i t) -> p u t i", i=4, t=4),
+                w2_raw[:].rearrange("p t (u i) -> p u t i", i=4),
+            )
+
         def quantise_w2():
-            w2_grouped = held("w2_bf16", [P, 4 * N], BF16)
-            for c in range(N // P):
-                nc.gpsimd.tensor_scalar(
-                    w2_grouped[:, 4 * P * c : 4 * P * (c + 1)].rearrange("p (n t) -> p n t", t=4),
-                    w2_raw[:, :, P * c : P * (c + 1)].rearrange("p t n -> p n t"),
-                    1.0, 0.0, ALU.mult, ALU.add,
-                )
             nc.vector.quantize_mx(out=w2_codes[:].bitcast(FP8X4), scales=w2_scales[:], in_=w2_grouped[:])
 
         w2_scales = held("w2_scales", [P, N], U8)
@@ -284,18 +286,25 @@ def tile_list_coldchain_spoilage_scores_kernel(
                     ALU.mult, ALU.mult,
                 )
 
-        def interleave(half, first, width):
-            h_grouped = grouped_of[half, first] = held("h_grouped%d_%d" % (half, first), [P, 4 * width], BF16)
+        def interleave(half, first, width, part=slice(None)):
+            rows = rows_of[half, first][:, :, part]
+            h_grouped = held("h_grouped%d_%d_%s" % (half, first, part.start), [P, 4 * rows.shape[2]], BF16)
+            grouped_of[half, first, part.start] = h_grouped
             nc.vector.tensor_copy(
                 h_grouped[:].rearrange("p (u i t) -> p u t i", i=4, t=4),
-                rows_of[half, first][:].rearrange("p t (u i) -> p u t i", i=4),
+                rows.rearrange("p t (u i) -> p u t i", i=4),
             )
 
-        def quantise_h(half, first, width):
-            h_codes = held("h_codes%d_%d" % (half, first), [P, width], U32)
-            h_scales = held("h_scales%d_%d" % (half, first), [P, width], U8)
-            nc.vector.quantize_mx(out=h_codes[:].bitcast(FP8X4), scales=h_scales[:], in_=grouped_of[half, first][:])
-            h_of[half, first] = (h_codes, h_scales)
+        def quantise_h(half, first, width, part=slice(None)):
+            if (half, first) not in h_of:
+                h_of[half, first] = (
+                    held("h_codes%d_%d" % (half, first), [P, width], U32),
+                    held("h_scales%d_%d" % (half, first), [P, width], U8),
+                )
+            h_codes, h_scales = h_of[half, first]
+            nc.vector.quantize_mx(
+                out=h_codes[:, part].bitcast(FP8X4), scales=h_scales[:, part], in_=grouped_of[half, first, part.start][:]
+            )
 
         def scores_of(half, first, width, on_vector_rows, numbers):
             h_codes, h_scales = h_of[half, first]
@@ -315,8 +324,7 @@ def tile_list_coldchain_spoilage_scores_kernel(
             nc.sync.dma_start(out_view[:, :, at : at + width], result[:])
 
         cos_of, sin_of, rows_of, grouped_of, h_of = {}, {}, {}, {}, {}
-        for half in range(2):
-            diffs[half] = held("diff%d" % half, [P, 4, HALF], F32)
+        diffs[0] = held("diff0", [P, 4, HALF], F32)
         routes = [bank(t) for t in range(4)]
         for a in range(2):
             for t in range(4):
@@ -324,7 +332,7 @@ def tile_list_coldchain_spoilage_scores_kernel(
         for t in range(4):
             subtract(routes[t], 0, t)
             if t == 1:
-                v[1, 1] = pick_words("v1_1", tab1_tile, lists, 1, "depot0_0")
+                v[1, 1] = pick_words(held("v1_1", [P, HALF], U32, "depot0_0"), tab1_tile, lists, 1)
         for t in range(4):
             cosines(0, 0, HALF, (t,))
             open_total(0, t, 4 + t)
@@ -335,14 +343,16 @@ def tile_list_coldchain_spoilage_scores_kernel(
             subtract(route, 1, t)
 
         quantise_from_gpsimd("wd", (0, 1), held("wd_codes_0", [P, 2 * P], U32, "depot0_2"))
-        difference(0, 0)
-        difference(1, 1)
+        diffs[1] = held("diff1", [P, 4, HALF], F32, "wd_0_bf16")
         close_total(0, 0)
         close_total(0, 1)
+        difference(0, 0)
+        difference(1, 1)
         quantise_from_gpsimd("wd", (2, 3), reused.tile([P, 2 * P], U32, name="wd_codes_2", offset=0, align_bytes=64))
-        difference(2, 2)
         close_total(0, 2)
         close_total(0, 3)
+        difference(2, 2)
+        round_w2()
         sines(0, 0, HALF, range(4))
         difference(3, 4)
         for n, number in enumerate((3, 5, 6, 7)):
@@ -350,13 +360,16 @@ def tile_list_coldchain_spoilage_scores_kernel(
         products(0, 0, HALF)
         w2_codes = held("w2_codes", [P, N], U32, "cosine0_0_2")
         quantise_w2()
-        interleave(0, 0, HALF)
+        left, right = slice(0, HALF // 2), slice(HALF // 2, HALF)
+        interleave(0, 0, HALF, left)
+        interleave(0, 0, HALF, right)
+        quantise_h(0, 0, HALF, left)
         pieces = ((0, 256), (256, 128), (384, 128))
         for first, width in pieces:
             cosines(1, first, width, (0, 1, 2, 3))
             piece_sines(first, width)
-        quantise_h(0, 0, HALF)
         products(1, *pieces[0])
+        quantise_h(0, 0, HALF, right)
         interleave(1, *pieces[0])
         products(1, *pieces[1])
         quantise_h(1, *pieces[0])

@@ -38,13 +38,14 @@ def tile_list_coldchain_spoilage_scores_kernel(
         list2 = held("list2", [P, S // 16], U16)
         tab_rows = held("tab_rows", [P, T], U8)
         tab2_rows = held("tab2_rows", [P, T], U8)
-        w4_rows = held("w4_rows", [P, H], U8)
-        w8_rows = reused.tile([P, H], U8, name="w8_rows", offset=16 * HALF + S + H // 2, align_bytes=64)
-        planes = held("planes", [P, 2, S + H], U8)
+        w4_rows = held("w4_rows", [P, 2, H], U8)
+        w8_rows = held("w8_rows", [P, H], U8)
+        planes = held("planes", [P, 2, S], U8)
         nc.vector.memset(tab_rows[:, 0 : T // 2].bitcast(I32), 0)
         nc.gpsimd.memset(tab_rows[:, T // 2 : T].bitcast(I32), 0)
-        for rows in (tab2_rows, w4_rows, w8_rows):
-            nc.vector.memset(rows[:].bitcast(I32), 0)
+        nc.gpsimd.memset(w4_rows[:].rearrange("p a c -> p (a c)").bitcast(I32), 0)
+        nc.vector.memset(tab2_rows[:].bitcast(I32), 0)
+        nc.vector.memset(w8_rows[:].bitcast(I32), 0)
         nc.vector.memset(planes[:].rearrange("p a c -> p (a c)").bitcast(I32), 0)
         warm = held("warm", [P, 8], F32)
         nc.gpsimd.memset(warm[:], 0.0)
@@ -61,19 +62,19 @@ def tile_list_coldchain_spoilage_scores_kernel(
             nc.sync.dma_start(tile[:], words.rearrange("p n i -> p (n i)").bitcast(I32))
             return tile
 
-        def load_plane(rows, scales, quadrants):
-            for d in quadrants:
-                nc.sync.dma_start(rows[32 * d : 32 * d + 4, :].bitcast(I32), scales[4 * d : 4 * d + 4, :].bitcast(I32))
+        def load_plane(queue, rows, scales):
+            for d in range(4):
+                queue.dma_start(rows[32 * d : 32 * d + 4, :].bitcast(I32), scales[4 * d : 4 * d + 4, :].bitcast(I32))
 
         def move_planes():
             for d in range(4):
-                nc.sync.dma_start(
+                nc.gpsimd.dma_start(
                     planes[32 * d : 32 * d + 4, :, :].bitcast(I32),
-                    staged[32 * d : 32 * d + 32 : 4, :].bitcast(I32),
+                    tab_picked[32 * d : 32 * d + 32 : 4, :].bitcast(I32),
                 )
 
-        def permute(dst, src, words):
-            nc.vector.tensor_copy(
+        def permute(engine, dst, src, words):
+            engine.tensor_copy(
                 dst.rearrange("p (t q w) -> p t q w", t=4, w=words),
                 src.rearrange("p (q t w) -> p t q w", t=4, w=words),
             )
@@ -89,28 +90,28 @@ def tile_list_coldchain_spoilage_scores_kernel(
         raw = {}
         raw["wr0"] = load_rows("wr0_raw", wr[0:512, :])
         nc.sync.dma_start(list2[:], offs2)
-        tab_picked = held("tab_picked", [P, S], U8)
-        tab2_plane = held("tab2_plane", [P, S], U8)
-        nc.vector.tensor_copy(tab_picked[:], tab_rows[:].indirect(lists[:]))
-        load_plane(tab2_rows, tab2_scales[0], range(4))
+        load_plane(nc.sync, tab2_rows, tab2_scales[0])
         tab2_tile = load_words("tab2_tile", tab2_words[0])
-        nc.sync.dma_start(w4_rows[0:P:4, :].bitcast(I32), w4_scales.bitcast(I32).rearrange("a q c -> q a c"))
-        load_plane(w8_rows, w8_scales[0], range(4))
+        load_plane(nc.sync, w8_rows, w8_scales[0])
         tab0_tile = load_words("tab0_tile", tab_words[0])
         raw["wr1"] = load_rows("wr1_raw", wr[512:1024, :], reused.tile([P, 4, H], F32, name="wr1_raw", offset=0))
         tab1_tile = load_words("tab1_tile", tab_words[1])
-        nc.vector.tensor_copy(tab2_plane[:], tab2_rows[:].indirect(list2[:]))
+        for d in range(4):
+            nc.gpsimd.dma_start(
+                w4_rows[32 * d : 32 * d + 4, :, :].bitcast(I32),
+                w4_scales[:, 4 * d : 4 * d + 4, :].bitcast(I32).rearrange("a q c -> q a c"),
+            )
         w8_codes = held("w8_codes", [P, H], I32)
-        permute(w8_codes[:], w8_raw[:], 8)
+        permute(nc.vector, w8_codes[:], w8_raw[:], 8)
+        tab_picked = held("tab_picked", [P, S], U8)
+        nc.vector.tensor_copy(tab_picked[:], tab_rows[:].indirect(lists[:]))
+        move_planes()
+        tab2_plane = held("tab2_plane", [P, S], U8)
+        nc.vector.tensor_copy(tab2_plane[:], tab2_rows[:].indirect(list2[:]))
         v2 = [pick_words(held("v2_0", [P, HALF], U32), tab2_tile, list2, 0)]
         w8_plane = held("w8_plane", [P, H], U8)
-        permute(w8_plane[:].bitcast(I32), w8_rows[:].bitcast(I32), 2)
-        v2_second = reused.tile([P, HALF], U32, name="v2_1", offset=16 * HALF + S + H, align_bytes=64)
-        v2.append(pick_words(v2_second, tab2_tile, list2, 1))
-        staged = reused.tile([P, S + H], U8, name="staged", offset=16 * HALF, align_bytes=64)
-        nc.vector.tensor_copy(staged[:, 0:S].bitcast(I32), tab_picked[:].bitcast(I32))
-        permute(staged[:, S : S + H].bitcast(I32), w4_rows[:].bitcast(I32), 2)
-        move_planes()
+        permute(nc.vector, w8_plane[:].bitcast(I32), w8_rows[:].bitcast(I32), 2)
+        v2.append(pick_words(held("v2_1", [P, HALF], U32, "w8_rows"), tab2_tile, list2, 1))
         w4_raw = held("w4_raw", [P, 2, H // 2], I32)
         nc.sync.dma_start(w4_raw[:], w4_words.bitcast(I32).rearrange("a p c -> p a c"))
         raw["wd"] = load_rows("wd_raw", wd)
@@ -162,6 +163,11 @@ def tile_list_coldchain_spoilage_scores_kernel(
         made = {}
         quantise_weight("wr0", (0, 1, 2, 3), on_scalar, "tab2_tile")
 
+        w4_planes = held("w4_planes", [P, 2, H], U8, "wr0_0_bf16")
+        nc.gpsimd.tensor_copy(
+            w4_planes[:].bitcast(I32).rearrange("p a (t q w) -> p a t q w", t=4, w=2),
+            w4_rows[:].bitcast(I32).rearrange("p a (q t w) -> p a t q w", t=4, w=2),
+        )
         depot = {}
 
         def depot_products(half, tiles):
@@ -218,7 +224,7 @@ def tile_list_coldchain_spoilage_scores_kernel(
             for a in range(2):
                 nc.tensor.matmul_mx(
                     out=total[:], lhsT=w4_codes[:, a, t * P // 2 : (t + 1) * P // 2].bitcast(FP4X4),
-                    lhsT_scale=planes[:, a, S + t * P : S + (t + 1) * P], rhs=v[a, half][:].bitcast(FP8X4),
+                    lhsT_scale=w4_planes[:, a, t * P : (t + 1) * P], rhs=v[a, half][:].bitcast(FP8X4),
                     rhs_scale=planes[:, a, half * HALF : (half + 1) * HALF], start=(a == 0), stop=False,
                 )
 
@@ -237,7 +243,7 @@ def tile_list_coldchain_spoilage_scores_kernel(
                 for a in range(2):
                     nc.tensor.matmul_mx(
                         out=total[:, cols], lhsT=w4_codes[:, a, t * P // 2 : (t + 1) * P // 2].bitcast(FP4X4),
-                        lhsT_scale=planes[:, a, S + t * P : S + (t + 1) * P],
+                        lhsT_scale=w4_planes[:, a, t * P : (t + 1) * P],
                         rhs=v[a, 1][:, first : first + P].bitcast(FP8X4), rhs_scale=planes[:, a, at : at + P],
                         start=(a == 0), stop=False,
                     )

@@ -297,8 +297,8 @@ def tile_list_coldchain_spoilage_scores_kernel(
             h_grouped = held("h_grouped%d_%d_%s" % (half, first, part.start), [P, 4 * rows.shape[2]], BF16)
             grouped_of[half, first, part.start] = h_grouped
             nc.vector.tensor_copy(
-                h_grouped[:].rearrange("p (u i t) -> p u t i", i=4, t=4),
-                rows.rearrange("p t (u i) -> p u t i", i=4),
+                h_grouped[:].rearrange("p (c t) -> p c t", t=4),
+                rows.rearrange("p t c -> p c t"),
             )
 
         def quantise_h(half, first, width, part=slice(None)):

@@ -39,10 +39,9 @@ def tile_list_coldchain_spoilage_scores_kernel(
         tab_rows = held("tab_rows", [P, T], U8)
         tab2_rows = held("tab2_rows", [P, T], U8)
         w4_rows = held("w4_rows", [P, 2, H], U8)
-        w8_rows = held("w8_rows", [P, H], U8)
+        w8_rows = reused.tile([P, H], U8, name="w8_rows", offset=20 * HALF - H // 2, align_bytes=64)
         planes = held("planes", [P, 2, S], U8)
-        nc.vector.memset(tab_rows[:, 0 : T // 2].bitcast(I32), 0)
-        nc.gpsimd.memset(tab_rows[:, T // 2 : T].bitcast(I32), 0)
+        nc.vector.memset(tab_rows[:].bitcast(I32), 0)
         nc.gpsimd.memset(w4_rows[:].rearrange("p a c -> p (a c)").bitcast(I32), 0)
         nc.vector.memset(tab2_rows[:].bitcast(I32), 0)
         nc.vector.memset(w8_rows[:].bitcast(I32), 0)
@@ -68,7 +67,7 @@ def tile_list_coldchain_spoilage_scores_kernel(
 
         def move_planes():
             for d in range(4):
-                nc.gpsimd.dma_start(
+                nc.sync.dma_start(
                     planes[32 * d : 32 * d + 4, :, :].bitcast(I32),
                     tab_picked[32 * d : 32 * d + 32 : 4, :].bitcast(I32),
                 )
@@ -93,9 +92,7 @@ def tile_list_coldchain_spoilage_scores_kernel(
         load_plane(nc.sync, tab2_rows, tab2_scales[0])
         tab2_tile = load_words("tab2_tile", tab2_words[0])
         load_plane(nc.sync, w8_rows, w8_scales[0])
-        tab0_tile = load_words("tab0_tile", tab_words[0])
         raw["wr1"] = load_rows("wr1_raw", wr[512:1024, :], reused.tile([P, 4, H], F32, name="wr1_raw", offset=0))
-        tab1_tile = load_words("tab1_tile", tab_words[1])
         for d in range(4):
             nc.gpsimd.dma_start(
                 w4_rows[32 * d : 32 * d + 4, :, :].bitcast(I32),
@@ -106,12 +103,13 @@ def tile_list_coldchain_spoilage_scores_kernel(
         tab_picked = held("tab_picked", [P, S], U8)
         nc.vector.tensor_copy(tab_picked[:], tab_rows[:].indirect(lists[:]))
         move_planes()
+        tab0_tile = load_words("tab0_tile", tab_words[0])
+        tab1_tile = load_words("tab1_tile", tab_words[1])
         tab2_plane = held("tab2_plane", [P, S], U8)
         nc.vector.tensor_copy(tab2_plane[:], tab2_rows[:].indirect(list2[:]))
         v2 = [pick_words(held("v2_0", [P, HALF], U32), tab2_tile, list2, 0)]
         w8_plane = held("w8_plane", [P, H], U8)
         permute(nc.vector, w8_plane[:].bitcast(I32), w8_rows[:].bitcast(I32), 2)
-        v2.append(pick_words(held("v2_1", [P, HALF], U32, "w8_rows"), tab2_tile, list2, 1))
         w4_raw = held("w4_raw", [P, 2, H // 2], I32)
         nc.sync.dma_start(w4_raw[:], w4_words.bitcast(I32).rearrange("a p c -> p a c"))
         raw["wd"] = load_rows("wd_raw", wd)
@@ -125,24 +123,21 @@ def tile_list_coldchain_spoilage_scores_kernel(
                 nc.sync.dma_start(gains[:, t, 0:1], gain.rearrange("(q t i o) -> t q i o", t=4, i=8, o=1)[t])
             nc.sync.dma_start(shifts[:], shift.rearrange("(c p) -> p c", p=P))
 
-        def quantise_weight(name, slots, copy, after=None):
+        def quantise_weight(name, slots, copy, grouped, codes):
             width = len(slots) * P
             label = "%s_%d" % (name, slots[0])
-            grouped = held(label + "_bf16", [P, 4 * width], BF16)
             for n, t in enumerate(slots):
                 copy(
                     grouped[:, n * 4 * P : (n + 1) * 4 * P].rearrange("p (q u i j) -> p q u j i", u=2, i=4, j=4),
                     raw[name][:].rearrange("p j (q t u i) -> p t q u j i", t=4, u=2, i=4)[:, t],
                 )
-            codes = held(label + "_codes", [P, width], U32, after)
             scales = held(label + "_scales", [P, width], U8)
             nc.vector.quantize_mx(out=codes[:].bitcast(FP8X4), scales=scales[:], in_=grouped[:])
             for n, t in enumerate(slots):
                 made[name, t] = (codes[:, n * P : (n + 1) * P], scales[:, n * P : (n + 1) * P])
 
-        def quantise_from_gpsimd(name, slots, codes):
+        def quantise_from_gpsimd(name, slots, grouped, codes):
             width = len(slots) * P
-            grouped = held("%s_%d_bf16" % (name, slots[0]), [P, len(slots), 4 * P], BF16)
             for n, t in enumerate(slots):
                 nc.gpsimd.tensor_scalar(
                     grouped[:, n, :].rearrange("p (q i j) -> p q i j", i=8, j=4),
@@ -161,8 +156,9 @@ def tile_list_coldchain_spoilage_scores_kernel(
 
         on_scalar, on_vector = nc.scalar.copy, nc.vector.tensor_copy
         made = {}
-        quantise_weight("wr0", (0, 1, 2, 3), on_scalar, "tab2_tile")
+        quantise_weight("wr0", (0, 1, 2, 3), on_scalar, held("wr0_0_bf16", [P, 4 * H], BF16), reused.tile([P, H], U32, name="wr0_codes", offset=16 * HALF, align_bytes=64))
 
+        v2.append(pick_words(reused.tile([P, HALF], U32, name="v2_1", offset=20 * HALF, align_bytes=64), tab2_tile, list2, 1))
         w4_planes = held("w4_planes", [P, 2, H], U8, "wr0_0_bf16")
         nc.gpsimd.tensor_copy(
             w4_planes[:].bitcast(I32).rearrange("p a (t q w) -> p a t q w", t=4, w=2),
@@ -182,27 +178,33 @@ def tile_list_coldchain_spoilage_scores_kernel(
                 depot[half, t] = tiles[t]
                 nc.scalar.copy(tiles[t], product[:])
 
-        depot_products(0, [held("depot0_%d" % t, [P, HALF], F32)[:] for t in range(4)])
         v = {}
+        wr1_grouped = [
+            reused.tile([P, 2 * H], BF16, name="wr1_bf16_%d" % n, offset=(44 + 4 * n) * HALF, align_bytes=64)
+            for n in range(2)
+        ]
+        quantise_weight("wr1", (0, 1), on_scalar, wr1_grouped[0], held("wr1_codes_0", [P, 2 * P], U32))
         for half in range(2):
             v[0, half] = pick_words(held("v0_%d" % half, [P, HALF], U32), tab0_tile, lists, half)
-        quantise_weight("wr1", (0, 1), on_scalar)
+        quantise_weight("wr1", (2, 3), on_scalar, wr1_grouped[1], held("wr1_codes_2", [P, 2 * P], U32, "tab0_tile"))
         v[1, 0] = pick_words(held("v1_0", [P, HALF], U32), tab1_tile, lists, 0)
-        quantise_weight("wr1", (2, 3), on_scalar)
-        depot_products(1, [reused.tile([P, HALF], F32, name="depot1_%d" % t, offset=t * 4 * HALF)[:] for t in range(4)])
+        depot_products(0, [reused.tile([P, HALF], F32, name="depot0_%d" % t, offset=t * 4 * HALF)[:] for t in range(4)])
+        pairs = [reused.tile([P, 2, HALF], F32, name="depot1_%d" % n, offset=(41 + 8 * n) * HALF) for n in range(2)]
+        depot_products(1, [pairs[t // 2][:, t % 2, :] for t in range(4)])
         w4_codes = held("w4_codes", [P, 2, H // 2], I32)
         nc.vector.tensor_copy(
             w4_codes[:].rearrange("p a (t q w) -> p a t q w", t=4, w=4),
             w4_raw[:].rearrange("p a (q t w) -> p a t q w", t=4, w=4),
         )
 
-        w2_grouped = held("w2_bf16", [P, 4 * N], BF16)
 
         def round_w2():
-            nc.vector.tensor_copy(
-                w2_grouped[:].rearrange("p (u i t) -> p u t i", i=4, t=4),
-                w2_raw[:].rearrange("p t (u i) -> p u t i", i=4),
-            )
+            for c in range(N // P):
+                nc.gpsimd.tensor_scalar(
+                    w2_grouped[:, 4 * P * c : 4 * P * (c + 1)].rearrange("p (n t) -> p n t", t=4),
+                    w2_raw[:, :, P * c : P * (c + 1)].rearrange("p t n -> p n t"),
+                    1.0, 0.0, ALU.mult, ALU.add,
+                )
 
         def quantise_w2():
             nc.vector.quantize_mx(out=w2_codes[:].bitcast(FP8X4), scales=w2_scales[:], in_=w2_grouped[:])
@@ -267,12 +269,16 @@ def tile_list_coldchain_spoilage_scores_kernel(
                 sin_of[1, first, t] = sine[:, t, :]
 
         def subtract(route, half, t):
-            nc.vector.tensor_tensor(diffs[half][:, t, :], route[:], depot[half, t], ALU.subtract)
+            nc.vector.tensor_tensor(diffs[half, t // 2][:, t % 2, :], route[:], depot[half, t], ALU.subtract)
 
         def cosines(half, first, width, slots):
             cols = slice(first, first + width)
             size = keep.tile([P, len(slots), width], F32, name="size", bufs=2)
-            nc.scalar.activation(size[:], diffs[half][:, slots[0] : slots[-1] + 1, cols], ACT.Abs)
+            for n in range(0, len(slots), 2):
+                low, count = slots[n] % 2, min(2, len(slots))
+                nc.scalar.activation(
+                    size[:, n : n + count, :], diffs[half, slots[n] // 2][:, low : low + count, cols], ACT.Abs
+                )
             cosine = held("cosine%d_%d_%d" % (half, first, slots[0]), [P, len(slots), width], F32)
             nc.scalar.activation(cosine[:], size[:], ACT.Sin, bias=math.pi / 2, scale=-1.0)
             for n, t in enumerate(slots):
@@ -292,11 +298,11 @@ def tile_list_coldchain_spoilage_scores_kernel(
                     ALU.mult, ALU.mult,
                 )
 
-        def interleave(half, first, width, part=slice(None)):
+        def interleave(half, first, width, part=slice(None), copy=on_vector):
             rows = rows_of[half, first][:, :, part]
             h_grouped = held("h_grouped%d_%d_%s" % (half, first, part.start), [P, 4 * rows.shape[2]], BF16)
             grouped_of[half, first, part.start] = h_grouped
-            nc.vector.tensor_copy(
+            copy(
                 h_grouped[:].rearrange("p (c t) -> p c t", t=4),
                 rows.rearrange("p t c -> p c t"),
             )
@@ -314,6 +320,7 @@ def tile_list_coldchain_spoilage_scores_kernel(
 
         def scores_of(half, first, width, on_vector_rows, numbers):
             h_codes, h_scales = h_of[half, first]
+            at = half * HALF + first
             result = held("result%d_%d" % (half, first), [P, N // P, width], F32)
             for c in range(N // P):
                 rows = slice(c * P, (c + 1) * P)
@@ -326,11 +333,14 @@ def tile_list_coldchain_spoilage_scores_kernel(
                     nc.vector.tensor_scalar_add(result[:, c, :], scores[:, 0:width], shifts[:, c : c + 1])
                 else:
                     nc.scalar.activation(result[:, c, :], scores[:, 0:width], ACT.Identity, bias=shifts[:, c : c + 1])
-            at = half * HALF + first
-            nc.sync.dma_start(out_view[:, :, at : at + width], result[:])
+                if width == HALF:
+                    nc.sync.dma_start(out_view[:, c, at : at + width], result[:, c, :])
+            if width < HALF:
+                nc.sync.dma_start(out_view[:, :, at : at + width], result[:])
 
         cos_of, sin_of, rows_of, grouped_of, h_of = {}, {}, {}, {}, {}
-        diffs[0] = held("diff0", [P, 4, HALF], F32)
+        for half, pair in ((0, 0), (0, 1)):
+            diffs[half, pair] = held("diff%d_%d" % (half, pair), [P, 2, HALF], F32)
         routes = [bank(t) for t in range(4)]
         for a in range(2):
             for t in range(4):
@@ -338,7 +348,7 @@ def tile_list_coldchain_spoilage_scores_kernel(
         for t in range(4):
             subtract(routes[t], 0, t)
             if t == 1:
-                v[1, 1] = pick_words(held("v1_1", [P, HALF], U32, "depot0_0"), tab1_tile, lists, 1)
+                v[1, 1] = pick_words(reused.tile([P, HALF], U32, name="v1_1", offset=0, align_bytes=64), tab1_tile, lists, 1)
         for t in range(4):
             cosines(0, 0, HALF, (t,))
             open_total(0, t, 4 + t)
@@ -348,17 +358,21 @@ def tile_list_coldchain_spoilage_scores_kernel(
                 route_pass(route, 1, t, a)
             subtract(route, 1, t)
 
-        quantise_from_gpsimd("wd", (0, 1), held("wd_codes_0", [P, 2 * P], U32, "depot0_2"))
-        diffs[1] = held("diff1", [P, 4, HALF], F32, "wd_0_bf16")
+        first_pair = reused.tile([P, 2, 4 * P], BF16, name="wd_bf16_0", offset=62 * HALF, align_bytes=64)
+        quantise_from_gpsimd("wd", (0, 1), first_pair, reused.tile([P, 2 * P], U32, name="wd_codes_0", offset=8 * HALF, align_bytes=64))
         close_total(0, 0)
         close_total(0, 1)
+        diffs[1, 0] = reused.tile([P, 2, HALF], F32, name="diff1_0", offset=64 * HALF, align_bytes=64)
         difference(0, 0)
         difference(1, 1)
-        quantise_from_gpsimd("wd", (2, 3), reused.tile([P, 2 * P], U32, name="wd_codes_2", offset=0, align_bytes=64))
+        second_pair = reused.tile([P, 2, 4 * P], BF16, name="wd_bf16_2", offset=26 * HALF, align_bytes=64)
+        quantise_from_gpsimd("wd", (2, 3), second_pair, reused.tile([P, 2 * P], U32, name="wd_codes_2", offset=12 * HALF, align_bytes=64))
         close_total(0, 2)
         close_total(0, 3)
-        difference(2, 2)
+        w2_grouped = held("w2_bf16", [P, 4 * N], BF16)
         round_w2()
+        diffs[1, 1] = reused.tile([P, 2, HALF], F32, name="diff1_1", offset=28 * HALF, align_bytes=64)
+        difference(2, 2)
         sines(0, 0, HALF, range(4))
         difference(3, 4)
         for n, number in enumerate((3, 5, 6, 7)):
@@ -377,13 +391,13 @@ def tile_list_coldchain_spoilage_scores_kernel(
         products(1, *pieces[0])
         quantise_h(0, 0, HALF, right)
         interleave(1, *pieces[0])
+        scores_of(0, 0, HALF, (1,), (0, 1))
         products(1, *pieces[1])
         quantise_h(1, *pieces[0])
-        interleave(1, *pieces[1])
+        interleave(1, *pieces[1], copy=on_scalar)
         products(1, *pieces[2])
         quantise_h(1, *pieces[1])
         interleave(1, *pieces[2])
         quantise_h(1, *pieces[2])
-        scores_of(0, 0, HALF, (), (0, 1))
-        for (first, width), numbers in zip(pieces, ((2, 4), (0, 1), (2, 4))):
+        for (first, width), numbers in zip(pieces, ((2, 4), (3, 5), (6, 7))):
             scores_of(1, first, width, (1,) if first + width == HALF else (), numbers)

@@ -1,10 +1,7 @@
 import math
 from contextlib import ExitStack
 
-import concourse.mybir as mybir
-
-K, K2, T, S, H, N = 1024, 512, 2048, 1024, 512, 256
-FLOPS = 2 * S * H * (2 * K + 2 * K2) + 2 * S * H * N
+from concourse import mybir
 
 F32 = mybir.dt.float32
 BF16 = mybir.dt.bfloat16
@@ -18,158 +15,178 @@ ACT = mybir.ActivationFunctionType
 ALU = mybir.AluOpType
 
 P = 128
+T = 2048
+S = 1024
+H = 512
+N = 256
 HALF = 512
+SLOTS = 4
+GROUP = 16
+PIECES = ((0, 256), (256, 128), (384, 128))
+PIECE_BANKS = (3, 5, 6, 7)
+SCORE_BANKS = ((2, 4), (3, 5), (6, 7))
+
+PLACES = {
+    "wr1_raw": 0,
+    "depot0_0": 0, "depot0_1": 2048, "depot0_2": 4096, "depot0_3": 6144,
+    "v1_1": 0,
+    "wd_codes_0": 4096,
+    "wd_codes_2": 6144,
+    "wd_bf16_2": 13312,
+    "diff1_1": 14336,
+    "wr1_bf16_0": 22528, "wr1_bf16_2": 24576,
+    "depot1_0": 20992, "depot1_1": 25088,
+    "wd_bf16_0": 31744,
+    "diff1_0": 32768,
+}
 
 
 def tile_list_coldchain_spoilage_scores_kernel(
-    tc, tab_words, tab_scales, tab2_words, tab2_scales, offs, offs2,
-    w4_words, w4_scales, w8_words, w8_scales, wd, wr, gain, w2, shift, out,
+    tc, tab_words, tab_scales, tab2_words, tab2_scales, offs, offs2, w4_words, w4_scales, w8_words, w8_scales,
+    wd, wr, gain, w2, shift, out,
 ):
     nc = tc.nc
     with ExitStack() as ctx:
         keep = ctx.enter_context(tc.tile_pool(name="keep", bufs=1))
-        reused = ctx.enter_context(tc.tile_pool(name="reused", bufs=1))
+        shared = ctx.enter_context(tc.tile_pool(name="shared", bufs=1))
         psum = ctx.enter_context(tc.psum_pool(name="psum", bufs=1))
 
         def held(name, shape, dtype, after=None):
+            if name in PLACES:
+                return shared.tile(shape, dtype, name=name, offset=PLACES[name], align_bytes=64)
             return keep.tile(shape, dtype, name=name, tag=after or name, align_bytes=64)
 
-        lists = held("lists", [P, S // 16], U16)
-        list2 = held("list2", [P, S // 16], U16)
+        def bank(number):
+            return psum.tile([P, HALF], F32, name="bank%d" % number)
+
+        lists = held("lists", [P, S // GROUP], U16)
+        list2 = held("list2", [P, S // GROUP], U16)
         tab_rows = held("tab_rows", [P, T], U8)
         tab2_rows = held("tab2_rows", [P, T], U8)
         w4_rows = held("w4_rows", [P, 2, H], U8)
-        w8_rows = reused.tile([P, H], U8, name="w8_rows", offset=20 * HALF - H // 2, align_bytes=64)
+        w8_rows = held("w8_rows", [P, H], U8)
         planes = held("planes", [P, 2, S], U8)
         nc.vector.memset(tab_rows[:].bitcast(I32), 0)
-        nc.gpsimd.memset(w4_rows[:].rearrange("p a c -> p (a c)").bitcast(I32), 0)
+        nc.gpsimd.memset(w8_rows[:].bitcast(I32), 0)
         nc.vector.memset(tab2_rows[:].bitcast(I32), 0)
-        nc.vector.memset(w8_rows[:].bitcast(I32), 0)
-        nc.vector.memset(planes[:].rearrange("p a c -> p (a c)").bitcast(I32), 0)
-        warm = held("warm", [P, 8], F32)
-        nc.gpsimd.memset(warm[:], 0.0)
-        warmed = held("warmed", [P, 8], F32)
-        nc.scalar.activation(warmed[:], warm[:], ACT.Sin)
+        for rows in (planes, w4_rows):
+            nc.vector.memset(rows[:].rearrange("p a c -> p (a c)").bitcast(I32), 0)
+        zeros = held("zeros", [P, 8], F32)
+        nc.vector.memset(zeros[:], 0.0)
+        preload = held("preload", [P, 8], F32)
+        nc.scalar.activation(preload[:], zeros[:], ACT.Sin)
 
-        def load_rows(name, rows, raw=None):
-            raw = held(name, [P, 4, H], F32) if raw is None else raw
+        def load_rows(name, rows):
+            raw = held(name, [P, 4, H], F32)
             nc.sync.dma_start(raw[:], rows.rearrange("(p j) c -> p j c", j=4))
             return raw
 
         def load_words(name, words):
             tile = held(name, [P, words.shape[1]], I32)
-            nc.sync.dma_start(tile[:], words.rearrange("p n i -> p (n i)").bitcast(I32))
+            nc.sync.dma_start(tile[:], words.rearrange("p c b -> p (c b)").bitcast(I32))
             return tile
 
         def load_plane(queue, rows, scales):
             for d in range(4):
                 queue.dma_start(rows[32 * d : 32 * d + 4, :].bitcast(I32), scales[4 * d : 4 * d + 4, :].bitcast(I32))
 
-        def move_planes():
-            for d in range(4):
-                nc.sync.dma_start(
-                    planes[32 * d : 32 * d + 4, :, :].bitcast(I32),
-                    tab_picked[32 * d : 32 * d + 32 : 4, :].bitcast(I32),
-                )
-
-        def permute(engine, dst, src, words):
-            engine.tensor_copy(
-                dst.rearrange("p (t q w) -> p t q w", t=4, w=words),
-                src.rearrange("p (q t w) -> p t q w", t=4, w=words),
+        def by_slot(dst, src, words):
+            nc.vector.tensor_copy(
+                dst.rearrange("p (t q w) -> p t q w", t=SLOTS, w=words),
+                src.rearrange("p (q t w) -> p t q w", t=SLOTS, w=words),
             )
 
-        def pick_words(picked, table, offsets, half):
-            cols = slice(half * HALF // 16, (half + 1) * HALF // 16)
+        def pick_words(name, table, offsets, half):
+            picked = held(name, [P, HALF], U32)
+            cols = slice(half * HALF // GROUP, (half + 1) * HALF // GROUP)
             nc.vector.tensor_copy(picked[:], table[:].bitcast(U32).indirect(offsets[:, cols]))
             return picked
 
         w8_raw = load_words("w8_raw", w8_words[0])
         nc.sync.dma_start(lists[:], offs)
         nc.sync.dma_start(tab_rows[0:P:4, :].bitcast(I32), tab_scales.bitcast(I32).rearrange("a q t -> q a t"))
-        raw = {}
-        raw["wr0"] = load_rows("wr0_raw", wr[0:512, :])
+        raw = {"wr0": load_rows("wr0_raw", wr[0:512, :])}
         nc.sync.dma_start(list2[:], offs2)
         load_plane(nc.sync, tab2_rows, tab2_scales[0])
         tab2_tile = load_words("tab2_tile", tab2_words[0])
-        load_plane(nc.sync, w8_rows, w8_scales[0])
-        raw["wr1"] = load_rows("wr1_raw", wr[512:1024, :], reused.tile([P, 4, H], F32, name="wr1_raw", offset=0))
+        raw["wr1"] = load_rows("wr1_raw", wr[512:1024, :])
+        load_plane(nc.gpsimd, w8_rows, w8_scales[0])
+        w8_codes = held("w8_codes", [P, H], I32)
+        by_slot(w8_codes[:], w8_raw[:], 8)
+        tab_picked = held("tab_picked", [P, S], U8)
+        nc.vector.tensor_copy(tab_picked[:], tab_rows[:].indirect(lists[:]))
+        for d in range(4):
+            nc.gpsimd.dma_start(
+                planes[32 * d : 32 * d + 4, :, :].bitcast(I32), tab_picked[32 * d : 32 * d + 32 : 4, :].bitcast(I32)
+            )
         for d in range(4):
             nc.gpsimd.dma_start(
                 w4_rows[32 * d : 32 * d + 4, :, :].bitcast(I32),
                 w4_scales[:, 4 * d : 4 * d + 4, :].bitcast(I32).rearrange("a q c -> q a c"),
             )
-        w8_codes = held("w8_codes", [P, H], I32)
-        permute(nc.vector, w8_codes[:], w8_raw[:], 8)
-        tab_picked = held("tab_picked", [P, S], U8)
-        nc.vector.tensor_copy(tab_picked[:], tab_rows[:].indirect(lists[:]))
-        move_planes()
         tab0_tile = load_words("tab0_tile", tab_words[0])
         tab1_tile = load_words("tab1_tile", tab_words[1])
         tab2_plane = held("tab2_plane", [P, S], U8)
         nc.vector.tensor_copy(tab2_plane[:], tab2_rows[:].indirect(list2[:]))
-        v2 = [pick_words(held("v2_0", [P, HALF], U32), tab2_tile, list2, 0)]
-        w8_plane = held("w8_plane", [P, H], U8)
-        permute(nc.vector, w8_plane[:].bitcast(I32), w8_rows[:].bitcast(I32), 2)
         w4_raw = held("w4_raw", [P, 2, H // 2], I32)
         nc.sync.dma_start(w4_raw[:], w4_words.bitcast(I32).rearrange("a p c -> p a c"))
         raw["wd"] = load_rows("wd_raw", wd)
-        w2_raw = held("w2_raw", [P, 4, N], F32)
-        for t in range(4):
-            nc.sync.dma_start(w2_raw[:, t, :], w2.rearrange("(q t i) n -> t q i n", t=4, i=8)[t])
-        gains = held("gains", [P, 4, 8], F32)
+        w2_raw = held("w2_raw", [P, SLOTS, N], F32)
+        for t in range(SLOTS):
+            nc.sync.dma_start(w2_raw[:, t, :], w2.rearrange("(q t i) n -> t q i n", t=SLOTS, i=8)[t])
+        gains = held("gains", [P, SLOTS, 8], F32)
         shifts = held("shifts", [P, N // P], F32)
         with nc.allow_non_contiguous_dma(reason="one value a partition"):
-            for t in range(4):
-                nc.sync.dma_start(gains[:, t, 0:1], gain.rearrange("(q t i o) -> t q i o", t=4, i=8, o=1)[t])
+            for t in range(SLOTS):
+                nc.sync.dma_start(gains[:, t, 0:1], gain.rearrange("(q t i o) -> t q i o", t=SLOTS, i=8, o=1)[t])
             nc.sync.dma_start(shifts[:], shift.rearrange("(c p) -> p c", p=P))
 
-        def quantise_weight(name, slots, copy, grouped, codes):
+        def round_on_scalar(grouped, rows, t):
+            nc.scalar.copy(
+                grouped.rearrange("p (q u i j) -> p q u j i", u=2, i=4, j=4),
+                rows.rearrange("p j (q t u i) -> p t q u j i", t=SLOTS, u=2, i=4)[:, t],
+            )
+
+        def round_on_gpsimd(grouped, rows, t):
+            nc.gpsimd.tensor_scalar(
+                grouped.rearrange("p (q i j) -> p q i j", i=8, j=4),
+                rows.rearrange("p j (q t i) -> p t q i j", t=SLOTS, i=8)[:, t],
+                1.0, 0.0, ALU.mult, ALU.add,
+            )
+
+        made = {}
+
+        def quantise_weight(name, slots, rounding, codes_name, after=None):
             width = len(slots) * P
-            label = "%s_%d" % (name, slots[0])
+            grouped = held("%s_bf16_%d" % (name, slots[0]), [P, 4 * width], BF16)
             for n, t in enumerate(slots):
-                copy(
-                    grouped[:, n * 4 * P : (n + 1) * 4 * P].rearrange("p (q u i j) -> p q u j i", u=2, i=4, j=4),
-                    raw[name][:].rearrange("p j (q t u i) -> p t q u j i", t=4, u=2, i=4)[:, t],
-                )
-            scales = held(label + "_scales", [P, width], U8)
+                rounding(grouped[:, n * 4 * P : (n + 1) * 4 * P], raw[name][:], t)
+            codes = held(codes_name, [P, width], U32, after)
+            scales = held("%s_scales_%d" % (name, slots[0]), [P, width], U8)
             nc.vector.quantize_mx(out=codes[:].bitcast(FP8X4), scales=scales[:], in_=grouped[:])
             for n, t in enumerate(slots):
                 made[name, t] = (codes[:, n * P : (n + 1) * P], scales[:, n * P : (n + 1) * P])
 
-        def quantise_from_gpsimd(name, slots, grouped, codes):
-            width = len(slots) * P
-            for n, t in enumerate(slots):
-                nc.gpsimd.tensor_scalar(
-                    grouped[:, n, :].rearrange("p (q i j) -> p q i j", i=8, j=4),
-                    raw[name][:].rearrange("p j (q t i) -> p t q i j", t=4, i=8)[:, t],
-                    1.0, 0.0, ALU.mult, ALU.add,
-                )
-            scales = held("%s_%d_scales" % (name, slots[0]), [P, width], U8)
-            nc.vector.quantize_mx(
-                out=codes[:].bitcast(FP8X4), scales=scales[:], in_=grouped[:].rearrange("p t c -> p (t c)")
-            )
-            for n, t in enumerate(slots):
-                made[name, t] = (codes[:, n * P : (n + 1) * P], scales[:, n * P : (n + 1) * P])
-
-        def bank(number):
-            return psum.tile([P, HALF], F32, name="bank%d" % number)
-
-        on_scalar, on_vector = nc.scalar.copy, nc.vector.tensor_copy
-        made = {}
-        quantise_weight("wr0", (0, 1, 2, 3), on_scalar, held("wr0_0_bf16", [P, 4 * H], BF16), reused.tile([P, H], U32, name="wr0_codes", offset=16 * HALF, align_bytes=64))
-
-        v2.append(pick_words(reused.tile([P, HALF], U32, name="v2_1", offset=20 * HALF, align_bytes=64), tab2_tile, list2, 1))
-        w4_planes = held("w4_planes", [P, 2, H], U8, "wr0_0_bf16")
+        quantise_weight("wr0", range(SLOTS), round_on_scalar, "wr0_codes", after="tab2_rows")
+        v2 = [pick_words("v2_%d" % half, tab2_tile, list2, half) for half in range(2)]
+        w8_plane = held("w8_plane", [P, H], U8, after="tab2_tile")
+        by_slot(w8_plane[:].bitcast(I32), w8_rows[:].bitcast(I32), 2)
+        w4_planes = held("w4_planes", [P, 2, H], U8, after="wr0_bf16_0")
         nc.gpsimd.tensor_copy(
-            w4_planes[:].bitcast(I32).rearrange("p a (t q w) -> p a t q w", t=4, w=2),
-            w4_rows[:].bitcast(I32).rearrange("p a (q t w) -> p a t q w", t=4, w=2),
+            w4_planes[:].bitcast(I32).rearrange("p a (t q w) -> p a t q w", t=SLOTS, w=2),
+            w4_rows[:].bitcast(I32).rearrange("p a (q t w) -> p a t q w", t=SLOTS, w=2),
         )
+        quantise_weight("wr1", (0, 1), round_on_scalar, "wr1_codes_0")
+        v = {(0, half): pick_words("v0_%d" % half, tab0_tile, lists, half) for half in range(2)}
+        quantise_weight("wr1", (2, 3), round_on_scalar, "wr1_codes_2", after="tab0_tile")
+        v[1, 0] = pick_words("v1_0", tab1_tile, lists, 0)
+
         depot = {}
 
         def depot_products(half, tiles):
-            for t in range(4):
+            for t in range(SLOTS):
                 cols = slice(t * P, (t + 1) * P)
-                product = bank(4 * half + t)
+                product = bank(SLOTS * half + t)
                 nc.tensor.matmul_mx(
                     out=product[:], lhsT=w8_codes[:, cols].bitcast(FP8X4), lhsT_scale=w8_plane[:, cols],
                     rhs=v2[half][:].bitcast(FP8X4), rhs_scale=tab2_plane[:, half * HALF : (half + 1) * HALF],
@@ -178,41 +195,16 @@ def tile_list_coldchain_spoilage_scores_kernel(
                 depot[half, t] = tiles[t]
                 nc.scalar.copy(tiles[t], product[:])
 
-        v = {}
-        wr1_grouped = [
-            reused.tile([P, 2 * H], BF16, name="wr1_bf16_%d" % n, offset=(44 + 4 * n) * HALF, align_bytes=64)
-            for n in range(2)
-        ]
-        quantise_weight("wr1", (0, 1), on_scalar, wr1_grouped[0], held("wr1_codes_0", [P, 2 * P], U32))
-        for half in range(2):
-            v[0, half] = pick_words(held("v0_%d" % half, [P, HALF], U32), tab0_tile, lists, half)
-        quantise_weight("wr1", (2, 3), on_scalar, wr1_grouped[1], held("wr1_codes_2", [P, 2 * P], U32, "tab0_tile"))
-        v[1, 0] = pick_words(held("v1_0", [P, HALF], U32), tab1_tile, lists, 0)
-        depot_products(0, [reused.tile([P, HALF], F32, name="depot0_%d" % t, offset=t * 4 * HALF)[:] for t in range(4)])
-        pairs = [reused.tile([P, 2, HALF], F32, name="depot1_%d" % n, offset=(41 + 8 * n) * HALF) for n in range(2)]
-        depot_products(1, [pairs[t // 2][:, t % 2, :] for t in range(4)])
+        depot_products(0, [held("depot0_%d" % t, [P, HALF], F32)[:] for t in range(SLOTS)])
+        pairs = [held("depot1_%d" % n, [P, 2, HALF], F32) for n in range(2)]
+        depot_products(1, [pairs[t // 2][:, t % 2, :] for t in range(SLOTS)])
         w4_codes = held("w4_codes", [P, 2, H // 2], I32)
         nc.vector.tensor_copy(
-            w4_codes[:].rearrange("p a (t q w) -> p a t q w", t=4, w=4),
-            w4_raw[:].rearrange("p a (q t w) -> p a t q w", t=4, w=4),
+            w4_codes[:].rearrange("p a (t q w) -> p a t q w", t=SLOTS, w=4),
+            w4_raw[:].rearrange("p a (q t w) -> p a t q w", t=SLOTS, w=4),
         )
 
-
-        def round_w2():
-            for c in range(N // P):
-                nc.gpsimd.tensor_scalar(
-                    w2_grouped[:, 4 * P * c : 4 * P * (c + 1)].rearrange("p (n t) -> p n t", t=4),
-                    w2_raw[:, :, P * c : P * (c + 1)].rearrange("p t n -> p n t"),
-                    1.0, 0.0, ALU.mult, ALU.add,
-                )
-
-        def quantise_w2():
-            nc.vector.quantize_mx(out=w2_codes[:].bitcast(FP8X4), scales=w2_scales[:], in_=w2_grouped[:])
-
-        w2_scales = held("w2_scales", [P, N], U8)
-
-        out_view = out.rearrange("(c p) j -> p c j", p=P)
-        totals, diffs = {}, {}
+        totals, diffs, cos_of, sin_of, rows_of, grouped_of, h_of = {}, {}, {}, {}, {}, {}, {}
 
         def route_pass(route, half, t, a):
             codes, scales = made["wr%d" % a, t]
@@ -221,102 +213,88 @@ def tile_list_coldchain_spoilage_scores_kernel(
                 rhs_scale=planes[:, a, half * HALF : (half + 1) * HALF], start=(a == 0), stop=(a == 1),
             )
 
-        def open_total(half, t, number):
-            total = totals[half, t] = bank(number)
-            for a in range(2):
-                nc.tensor.matmul_mx(
-                    out=total[:], lhsT=w4_codes[:, a, t * P // 2 : (t + 1) * P // 2].bitcast(FP4X4),
-                    lhsT_scale=w4_planes[:, a, t * P : (t + 1) * P], rhs=v[a, half][:].bitcast(FP8X4),
-                    rhs_scale=planes[:, a, half * HALF : (half + 1) * HALF], start=(a == 0), stop=False,
-                )
-
-        def close_total(half, t):
-            codes, scales = made["wd", t]
-            nc.tensor.matmul_mx(
-                out=totals[half, t][:], lhsT=codes.bitcast(FP8X4), lhsT_scale=scales, rhs=v2[half][:].bitcast(FP8X4),
-                rhs_scale=tab2_plane[:, half * HALF : (half + 1) * HALF], start=False, stop=True,
-            )
-
-        def total_piece(first, number):
-            total = totals[1, first] = bank(number)
-            at = HALF + first
-            for t in range(4):
-                cols = slice(t * P, (t + 1) * P)
-                for a in range(2):
-                    nc.tensor.matmul_mx(
-                        out=total[:, cols], lhsT=w4_codes[:, a, t * P // 2 : (t + 1) * P // 2].bitcast(FP4X4),
-                        lhsT_scale=w4_planes[:, a, t * P : (t + 1) * P],
-                        rhs=v[a, 1][:, first : first + P].bitcast(FP8X4), rhs_scale=planes[:, a, at : at + P],
-                        start=(a == 0), stop=False,
-                    )
-                codes, scales = made["wd", t]
-                nc.tensor.matmul_mx(
-                    out=total[:, cols], lhsT=codes.bitcast(FP8X4), lhsT_scale=scales,
-                    rhs=v2[1][:, first : first + P].bitcast(FP8X4), rhs_scale=tab2_plane[:, at : at + P],
-                    start=False, stop=True,
-                )
-
-        def piece_sines(first, width):
-            sine = held("sine1_%d" % first, [P, 4, width], F32)
-            for at in range(first, first + width, P):
-                step = min(P, width)
-                nc.scalar.activation(
-                    sine[:, :, at - first : at - first + step],
-                    totals[1, at - at % P][:].rearrange("p (t c) -> p t c", t=4)[:, :, at % P : at % P + step],
-                    ACT.Sin,
-                )
-            for t in range(4):
-                sin_of[1, first, t] = sine[:, t, :]
-
         def subtract(route, half, t):
             nc.vector.tensor_tensor(diffs[half, t // 2][:, t % 2, :], route[:], depot[half, t], ALU.subtract)
 
+        def second_difference(t, number):
+            route = bank(number)
+            for a in range(2):
+                route_pass(route, 1, t, a)
+            subtract(route, 1, t)
+
+        def open_total(total, t, half, first, width):
+            at = half * HALF + first
+            for a in range(2):
+                nc.tensor.matmul_mx(
+                    out=total, lhsT=w4_codes[:, a, t * P // 2 : (t + 1) * P // 2].bitcast(FP4X4),
+                    lhsT_scale=w4_planes[:, a, t * P : (t + 1) * P],
+                    rhs=v[a, half][:, first : first + width].bitcast(FP8X4), rhs_scale=planes[:, a, at : at + width],
+                    start=(a == 0), stop=False,
+                )
+
+        def close_total(total, t, half, first, width):
+            at = half * HALF + first
+            codes, scales = made["wd", t]
+            nc.tensor.matmul_mx(
+                out=total, lhsT=codes.bitcast(FP8X4), lhsT_scale=scales,
+                rhs=v2[half][:, first : first + width].bitcast(FP8X4), rhs_scale=tab2_plane[:, at : at + width],
+                start=False, stop=True,
+            )
+
         def cosines(half, first, width, slots):
-            cols = slice(first, first + width)
             size = keep.tile([P, len(slots), width], F32, name="size", bufs=2)
             for n in range(0, len(slots), 2):
                 low, count = slots[n] % 2, min(2, len(slots))
                 nc.scalar.activation(
-                    size[:, n : n + count, :], diffs[half, slots[n] // 2][:, low : low + count, cols], ACT.Abs
+                    size[:, n : n + count, :], diffs[half, slots[n] // 2][:, low : low + count, first : first + width],
+                    ACT.Abs,
                 )
             cosine = held("cosine%d_%d_%d" % (half, first, slots[0]), [P, len(slots), width], F32)
             nc.scalar.activation(cosine[:], size[:], ACT.Sin, bias=math.pi / 2, scale=-1.0)
             for n, t in enumerate(slots):
                 cos_of[half, first, t] = cosine[:, n, :]
 
-        def sines(half, first, width, slots):
-            for t in slots:
-                sine = held("sine%d_%d_%d" % (half, first, t), [P, width], F32)
-                nc.scalar.activation(sine[:], totals[half, t][:, first : first + width], ACT.Sin)
-                sin_of[half, first, t] = sine[:]
+        def piece_sines(first, width):
+            sine = held("sine1_%d" % first, [P, SLOTS, width], F32)
+            for at in range(first, first + width, P):
+                nc.scalar.activation(
+                    sine[:, :, at - first : at - first + P], totals[1, at][:].rearrange("p (t c) -> p t c", t=SLOTS),
+                    ACT.Sin,
+                )
+            for t in range(SLOTS):
+                sin_of[1, first, t] = sine[:, t, :]
 
         def products(half, first, width):
-            h_rows = rows_of[half, first] = held("h_rows%d_%d" % (half, first), [P, 4, width], BF16)
-            for t in range(4):
+            h_rows = rows_of[half, first] = held("h_rows%d_%d" % (half, first), [P, SLOTS, width], BF16)
+            for t in range(SLOTS):
                 nc.vector.scalar_tensor_tensor(
                     h_rows[:, t, :], cos_of[half, first, t], gains[:, t, 0:1], sin_of[half, first, t],
                     ALU.mult, ALU.mult,
                 )
 
-        def interleave(half, first, width, part=slice(None), copy=on_vector):
-            rows = rows_of[half, first][:, :, part]
-            h_grouped = held("h_grouped%d_%d_%s" % (half, first, part.start), [P, 4 * rows.shape[2]], BF16)
-            grouped_of[half, first, part.start] = h_grouped
+        def interleave(half, first, start, width, copy):
+            h_grouped = grouped_of[half, first + start] = held(
+                "h_grouped%d_%d" % (half, first + start), [P, SLOTS * width], BF16
+            )
             copy(
-                h_grouped[:].rearrange("p (c t) -> p c t", t=4),
-                rows.rearrange("p t c -> p c t"),
+                h_grouped[:].rearrange("p (c t) -> p c t", t=SLOTS),
+                rows_of[half, first][:, :, start : start + width].rearrange("p t c -> p c t"),
             )
 
-        def quantise_h(half, first, width, part=slice(None)):
-            if (half, first) not in h_of:
-                h_of[half, first] = (
-                    held("h_codes%d_%d" % (half, first), [P, width], U32),
-                    held("h_scales%d_%d" % (half, first), [P, width], U8),
-                )
-            h_codes, h_scales = h_of[half, first]
-            nc.vector.quantize_mx(
-                out=h_codes[:, part].bitcast(FP8X4), scales=h_scales[:, part], in_=grouped_of[half, first, part.start][:]
+        def h_tiles(half, first, width):
+            h_of[half, first] = (
+                held("h_codes%d_%d" % (half, first), [P, width], U32),
+                held("h_scales%d_%d" % (half, first), [P, width], U8),
             )
+
+        def quantise_h(half, first, start, width):
+            h_codes, h_scales = h_of[half, first]
+            cols = slice(start, start + width)
+            nc.vector.quantize_mx(
+                out=h_codes[:, cols].bitcast(FP8X4), scales=h_scales[:, cols], in_=grouped_of[half, first + start][:]
+            )
+
+        out_view = out.rearrange("(c p) j -> p c j", p=P)
 
         def scores_of(half, first, width, on_vector_rows, numbers):
             h_codes, h_scales = h_of[half, first]
@@ -333,71 +311,76 @@ def tile_list_coldchain_spoilage_scores_kernel(
                     nc.vector.tensor_scalar_add(result[:, c, :], scores[:, 0:width], shifts[:, c : c + 1])
                 else:
                     nc.scalar.activation(result[:, c, :], scores[:, 0:width], ACT.Identity, bias=shifts[:, c : c + 1])
-                if width == HALF:
+                if half == 0:
                     nc.sync.dma_start(out_view[:, c, at : at + width], result[:, c, :])
-            if width < HALF:
+            if half == 1:
                 nc.sync.dma_start(out_view[:, :, at : at + width], result[:])
 
-        cos_of, sin_of, rows_of, grouped_of, h_of = {}, {}, {}, {}, {}
-        for half, pair in ((0, 0), (0, 1)):
-            diffs[half, pair] = held("diff%d_%d" % (half, pair), [P, 2, HALF], F32)
-        routes = [bank(t) for t in range(4)]
+        for pair in range(2):
+            diffs[0, pair] = held("diff0_%d" % pair, [P, 2, HALF], F32)
+        routes = [bank(t) for t in range(SLOTS)]
         for a in range(2):
-            for t in range(4):
+            for t in range(SLOTS):
                 route_pass(routes[t], 0, t, a)
-        for t in range(4):
+        for t in range(SLOTS):
             subtract(routes[t], 0, t)
             if t == 1:
-                v[1, 1] = pick_words(reused.tile([P, HALF], U32, name="v1_1", offset=0, align_bytes=64), tab1_tile, lists, 1)
-        for t in range(4):
+                v[1, 1] = pick_words("v1_1", tab1_tile, lists, 1)
+        for t in range(SLOTS):
             cosines(0, 0, HALF, (t,))
-            open_total(0, t, 4 + t)
-        def difference(t, number):
-            route = bank(number)
-            for a in range(2):
-                route_pass(route, 1, t, a)
-            subtract(route, 1, t)
+            totals[0, t] = bank(SLOTS + t)
+            open_total(totals[0, t][:], t, 0, 0, HALF)
+        for pair in range(2):
+            slots = (2 * pair, 2 * pair + 1)
+            quantise_weight("wd", slots, round_on_gpsimd, "wd_codes_%d" % slots[0])
+            for t in slots:
+                close_total(totals[0, t][:], t, 0, 0, HALF)
+            if pair == 0:
+                diffs[1, 0] = held("diff1_0", [P, 2, HALF], F32)
+                second_difference(0, 0)
+                second_difference(1, 1)
+        w2_grouped = held("w2_bf16", [P, SLOTS * N], BF16)
+        for c in range(N // P):
+            nc.gpsimd.tensor_scalar(
+                w2_grouped[:, SLOTS * P * c : SLOTS * P * (c + 1)].rearrange("p (n t) -> p n t", t=SLOTS),
+                w2_raw[:, :, P * c : P * (c + 1)].rearrange("p t n -> p n t"),
+                1.0, 0.0, ALU.mult, ALU.add,
+            )
+        diffs[1, 1] = held("diff1_1", [P, 2, HALF], F32)
+        second_difference(2, 2)
+        for t in range(SLOTS):
+            sine = held("sine0_%d" % t, [P, HALF], F32)
+            nc.scalar.activation(sine[:], totals[0, t][:], ACT.Sin)
+            sin_of[0, 0, t] = sine[:]
+        second_difference(3, SLOTS)
+        for n, number in enumerate(PIECE_BANKS):
+            total = totals[1, n * P] = bank(number)
+            for t in range(SLOTS):
+                open_total(total[:, t * P : (t + 1) * P], t, 1, n * P, P)
+                close_total(total[:, t * P : (t + 1) * P], t, 1, n * P, P)
 
-        first_pair = reused.tile([P, 2, 4 * P], BF16, name="wd_bf16_0", offset=62 * HALF, align_bytes=64)
-        quantise_from_gpsimd("wd", (0, 1), first_pair, reused.tile([P, 2 * P], U32, name="wd_codes_0", offset=8 * HALF, align_bytes=64))
-        close_total(0, 0)
-        close_total(0, 1)
-        diffs[1, 0] = reused.tile([P, 2, HALF], F32, name="diff1_0", offset=64 * HALF, align_bytes=64)
-        difference(0, 0)
-        difference(1, 1)
-        second_pair = reused.tile([P, 2, 4 * P], BF16, name="wd_bf16_2", offset=26 * HALF, align_bytes=64)
-        quantise_from_gpsimd("wd", (2, 3), second_pair, reused.tile([P, 2 * P], U32, name="wd_codes_2", offset=12 * HALF, align_bytes=64))
-        close_total(0, 2)
-        close_total(0, 3)
-        w2_grouped = held("w2_bf16", [P, 4 * N], BF16)
-        round_w2()
-        diffs[1, 1] = reused.tile([P, 2, HALF], F32, name="diff1_1", offset=28 * HALF, align_bytes=64)
-        difference(2, 2)
-        sines(0, 0, HALF, range(4))
-        difference(3, 4)
-        for n, number in enumerate((3, 5, 6, 7)):
-            total_piece(n * P, number)
+        on_scalar, on_vector = nc.scalar.copy, nc.vector.tensor_copy
         products(0, 0, HALF)
-        w2_codes = held("w2_codes", [P, N], U32, "cosine0_0_2")
-        quantise_w2()
-        left, right = slice(0, HALF // 2), slice(HALF // 2, HALF)
-        interleave(0, 0, HALF, left)
-        interleave(0, 0, HALF, right)
-        quantise_h(0, 0, HALF, left)
-        pieces = ((0, 256), (256, 128), (384, 128))
-        for first, width in pieces:
-            cosines(1, first, width, (0, 1, 2, 3))
+        w2_codes = held("w2_codes", [P, N], U32, after="cosine0_0_2")
+        w2_scales = held("w2_scales", [P, N], U8)
+        nc.vector.quantize_mx(out=w2_codes[:].bitcast(FP8X4), scales=w2_scales[:], in_=w2_grouped[:])
+        quarter = HALF // 2
+        h_tiles(0, 0, HALF)
+        interleave(0, 0, 0, quarter, on_vector)
+        interleave(0, 0, quarter, quarter, on_vector)
+        quantise_h(0, 0, 0, quarter)
+        for first, width in PIECES:
+            cosines(1, first, width, range(SLOTS))
             piece_sines(first, width)
-        products(1, *pieces[0])
-        quantise_h(0, 0, HALF, right)
-        interleave(1, *pieces[0])
-        scores_of(0, 0, HALF, (1,), (0, 1))
-        products(1, *pieces[1])
-        quantise_h(1, *pieces[0])
-        interleave(1, *pieces[1], copy=on_scalar)
-        products(1, *pieces[2])
-        quantise_h(1, *pieces[1])
-        interleave(1, *pieces[2])
-        quantise_h(1, *pieces[2])
-        for (first, width), numbers in zip(pieces, ((2, 4), (3, 5), (6, 7))):
+            h_tiles(1, first, width)
+        products(1, *PIECES[0])
+        quantise_h(0, 0, quarter, quarter)
+        for n, (first, width) in enumerate(PIECES):
+            interleave(1, first, 0, width, on_scalar if n == 1 else on_vector)
+            if n == 0:
+                scores_of(0, 0, HALF, (1,), (0, 1))
+            if n + 1 < len(PIECES):
+                products(1, *PIECES[n + 1])
+            quantise_h(1, first, 0, width)
+        for (first, width), numbers in zip(PIECES, SCORE_BANKS):
             scores_of(1, first, width, (1,) if first + width == HALF else (), numbers)

@@ -22,23 +22,9 @@ N = 256
 HALF = 512
 SLOTS = 4
 GROUP = 16
+TAB2_ROW = 4
+W8_ROW = 8
 PIECES = ((0, 256), (256, 128), (384, 128))
-PIECE_BANKS = (3, 5, 6, 7)
-SCORE_BANKS = ((2, 4), (3, 5), (6, 7))
-
-PLACES = {
-    "wr1_raw": 0,
-    "depot0_0": 0, "depot0_1": 2048, "depot0_2": 4096, "depot0_3": 6144,
-    "v1_1": 0,
-    "wd_codes_0": 4096,
-    "wd_codes_2": 6144,
-    "wd_bf16_2": 13312,
-    "diff1_1": 14336,
-    "wr1_bf16_0": 22528, "wr1_bf16_2": 24576,
-    "depot1_0": 20992, "depot1_1": 25088,
-    "wd_bf16_0": 31744,
-    "diff1_0": 32768,
-}
 
 
 def tile_list_coldchain_spoilage_scores_kernel(
@@ -48,12 +34,9 @@ def tile_list_coldchain_spoilage_scores_kernel(
     nc = tc.nc
     with ExitStack() as ctx:
         keep = ctx.enter_context(tc.tile_pool(name="keep", bufs=1))
-        shared = ctx.enter_context(tc.tile_pool(name="shared", bufs=1))
         psum = ctx.enter_context(tc.psum_pool(name="psum", bufs=1))
 
         def held(name, shape, dtype, after=None):
-            if name in PLACES:
-                return shared.tile(shape, dtype, name=name, offset=PLACES[name], align_bytes=64)
             return keep.tile(shape, dtype, name=name, tag=after or name, align_bytes=64)
 
         def bank(number):
@@ -66,11 +49,11 @@ def tile_list_coldchain_spoilage_scores_kernel(
         w4_rows = held("w4_rows", [P, 2, H], U8)
         w8_rows = held("w8_rows", [P, H], U8)
         planes = held("planes", [P, 2, S], U8)
-        nc.vector.memset(tab_rows[:].bitcast(I32), 0)
-        nc.gpsimd.memset(w8_rows[:].bitcast(I32), 0)
+        nc.gpsimd.memset(tab_rows[:].bitcast(I32), 0)
         nc.vector.memset(tab2_rows[:].bitcast(I32), 0)
-        for rows in (planes, w4_rows):
-            nc.vector.memset(rows[:].rearrange("p a c -> p (a c)").bitcast(I32), 0)
+        nc.vector.memset(w8_rows[:].bitcast(I32), 0)
+        nc.gpsimd.memset(w4_rows[:].rearrange("p a c -> p (a c)").bitcast(I32), 0)
+        nc.vector.memset(planes[:].rearrange("p a c -> p (a c)").bitcast(I32), 0)
         zeros = held("zeros", [P, 8], F32)
         nc.vector.memset(zeros[:], 0.0)
         preload = held("preload", [P, 8], F32)
@@ -86,301 +69,242 @@ def tile_list_coldchain_spoilage_scores_kernel(
             nc.sync.dma_start(tile[:], words.rearrange("p c b -> p (c b)").bitcast(I32))
             return tile
 
-        def load_plane(queue, rows, scales):
-            for d in range(4):
-                queue.dma_start(rows[32 * d : 32 * d + 4, :].bitcast(I32), scales[4 * d : 4 * d + 4, :].bitcast(I32))
+        def load_plane(queue, rows, scales, first):
+            for r in range(4):
+                queue.dma_start(rows[first + r : P : 32, :].bitcast(I32), scales[r:16:4, :].bitcast(I32))
 
-        def by_slot(dst, src, words):
-            nc.vector.tensor_copy(
-                dst.rearrange("p (t q w) -> p t q w", t=SLOTS, w=words),
-                src.rearrange("p (q t w) -> p t q w", t=SLOTS, w=words),
+        def load_w4_rows(queue):
+            for r in range(4):
+                queue.dma_start(
+                    w4_rows[r:P:32, :, :].bitcast(I32), w4_scales[:, r:16:4, :].bitcast(I32).rearrange("a q c -> q a c")
+                )
+
+        def move_planes(queue):
+            for d in range(4):
+                queue.dma_start(
+                    planes[32 * d : 32 * d + 4, :, :].bitcast(I32), tab_picked[32 * d : 32 * d + 32 : 4, :].bitcast(I32)
+                )
+
+        def by_slot(copy, dst, src, words):
+            copy(
+                dst.rearrange("p (a t q w) -> p a t q w", t=SLOTS, q=16, w=words),
+                src.rearrange("p (a q t w) -> p a t q w", t=SLOTS, q=16, w=words),
             )
 
-        def pick_words(name, table, offsets, half):
-            picked = held(name, [P, HALF], U32)
+        def pick(name, dtype, table, offsets, half, after=None):
+            picked = held(name, [P, HALF], dtype, after)
             cols = slice(half * HALF // GROUP, (half + 1) * HALF // GROUP)
-            nc.vector.tensor_copy(picked[:], table[:].bitcast(U32).indirect(offsets[:, cols]))
+            nc.vector.tensor_copy(picked[:], table[:].bitcast(dtype).indirect(offsets[:, cols]))
             return picked
 
-        w8_raw = load_words("w8_raw", w8_words[0])
-        nc.sync.dma_start(lists[:], offs)
-        nc.sync.dma_start(tab_rows[0:P:4, :].bitcast(I32), tab_scales.bitcast(I32).rearrange("a q t -> q a t"))
-        raw = {"wr0": load_rows("wr0_raw", wr[0:512, :])}
-        nc.sync.dma_start(list2[:], offs2)
-        load_plane(nc.sync, tab2_rows, tab2_scales[0])
-        tab2_tile = load_words("tab2_tile", tab2_words[0])
-        raw["wr1"] = load_rows("wr1_raw", wr[512:1024, :])
-        load_plane(nc.gpsimd, w8_rows, w8_scales[0])
-        w8_codes = held("w8_codes", [P, H], I32)
-        by_slot(w8_codes[:], w8_raw[:], 8)
-        tab_picked = held("tab_picked", [P, S], U8)
-        nc.vector.tensor_copy(tab_picked[:], tab_rows[:].indirect(lists[:]))
-        for d in range(4):
-            nc.gpsimd.dma_start(
-                planes[32 * d : 32 * d + 4, :, :].bitcast(I32), tab_picked[32 * d : 32 * d + 32 : 4, :].bitcast(I32)
-            )
-        for d in range(4):
-            nc.gpsimd.dma_start(
-                w4_rows[32 * d : 32 * d + 4, :, :].bitcast(I32),
-                w4_scales[:, 4 * d : 4 * d + 4, :].bitcast(I32).rearrange("a q c -> q a c"),
-            )
-        tab0_tile = load_words("tab0_tile", tab_words[0])
-        tab1_tile = load_words("tab1_tile", tab_words[1])
-        tab2_plane = held("tab2_plane", [P, S], U8)
-        nc.vector.tensor_copy(tab2_plane[:], tab2_rows[:].indirect(list2[:]))
-        w4_raw = held("w4_raw", [P, 2, H // 2], I32)
-        nc.sync.dma_start(w4_raw[:], w4_words.bitcast(I32).rearrange("a p c -> p a c"))
-        raw["wd"] = load_rows("wd_raw", wd)
-        w2_raw = held("w2_raw", [P, SLOTS, N], F32)
-        for t in range(SLOTS):
-            nc.sync.dma_start(w2_raw[:, t, :], w2.rearrange("(q t i) n -> t q i n", t=SLOTS, i=8)[t])
-        gains = held("gains", [P, SLOTS, 8], F32)
-        shifts = held("shifts", [P, N // P], F32)
-        with nc.allow_non_contiguous_dma(reason="one value a partition"):
-            for t in range(SLOTS):
-                nc.sync.dma_start(gains[:, t, 0:1], gain.rearrange("(q t i o) -> t q i o", t=SLOTS, i=8, o=1)[t])
-            nc.sync.dma_start(shifts[:], shift.rearrange("(c p) -> p c", p=P))
-
-        def round_on_scalar(grouped, rows, t):
-            nc.scalar.copy(
-                grouped.rearrange("p (q u i j) -> p q u j i", u=2, i=4, j=4),
-                rows.rearrange("p j (q t u i) -> p t q u j i", t=SLOTS, u=2, i=4)[:, t],
-            )
-
-        def round_on_gpsimd(grouped, rows, t):
-            nc.gpsimd.tensor_scalar(
-                grouped.rearrange("p (q i j) -> p q i j", i=8, j=4),
-                rows.rearrange("p j (q t i) -> p t q i j", t=SLOTS, i=8)[:, t],
-                1.0, 0.0, ALU.mult, ALU.add,
+        def round_slot(copy, grouped, raw, t):
+            copy(
+                grouped.rearrange("p (q u i j) -> p q u j i", u=4, i=2, j=4),
+                raw[:].rearrange("p j (q t u i) -> p t q u j i", t=SLOTS, u=4, i=2)[:, t],
             )
 
         made = {}
 
-        def quantise_weight(name, slots, rounding, codes_name, after=None):
-            width = len(slots) * P
-            grouped = held("%s_bf16_%d" % (name, slots[0]), [P, 4 * width], BF16)
+        def round_weight(name, raw, slots, copy):
+            grouped = held("%s_bf16_%d" % (name, slots[0]), [P, len(slots) * HALF], BF16)
             for n, t in enumerate(slots):
-                rounding(grouped[:, n * 4 * P : (n + 1) * 4 * P], raw[name][:], t)
-            codes = held(codes_name, [P, width], U32, after)
-            scales = held("%s_scales_%d" % (name, slots[0]), [P, width], U8)
+                round_slot(copy, grouped[:, n * HALF : (n + 1) * HALF], raw, t)
+            return grouped
+
+        def quantise_weight(name, grouped, slots, after=None):
+            codes = held("%s_codes_%d" % (name, slots[0]), [P, len(slots) * P], U32, after)
+            scales = held("%s_scales_%d" % (name, slots[0]), [P, len(slots) * P], U8)
             nc.vector.quantize_mx(out=codes[:].bitcast(FP8X4), scales=scales[:], in_=grouped[:])
             for n, t in enumerate(slots):
-                made[name, t] = (codes[:, n * P : (n + 1) * P], scales[:, n * P : (n + 1) * P])
+                made[name, t] = (codes[:, n * P : (n + 1) * P].bitcast(FP8X4), scales[:, n * P : (n + 1) * P])
 
-        quantise_weight("wr0", range(SLOTS), round_on_scalar, "wr0_codes", after="tab2_rows")
-        v2 = [pick_words("v2_%d" % half, tab2_tile, list2, half) for half in range(2)]
-        w8_plane = held("w8_plane", [P, H], U8, after="tab2_tile")
-        by_slot(w8_plane[:].bitcast(I32), w8_rows[:].bitcast(I32), 2)
-        w4_planes = held("w4_planes", [P, 2, H], U8, after="wr0_bf16_0")
-        nc.gpsimd.tensor_copy(
-            w4_planes[:].bitcast(I32).rearrange("p a (t q w) -> p a t q w", t=SLOTS, w=2),
-            w4_rows[:].bitcast(I32).rearrange("p a (q t w) -> p a t q w", t=SLOTS, w=2),
-        )
-        quantise_weight("wr1", (0, 1), round_on_scalar, "wr1_codes_0")
-        v = {(0, half): pick_words("v0_%d" % half, tab0_tile, lists, half) for half in range(2)}
-        quantise_weight("wr1", (2, 3), round_on_scalar, "wr1_codes_2", after="tab0_tile")
-        v[1, 0] = pick_words("v1_0", tab1_tile, lists, 0)
+        w8_raw = load_words("w8_raw", w8_words[0])
+        nc.sync.dma_start(lists[:], offs)
+        nc.sync.dma_start(list2[:], offs2)
+        nc.sync.dma_start(tab_rows[0:P:4, :].bitcast(I32), tab_scales.bitcast(I32).rearrange("a q t -> q a t"))
+        wd_raw = load_rows("wd_raw", wd)
+        load_plane(nc.sync, tab2_rows, tab2_scales[0], TAB2_ROW)
+        load_w4_rows(nc.gpsimd)
+        w8_codes = held("w8_codes", [P, H], I32)
+        by_slot(nc.vector.tensor_copy, w8_codes[:], w8_raw[:], 8)
+        tab_picked = held("tab_picked", [P, S], U8)
+        nc.vector.tensor_copy(tab_picked[:], tab_rows[:].indirect(lists[:]))
+        tab2_tile = load_words("tab2_tile", tab2_words[0])
+        load_plane(nc.sync, w8_rows, w8_scales[0], W8_ROW)
+        tab0_tile = load_words("tab0_tile", tab_words[0])
+        move_planes(nc.gpsimd)
+        w4_raw = held("w4_raw", [P, 2, H // 2], I32)
+        nc.sync.dma_start(w4_raw[:], w4_words.bitcast(I32).rearrange("a p c -> p a c"))
+        tab1_tile = load_words("tab1_tile", tab_words[1])
+        wr0_raw = load_rows("wr0_raw", wr[0:512, :])
+        wr1_raw = load_rows("wr1_raw", wr[512:1024, :])
+        gains = held("gains", [P, SLOTS, 8], F32)
+        shifts = held("shifts", [P, N // P], F32)
+        w2_raw = held("w2_raw", [P, SLOTS, N], F32)
+        with nc.allow_non_contiguous_dma(reason="one value a partition"):
+            for t in range(SLOTS):
+                nc.sync.dma_start(gains[:, t, 0:1], gain.rearrange("(q t i o) -> t q i o", t=SLOTS, i=8, o=1)[t])
+            for t in range(SLOTS):
+                nc.sync.dma_start(w2_raw[:, t, :], w2.rearrange("(q t i) n -> t q i n", t=SLOTS, i=8)[t])
+            nc.sync.dma_start(shifts[:], shift.rearrange("(c p) -> p c", p=P))
+
+        tab2_plane = held("tab2_plane", [P, S], U8)
+        nc.vector.tensor_copy(tab2_plane[:], tab2_rows[:].indirect(list2[:]))
+        wd_grouped = round_weight("wd", wd_raw, range(SLOTS), nc.scalar.copy)
+        w8_plane = held("w8_plane", [P, H], U8)
+        by_slot(nc.gpsimd.tensor_copy, w8_plane[:].bitcast(I32), w8_rows[:].bitcast(I32), 2)
+        v2 = [pick("v2_0", U32, tab2_tile, list2, 0)]
+        v2.append(pick("v2_1", U32, tab2_tile, list2, 1))
+        quantise_weight("wd", wd_grouped, range(SLOTS), after="tab2_tile")
+
+        def span(half):
+            return slice(half * HALF, (half + 1) * HALF)
+
+        for n in range(4):
+            nc.tensor.matmul_mx(
+                out=bank(SLOTS + n % SLOTS)[:], lhsT=w8_codes[:, 0:P].bitcast(FP8X4), lhsT_scale=tab_picked[:, 0:P],
+                rhs=w8_codes[:].bitcast(FP8X4), rhs_scale=tab_picked[:, 0:HALF], start=True, stop=True,
+            )
 
         depot = {}
-
-        def depot_products(half, tiles):
+        for half in range(2):
             for t in range(SLOTS):
                 cols = slice(t * P, (t + 1) * P)
                 product = bank(SLOTS * half + t)
                 nc.tensor.matmul_mx(
-                    out=product[:], lhsT=w8_codes[:, cols].bitcast(FP8X4), lhsT_scale=w8_plane[:, cols],
-                    rhs=v2[half][:].bitcast(FP8X4), rhs_scale=tab2_plane[:, half * HALF : (half + 1) * HALF],
-                    start=True, stop=True,
+                    out=product[:], lhsT=w8_codes[:, cols].bitcast(FP8X4), lhsT_scale=w8_plane[W8_ROW:P, cols],
+                    rhs=v2[half][:].bitcast(FP8X4), rhs_scale=tab2_plane[TAB2_ROW:P, span(half)], start=True, stop=True,
                 )
-                depot[half, t] = tiles[t]
-                nc.scalar.copy(tiles[t], product[:])
+                depot[half, t] = held("depot%d_%d" % (half, t), [P, HALF], F32)
+                nc.scalar.copy(depot[half, t][:], product[:])
 
-        depot_products(0, [held("depot0_%d" % t, [P, HALF], F32)[:] for t in range(SLOTS)])
-        pairs = [held("depot1_%d" % n, [P, 2, HALF], F32) for n in range(2)]
-        depot_products(1, [pairs[t // 2][:, t % 2, :] for t in range(SLOTS)])
-        w4_codes = held("w4_codes", [P, 2, H // 2], I32)
-        nc.vector.tensor_copy(
-            w4_codes[:].rearrange("p a (t q w) -> p a t q w", t=SLOTS, w=4),
-            w4_raw[:].rearrange("p a (q t w) -> p a t q w", t=SLOTS, w=4),
+        w4_planes = held("w4_planes", [P, 2 * H], U8, after="w8_rows")
+        by_slot(
+            nc.gpsimd.tensor_copy, w4_planes[:].bitcast(I32), w4_rows[:].rearrange("p a c -> p (a c)").bitcast(I32), 2
         )
+        w4_codes = held("w4_codes", [P, H], I32)
+        by_slot(nc.gpsimd.tensor_copy, w4_codes[:], w4_raw[:].rearrange("p a c -> p (a c)"), 4)
+        v = {(a, half): pick("v%d_%d" % (a, half), U32, (tab0_tile, tab1_tile)[a], lists, half)
+             for a in range(2) for half in range(2)}
 
-        totals, diffs, cos_of, sin_of, rows_of, grouped_of, h_of = {}, {}, {}, {}, {}, {}, {}
-
-        def route_pass(route, half, t, a):
-            codes, scales = made["wr%d" % a, t]
+        def w4_pass(total, half, t, a, start, stop):
+            at = a * H + t * P
             nc.tensor.matmul_mx(
-                out=route[:], lhsT=codes.bitcast(FP8X4), lhsT_scale=scales, rhs=v[a, half][:].bitcast(FP8X4),
-                rhs_scale=planes[:, a, half * HALF : (half + 1) * HALF], start=(a == 0), stop=(a == 1),
+                out=total[:], lhsT=w4_codes[:, at // 2 : (at + P) // 2].bitcast(FP4X4),
+                lhsT_scale=w4_planes[:, at : at + P], rhs=v[a, half][:].bitcast(FP8X4),
+                rhs_scale=planes[:, a, span(half)], start=start, stop=stop,
             )
 
-        def subtract(route, half, t):
-            nc.vector.tensor_tensor(diffs[half, t // 2][:, t % 2, :], route[:], depot[half, t], ALU.subtract)
-
-        def second_difference(t, number):
-            route = bank(number)
-            for a in range(2):
-                route_pass(route, 1, t, a)
-            subtract(route, 1, t)
-
-        def open_total(total, t, half, first, width):
-            at = half * HALF + first
-            for a in range(2):
-                nc.tensor.matmul_mx(
-                    out=total, lhsT=w4_codes[:, a, t * P // 2 : (t + 1) * P // 2].bitcast(FP4X4),
-                    lhsT_scale=w4_planes[:, a, t * P : (t + 1) * P],
-                    rhs=v[a, half][:, first : first + width].bitcast(FP8X4), rhs_scale=planes[:, a, at : at + width],
-                    start=(a == 0), stop=False,
-                )
-
-        def close_total(total, t, half, first, width):
-            at = half * HALF + first
+        def wd_pass(total, half, t, start, stop):
             codes, scales = made["wd", t]
             nc.tensor.matmul_mx(
-                out=total, lhsT=codes.bitcast(FP8X4), lhsT_scale=scales,
-                rhs=v2[half][:, first : first + width].bitcast(FP8X4), rhs_scale=tab2_plane[:, at : at + width],
-                start=False, stop=True,
+                out=total[:], lhsT=codes, lhsT_scale=scales, rhs=v2[half][:].bitcast(FP8X4),
+                rhs_scale=tab2_plane[TAB2_ROW:P, span(half)], start=start, stop=stop,
             )
 
-        def cosines(half, first, width, slots):
-            size = keep.tile([P, len(slots), width], F32, name="size", bufs=2)
-            for n in range(0, len(slots), 2):
-                low, count = slots[n] % 2, min(2, len(slots))
-                nc.scalar.activation(
-                    size[:, n : n + count, :], diffs[half, slots[n] // 2][:, low : low + count, first : first + width],
-                    ACT.Abs,
-                )
-            cosine = held("cosine%d_%d_%d" % (half, first, slots[0]), [P, len(slots), width], F32)
-            nc.scalar.activation(cosine[:], size[:], ACT.Sin, bias=math.pi / 2, scale=-1.0)
-            for n, t in enumerate(slots):
-                cos_of[half, first, t] = cosine[:, n, :]
+        pairs = ((0, 1), (2, 3))
+        totals = {}
+        early = [(0, t) for t in range(SLOTS)] + [(1, 0), (1, 1)]
+        for half, t in early:
+            totals[half, t] = bank(SLOTS * half + t)
+            wd_pass(totals[half, t], half, t, True, False)
+            w4_pass(totals[half, t], half, t, 0, False, False)
+        sines = held("sines", [P, SLOTS, S], F32)
+        for half, t in early:
+            w4_pass(totals[half, t], half, t, 1, False, True)
+            nc.scalar.activation(sines[:, t, span(half)], totals[half, t][:], ACT.Sin)
+        for t in (2, 3):
+            total = bank(SLOTS + t)
+            w4_pass(total, 1, t, 1, True, False)
+            w4_pass(total, 1, t, 0, False, False)
+            wd_pass(total, 1, t, False, True)
+            nc.scalar.activation(sines[:, t, span(1)], total[:], ACT.Sin)
 
-        def piece_sines(first, width):
-            sine = held("sine1_%d" % first, [P, SLOTS, width], F32)
-            for at in range(first, first + width, P):
-                nc.scalar.activation(
-                    sine[:, :, at - first : at - first + P], totals[1, at][:].rearrange("p (t c) -> p t c", t=SLOTS),
-                    ACT.Sin,
-                )
+        for name, raw in (("wr0", wr0_raw), ("wr1", wr1_raw)):
+            grouped = [round_weight(name, raw, slots, nc.vector.tensor_copy) for slots in pairs]
+            for n, slots in enumerate(pairs):
+                quantise_weight(name, grouped[n], slots)
+
+        def route_pass(route, half, t, a, start):
+            codes, scales = made["wr%d" % a, t]
+            nc.tensor.matmul_mx(
+                out=route[:], lhsT=codes, lhsT_scale=scales, rhs=v[a, half][:].bitcast(FP8X4),
+                rhs_scale=planes[:, a, span(half)], start=start, stop=not start,
+            )
+
+        diffs = [held("diff%d" % half, [P, SLOTS, HALF], F32) for half in range(2)]
+        for half in range(2):
             for t in range(SLOTS):
-                sin_of[1, first, t] = sine[:, t, :]
+                route = bank(SLOTS * half + t)
+                route_pass(route, half, t, 1, True)
+                route_pass(route, half, t, 0, False)
+                nc.vector.tensor_tensor(diffs[half][:, t, :], route[:], depot[half, t][:], ALU.subtract)
 
-        def products(half, first, width):
-            h_rows = rows_of[half, first] = held("h_rows%d_%d" % (half, first), [P, SLOTS, width], BF16)
-            for t in range(SLOTS):
-                nc.vector.scalar_tensor_tensor(
-                    h_rows[:, t, :], cos_of[half, first, t], gains[:, t, 0:1], sin_of[half, first, t],
-                    ALU.mult, ALU.mult,
-                )
+        scaled = held("scaled", [P, SLOTS, S], F32, after="wr1_bf16_2")
+        for t in range(SLOTS):
+            nc.gpsimd.tensor_scalar(scaled[:, t, :], sines[:, t, :], gains[:, t, 0:1], 0.0, ALU.mult, ALU.add)
 
-        def interleave(half, first, start, width, copy):
-            h_grouped = grouped_of[half, first + start] = held(
-                "h_grouped%d_%d" % (half, first + start), [P, SLOTS * width], BF16
-            )
-            copy(
-                h_grouped[:].rearrange("p (c t) -> p c t", t=SLOTS),
-                rows_of[half, first][:, :, start : start + width].rearrange("p t c -> p c t"),
-            )
+        def cosines(cosine, diff):
+            size = keep.tile(list(diff.shape), F32, name="size", bufs=2)
+            nc.scalar.activation(size[:], diff, ACT.Abs)
+            nc.scalar.activation(cosine, size[:], ACT.Sin, bias=math.pi / 2, scale=-1.0)
 
-        def h_tiles(half, first, width):
-            h_of[half, first] = (
-                held("h_codes%d_%d" % (half, first), [P, width], U32),
-                held("h_scales%d_%d" % (half, first), [P, width], U8),
-            )
+        cos_of = {0: held("cosine0", [P, SLOTS, HALF], F32)}
+        for low, high in ((0, 1), (1, 2), (2, 4)):
+            cosines(cos_of[0][:, low:high, :], diffs[0][:, low:high, :])
+        for first, width in PIECES:
+            cos_of[HALF + first] = held("cosine1_%d" % first, [P, SLOTS, width], F32)
+            cosines(cos_of[HALF + first][:], diffs[1][:, :, first : first + width])
 
-        def quantise_h(half, first, start, width):
-            h_codes, h_scales = h_of[half, first]
-            cols = slice(start, start + width)
-            nc.vector.quantize_mx(
-                out=h_codes[:, cols].bitcast(FP8X4), scales=h_scales[:, cols], in_=grouped_of[half, first + start][:]
+        w2_grouped = held("w2_bf16", [P, SLOTS * N], BF16, after="depot1_2")
+        nc.vector.tensor_copy(
+            w2_grouped[:].rearrange("p (n i t) -> p n t i", t=SLOTS, i=2),
+            w2_raw[:].rearrange("p t (n i) -> p n t i", i=2),
+        )
+
+        def products(at, width):
+            h_grouped = held("h_bf16_%d" % at, [P, SLOTS * width], BF16)
+            nc.vector.tensor_tensor(
+                h_grouped[:].rearrange("p (c i t) -> p c t i", t=SLOTS, i=2),
+                cos_of[at][:].rearrange("p t (c i) -> p c t i", i=2),
+                scaled[:, :, at : at + width].rearrange("p t (c i) -> p c t i", i=2),
+                ALU.mult,
             )
+            return h_grouped
+
+        def quantise_h(at, width, h_grouped):
+            h_codes = held("h_codes_%d" % at, [P, width], U32)
+            h_scales = held("h_scales_%d" % at, [P, width], U8)
+            nc.vector.quantize_mx(out=h_codes[:].bitcast(FP8X4), scales=h_scales[:], in_=h_grouped[:])
+            return h_codes, h_scales
 
         out_view = out.rearrange("(c p) j -> p c j", p=P)
 
-        def scores_of(half, first, width, on_vector_rows, numbers):
-            h_codes, h_scales = h_of[half, first]
-            at = half * HALF + first
-            result = held("result%d_%d" % (half, first), [P, N // P, width], F32)
+        def scores_of(at, width, h, numbers, on_vector_rows):
+            result = held("result_%d" % at, [P, N // P, width], F32)
             for c in range(N // P):
                 rows = slice(c * P, (c + 1) * P)
                 scores = bank(numbers[c])
                 nc.tensor.matmul_mx(
                     out=scores[:, 0:width], lhsT=w2_codes[:, rows].bitcast(FP8X4), lhsT_scale=w2_scales[:, rows],
-                    rhs=h_codes[:].bitcast(FP8X4), rhs_scale=h_scales[:], start=True, stop=True,
+                    rhs=h[0][:].bitcast(FP8X4), rhs_scale=h[1][:], start=True, stop=True,
                 )
                 if c in on_vector_rows:
                     nc.vector.tensor_scalar_add(result[:, c, :], scores[:, 0:width], shifts[:, c : c + 1])
                 else:
                     nc.scalar.activation(result[:, c, :], scores[:, 0:width], ACT.Identity, bias=shifts[:, c : c + 1])
-                if half == 0:
-                    nc.sync.dma_start(out_view[:, c, at : at + width], result[:, c, :])
-            if half == 1:
-                nc.sync.dma_start(out_view[:, :, at : at + width], result[:])
+            nc.sync.dma_start(out_view[:, :, at : at + width], result[:])
 
-        for pair in range(2):
-            diffs[0, pair] = held("diff0_%d" % pair, [P, 2, HALF], F32)
-        routes = [bank(t) for t in range(SLOTS)]
-        for a in range(2):
-            for t in range(SLOTS):
-                route_pass(routes[t], 0, t, a)
-        for t in range(SLOTS):
-            subtract(routes[t], 0, t)
-            if t == 1:
-                v[1, 1] = pick_words("v1_1", tab1_tile, lists, 1)
-        for t in range(SLOTS):
-            cosines(0, 0, HALF, (t,))
-            totals[0, t] = bank(SLOTS + t)
-            open_total(totals[0, t][:], t, 0, 0, HALF)
-        for pair in range(2):
-            slots = (2 * pair, 2 * pair + 1)
-            quantise_weight("wd", slots, round_on_gpsimd, "wd_codes_%d" % slots[0])
-            for t in slots:
-                close_total(totals[0, t][:], t, 0, 0, HALF)
-            if pair == 0:
-                diffs[1, 0] = held("diff1_0", [P, 2, HALF], F32)
-                second_difference(0, 0)
-                second_difference(1, 1)
-        w2_grouped = held("w2_bf16", [P, SLOTS * N], BF16)
-        for c in range(N // P):
-            nc.gpsimd.tensor_scalar(
-                w2_grouped[:, SLOTS * P * c : SLOTS * P * (c + 1)].rearrange("p (n t) -> p n t", t=SLOTS),
-                w2_raw[:, :, P * c : P * (c + 1)].rearrange("p t n -> p n t"),
-                1.0, 0.0, ALU.mult, ALU.add,
-            )
-        diffs[1, 1] = held("diff1_1", [P, 2, HALF], F32)
-        second_difference(2, 2)
-        for t in range(SLOTS):
-            sine = held("sine0_%d" % t, [P, HALF], F32)
-            nc.scalar.activation(sine[:], totals[0, t][:], ACT.Sin)
-            sin_of[0, 0, t] = sine[:]
-        second_difference(3, SLOTS)
-        for n, number in enumerate(PIECE_BANKS):
-            total = totals[1, n * P] = bank(number)
-            for t in range(SLOTS):
-                open_total(total[:, t * P : (t + 1) * P], t, 1, n * P, P)
-                close_total(total[:, t * P : (t + 1) * P], t, 1, n * P, P)
-
-        on_scalar, on_vector = nc.scalar.copy, nc.vector.tensor_copy
-        products(0, 0, HALF)
-        w2_codes = held("w2_codes", [P, N], U32, after="cosine0_0_2")
+        steps = [(0, HALF)] + [(HALF + first, width) for first, width in PIECES]
+        h_grouped = products(*steps[0])
+        w2_codes = held("w2_codes", [P, N], U32)
         w2_scales = held("w2_scales", [P, N], U8)
         nc.vector.quantize_mx(out=w2_codes[:].bitcast(FP8X4), scales=w2_scales[:], in_=w2_grouped[:])
-        quarter = HALF // 2
-        h_tiles(0, 0, HALF)
-        interleave(0, 0, 0, quarter, on_vector)
-        interleave(0, 0, quarter, quarter, on_vector)
-        quantise_h(0, 0, 0, quarter)
-        for first, width in PIECES:
-            cosines(1, first, width, range(SLOTS))
-            piece_sines(first, width)
-            h_tiles(1, first, width)
-        products(1, *PIECES[0])
-        quantise_h(0, 0, quarter, quarter)
-        for n, (first, width) in enumerate(PIECES):
-            interleave(1, first, 0, width, on_scalar if n == 1 else on_vector)
-            if n == 0:
-                scores_of(0, 0, HALF, (1,), (0, 1))
-            if n + 1 < len(PIECES):
-                products(1, *PIECES[n + 1])
-            quantise_h(1, first, 0, width)
-        for (first, width), numbers in zip(PIECES, SCORE_BANKS):
-            scores_of(1, first, width, (1,) if first + width == HALF else (), numbers)
+        h_of = [quantise_h(0, HALF, h_grouped)]
+        h_grouped = products(*steps[1])
+        for n in range(1, len(steps)):
+            later = products(*steps[n + 1]) if n + 1 < len(steps) else None
+            h_of.append(quantise_h(steps[n][0], steps[n][1], h_grouped))
+            h_grouped = later
+        for n, (at, width) in enumerate(steps):
+            scores_of(at, width, h_of[n], (2 * n, 2 * n + 1), (1,) if n + 1 == len(steps) else ())

@@ -160,12 +160,6 @@ def tile_list_coldchain_spoilage_scores_kernel(
         def span(half):
             return slice(half * HALF, (half + 1) * HALF)
 
-        for n in range(4):
-            nc.tensor.matmul_mx(
-                out=bank(SLOTS + n % SLOTS)[:], lhsT=w8_codes[:, 0:P].bitcast(FP8X4), lhsT_scale=tab_picked[:, 0:P],
-                rhs=w8_codes[:].bitcast(FP8X4), rhs_scale=tab_picked[:, 0:HALF], start=True, stop=True,
-            )
-
         depot = {}
         for half in range(2):
             for t in range(SLOTS):

@@ -20,11 +20,15 @@ S = 1024
 H = 512
 N = 256
 HALF = 512
+QUARTER = 256
 SLOTS = 4
 GROUP = 16
 TAB2_ROW = 4
 W8_ROW = 8
-PIECES = ((0, 256), (256, 128), (384, 128))
+EARLY_TOTALS = 4
+EARLY_ROUTES = 2
+PIECES = ((0, 512), (512, 256), (768, 128), (896, 128))
+FLOPS = 2 * S * (2 * (1024 + 512) * H + H * N)
 
 
 def tile_list_coldchain_spoilage_scores_kernel(
@@ -42,6 +46,9 @@ def tile_list_coldchain_spoilage_scores_kernel(
         def bank(number):
             return psum.tile([P, HALF], F32, name="bank%d" % number)
 
+        def span(half):
+            return slice(half * HALF, (half + 1) * HALF)
+
         lists = held("lists", [P, S // GROUP], U16)
         list2 = held("list2", [P, S // GROUP], U16)
         tab_rows = held("tab_rows", [P, T], U8)
@@ -49,7 +56,8 @@ def tile_list_coldchain_spoilage_scores_kernel(
         w4_rows = held("w4_rows", [P, 2, H], U8)
         w8_rows = held("w8_rows", [P, H], U8)
         planes = held("planes", [P, 2, S], U8)
-        nc.gpsimd.memset(tab_rows[:].bitcast(I32), 0)
+        nc.gpsimd.memset(tab_rows[:, 0 : T // 2].bitcast(I32), 0)
+        nc.vector.memset(tab_rows[:, T // 2 : T].bitcast(I32), 0)
         nc.vector.memset(tab2_rows[:].bitcast(I32), 0)
         nc.vector.memset(w8_rows[:].bitcast(I32), 0)
         nc.gpsimd.memset(w4_rows[:].rearrange("p a c -> p (a c)").bitcast(I32), 0)
@@ -73,42 +81,27 @@ def tile_list_coldchain_spoilage_scores_kernel(
             for r in range(4):
                 queue.dma_start(rows[first + r : P : 32, :].bitcast(I32), scales[r:16:4, :].bitcast(I32))
 
-        def load_w4_rows(queue):
-            for r in range(4):
-                queue.dma_start(
-                    w4_rows[r:P:32, :, :].bitcast(I32), w4_scales[:, r:16:4, :].bitcast(I32).rearrange("a q c -> q a c")
-                )
-
-        def move_planes(queue):
-            for d in range(4):
-                queue.dma_start(
-                    planes[32 * d : 32 * d + 4, :, :].bitcast(I32), tab_picked[32 * d : 32 * d + 32 : 4, :].bitcast(I32)
-                )
-
-        def by_slot(copy, dst, src, words):
-            copy(
-                dst.rearrange("p (a t q w) -> p a t q w", t=SLOTS, q=16, w=words),
-                src.rearrange("p (a q t w) -> p a t q w", t=SLOTS, q=16, w=words),
+        def by_slot(dst, src, words):
+            nc.scalar.copy(
+                dst.bitcast(U32).rearrange("p (a t q w) -> p a t q w", t=SLOTS, q=16, w=words),
+                src.bitcast(U32).rearrange("p (a q t w) -> p a t q w", t=SLOTS, q=16, w=words),
             )
 
-        def pick(name, dtype, table, offsets, half, after=None):
-            picked = held(name, [P, HALF], dtype, after)
+        def pick(name, dtype, table, offsets, half):
+            picked = held(name, [P, HALF], dtype)
             cols = slice(half * HALF // GROUP, (half + 1) * HALF // GROUP)
             nc.vector.tensor_copy(picked[:], table[:].bitcast(dtype).indirect(offsets[:, cols]))
             return picked
 
-        def round_slot(copy, grouped, raw, t):
-            copy(
-                grouped.rearrange("p (q u i j) -> p q u j i", u=4, i=2, j=4),
-                raw[:].rearrange("p j (q t u i) -> p t q u j i", t=SLOTS, u=4, i=2)[:, t],
-            )
-
         made = {}
 
-        def round_weight(name, raw, slots, copy):
-            grouped = held("%s_bf16_%d" % (name, slots[0]), [P, len(slots) * HALF], BF16)
+        def round_weight(name, raw, slots, copy, after=None):
+            grouped = held("%s_bf16_%d" % (name, slots[0]), [P, len(slots) * HALF], BF16, after)
             for n, t in enumerate(slots):
-                round_slot(copy, grouped[:, n * HALF : (n + 1) * HALF], raw, t)
+                copy(
+                    grouped[:, n * HALF : (n + 1) * HALF].rearrange("p (q u i j) -> p q u j i", u=4, i=2, j=4),
+                    raw[:].rearrange("p j (q t u i) -> p t q u j i", t=SLOTS, u=4, i=2)[:, t],
+                )
             return grouped
 
         def quantise_weight(name, grouped, slots, after=None):
@@ -118,66 +111,89 @@ def tile_list_coldchain_spoilage_scores_kernel(
             for n, t in enumerate(slots):
                 made[name, t] = (codes[:, n * P : (n + 1) * P].bitcast(FP8X4), scales[:, n * P : (n + 1) * P])
 
-        w8_raw = load_words("w8_raw", w8_words[0])
         nc.sync.dma_start(lists[:], offs)
         nc.sync.dma_start(list2[:], offs2)
         nc.sync.dma_start(tab_rows[0:P:4, :].bitcast(I32), tab_scales.bitcast(I32).rearrange("a q t -> q a t"))
         wd_raw = load_rows("wd_raw", wd)
         load_plane(nc.sync, tab2_rows, tab2_scales[0], TAB2_ROW)
-        load_w4_rows(nc.gpsimd)
-        w8_codes = held("w8_codes", [P, H], I32)
-        by_slot(nc.vector.tensor_copy, w8_codes[:], w8_raw[:], 8)
-        tab_picked = held("tab_picked", [P, S], U8)
-        nc.vector.tensor_copy(tab_picked[:], tab_rows[:].indirect(lists[:]))
+        w8_raw = load_words("w8_raw", w8_words[0])
         tab2_tile = load_words("tab2_tile", tab2_words[0])
         load_plane(nc.sync, w8_rows, w8_scales[0], W8_ROW)
-        tab0_tile = load_words("tab0_tile", tab_words[0])
-        move_planes(nc.gpsimd)
+        for r in range(4):
+            nc.gpsimd.dma_start(
+                w4_rows[r:P:32, :, :].bitcast(I32), w4_scales[:, r:16:4, :].bitcast(I32).rearrange("a q c -> q a c")
+            )
         w4_raw = held("w4_raw", [P, 2, H // 2], I32)
         nc.sync.dma_start(w4_raw[:], w4_words.bitcast(I32).rearrange("a p c -> p a c"))
+        tab0_tile = load_words("tab0_tile", tab_words[0])
+        tab_picked = held("tab_picked", [P, S], U8)
+        nc.vector.tensor_copy(tab_picked[:], tab_rows[:].indirect(lists[:]))
+        for d in range(4):
+            nc.sync.dma_start(
+                planes[32 * d : 32 * d + 4, :, :].bitcast(I32), tab_picked[32 * d : 32 * d + 32 : 4, :].bitcast(I32)
+            )
         tab1_tile = load_words("tab1_tile", tab_words[1])
         wr0_raw = load_rows("wr0_raw", wr[0:512, :])
         wr1_raw = load_rows("wr1_raw", wr[512:1024, :])
         gains = held("gains", [P, SLOTS, 8], F32)
         shifts = held("shifts", [P, N // P], F32)
         w2_raw = held("w2_raw", [P, SLOTS, N], F32)
-        with nc.allow_non_contiguous_dma(reason="one value a partition"):
-            for t in range(SLOTS):
-                nc.sync.dma_start(gains[:, t, 0:1], gain.rearrange("(q t i o) -> t q i o", t=SLOTS, i=8, o=1)[t])
+        with nc.allow_non_contiguous_dma(reason="one value a partition and slot"):
             for t in range(SLOTS):
                 nc.sync.dma_start(w2_raw[:, t, :], w2.rearrange("(q t i) n -> t q i n", t=SLOTS, i=8)[t])
+            for t in range(SLOTS):
+                nc.sync.dma_start(gains[:, t, 0:1], gain.rearrange("(q t i o) -> t q i o", t=SLOTS, i=8, o=1)[t])
             nc.sync.dma_start(shifts[:], shift.rearrange("(c p) -> p c", p=P))
 
         tab2_plane = held("tab2_plane", [P, S], U8)
         nc.vector.tensor_copy(tab2_plane[:], tab2_rows[:].indirect(list2[:]))
-        wd_grouped = round_weight("wd", wd_raw, range(SLOTS), nc.scalar.copy)
+        pairs = ((0, 1), (2, 3))
+        wd_grouped = [round_weight("wd", wd_raw, slots, nc.scalar.copy) for slots in pairs]
+        quantise_weight("wd", wd_grouped[0], pairs[0], after="tab2_rows")
+        quantise_weight("wd", wd_grouped[1], pairs[1], after="wd_bf16_0")
+        v2 = [held("v2_%d" % half, [P, HALF], U32) for half in range(2)]
+        for first, width in ((0, QUARTER), (QUARTER, QUARTER), (HALF, HALF)):
+            nc.vector.tensor_copy(
+                v2[first // HALF][:, first % HALF : first % HALF + width],
+                tab2_tile[:].bitcast(U32).indirect(list2[:, first // GROUP : (first + width) // GROUP]),
+            )
+        w8_codes = held("w8_codes", [P, H], I32)
+        by_slot(w8_codes[:], w8_raw[:], 8)
         w8_plane = held("w8_plane", [P, H], U8)
-        by_slot(nc.gpsimd.tensor_copy, w8_plane[:].bitcast(I32), w8_rows[:].bitcast(I32), 2)
-        v2 = [pick("v2_0", U32, tab2_tile, list2, 0)]
-        v2.append(pick("v2_1", U32, tab2_tile, list2, 1))
-        quantise_weight("wd", wd_grouped, range(SLOTS), after="tab2_tile")
-
-        def span(half):
-            return slice(half * HALF, (half + 1) * HALF)
-
-        depot = {}
-        for half in range(2):
-            for t in range(SLOTS):
-                cols = slice(t * P, (t + 1) * P)
-                product = bank(SLOTS * half + t)
-                nc.tensor.matmul_mx(
-                    out=product[:], lhsT=w8_codes[:, cols].bitcast(FP8X4), lhsT_scale=w8_plane[W8_ROW:P, cols],
-                    rhs=v2[half][:].bitcast(FP8X4), rhs_scale=tab2_plane[TAB2_ROW:P, span(half)], start=True, stop=True,
-                )
-                depot[half, t] = held("depot%d_%d" % (half, t), [P, HALF], F32)
-                nc.scalar.copy(depot[half, t][:], product[:])
-
-        w4_planes = held("w4_planes", [P, 2 * H], U8, after="w8_rows")
-        by_slot(
-            nc.gpsimd.tensor_copy, w4_planes[:].bitcast(I32), w4_rows[:].rearrange("p a c -> p (a c)").bitcast(I32), 2
-        )
+        by_slot(w8_plane[:], w8_rows[:], 2)
         w4_codes = held("w4_codes", [P, H], I32)
-        by_slot(nc.gpsimd.tensor_copy, w4_codes[:], w4_raw[:].rearrange("p a c -> p (a c)"), 4)
+        by_slot(w4_codes[:], w4_raw[:].rearrange("p a c -> p (a c)"), 4)
+
+        units = [(half, t) for half in range(2) for t in range(SLOTS)]
+        depot_sums = [bank(n) for n in range(len(units))]
+        depot = [held("depot%d" % half, [P, SLOTS, HALF], F32) for half in range(2)]
+
+        def depot_pass(target, t, first, width):
+            cols = slice(t * P, (t + 1) * P)
+            nc.tensor.matmul_mx(
+                out=target, lhsT=w8_codes[:, cols].bitcast(FP8X4), lhsT_scale=w8_plane[W8_ROW:P, cols],
+                rhs=v2[first // HALF][:, first % HALF : first % HALF + width].bitcast(FP8X4),
+                rhs_scale=tab2_plane[TAB2_ROW:P, first : first + width], start=True, stop=True,
+            )
+
+        places = []
+        for quarter in range(2):
+            for n, slots in enumerate(pairs):
+                for m, t in enumerate(slots):
+                    depot_pass(depot_sums[2 * quarter + n][:, m * QUARTER : (m + 1) * QUARTER], t, quarter * QUARTER, QUARTER)
+                places.append(depot[0][:, slots[0] : slots[0] + 2, quarter * QUARTER : (quarter + 1) * QUARTER])
+        for t in range(SLOTS):
+            depot_pass(depot_sums[SLOTS + t][:], t, HALF, HALF)
+            places.append(depot[1][:, t : t + 1, :])
+
+        def copy_depots(first, last):
+            for n in range(first, last):
+                nc.scalar.copy(places[n], depot_sums[n][:].rearrange("p (m c) -> p m c", m=places[n].shape[1]))
+
+        copy_depots(0, 6)
+        w4_planes = held("w4_planes", [P, 2 * H], U8, after="w8_codes")
+        by_slot(w4_planes[:], w4_rows[:].rearrange("p a c -> p (a c)"), 2)
+        copy_depots(6, len(units))
         v = {(a, half): pick("v%d_%d" % (a, half), U32, (tab0_tile, tab1_tile)[a], lists, half)
              for a in range(2) for half in range(2)}
 
@@ -196,28 +212,34 @@ def tile_list_coldchain_spoilage_scores_kernel(
                 rhs_scale=tab2_plane[TAB2_ROW:P, span(half)], start=start, stop=stop,
             )
 
-        pairs = ((0, 1), (2, 3))
-        totals = {}
-        early = [(0, t) for t in range(SLOTS)] + [(1, 0), (1, 1)]
-        for half, t in early:
-            totals[half, t] = bank(SLOTS * half + t)
+        totals = {unit: bank(n) for n, unit in enumerate(units[:EARLY_TOTALS])}
+        for half, t in units[:EARLY_TOTALS]:
             wd_pass(totals[half, t], half, t, True, False)
+        for half, t in units[:EARLY_TOTALS]:
             w4_pass(totals[half, t], half, t, 0, False, False)
         sines = held("sines", [P, SLOTS, S], F32)
-        for half, t in early:
+        for half, t in units[:EARLY_TOTALS]:
             w4_pass(totals[half, t], half, t, 1, False, True)
             nc.scalar.activation(sines[:, t, span(half)], totals[half, t][:], ACT.Sin)
-        for t in (2, 3):
-            total = bank(SLOTS + t)
-            w4_pass(total, 1, t, 1, True, False)
-            w4_pass(total, 1, t, 0, False, False)
-            wd_pass(total, 1, t, False, True)
-            nc.scalar.activation(sines[:, t, span(1)], total[:], ACT.Sin)
+        for half, t in units[EARLY_TOTALS:]:
+            total = bank(SLOTS * half + t)
+            w4_pass(total, half, t, 1, True, False)
+            w4_pass(total, half, t, 0, False, False)
+            wd_pass(total, half, t, False, True)
+            nc.scalar.activation(sines[:, t, span(half)], total[:], ACT.Sin)
 
-        for name, raw in (("wr0", wr0_raw), ("wr1", wr1_raw)):
-            grouped = [round_weight(name, raw, slots, nc.vector.tensor_copy) for slots in pairs]
-            for n, slots in enumerate(pairs):
-                quantise_weight(name, grouped[n], slots)
+        w2_grouped = held("w2_bf16", [P, SLOTS * N], BF16, after="wd_bf16_0")
+        nc.scalar.copy(
+            w2_grouped[:].rearrange("p (n i t) -> p n t i", t=SLOTS, i=2),
+            w2_raw[:].rearrange("p t (n i) -> p n t i", i=2),
+        )
+
+        grouped = [round_weight("wr0", wr0_raw, slots, nc.vector.tensor_copy) for slots in pairs]
+        for n, slots in enumerate(pairs):
+            quantise_weight("wr0", grouped[n], slots)
+        grouped = [round_weight("wr1", wr1_raw, slots, nc.vector.tensor_copy) for slots in pairs]
+        quantise_weight("wr1", grouped[0], pairs[0])
+        quantise_weight("wr1", grouped[1], pairs[1])
 
         def route_pass(route, half, t, a, start):
             codes, scales = made["wr%d" % a, t]
@@ -227,44 +249,54 @@ def tile_list_coldchain_spoilage_scores_kernel(
             )
 
         diffs = [held("diff%d" % half, [P, SLOTS, HALF], F32) for half in range(2)]
-        for half in range(2):
-            for t in range(SLOTS):
-                route = bank(SLOTS * half + t)
-                route_pass(route, half, t, 1, True)
-                route_pass(route, half, t, 0, False)
-                nc.vector.tensor_tensor(diffs[half][:, t, :], route[:], depot[half, t][:], ALU.subtract)
+        routes = {}
+        for half, t in units[:EARLY_ROUTES]:
+            routes[half, t] = bank(SLOTS * half + t)
+            route_pass(routes[half, t], half, t, 0, True)
+        for half, t in units:
+            if (half, t) in routes:
+                route_pass(routes[half, t], half, t, 1, False)
+            else:
+                routes[half, t] = bank(SLOTS * half + t)
+                route_pass(routes[half, t], half, t, 1, True)
+                route_pass(routes[half, t], half, t, 0, False)
+            nc.vector.tensor_tensor(diffs[half][:, t, :], routes[half, t][:], depot[half][:, t, :], ALU.subtract)
 
         scaled = held("scaled", [P, SLOTS, S], F32, after="wr1_bf16_2")
         for t in range(SLOTS):
             nc.gpsimd.tensor_scalar(scaled[:, t, :], sines[:, t, :], gains[:, t, 0:1], 0.0, ALU.mult, ALU.add)
 
-        def cosines(cosine, diff):
-            size = keep.tile(list(diff.shape), F32, name="size", bufs=2)
-            nc.scalar.activation(size[:], diff, ACT.Abs)
-            nc.scalar.activation(cosine, size[:], ACT.Sin, bias=math.pi / 2, scale=-1.0)
+        first_half = held("cosine0", [P, 2, SLOTS, HALF // 2], F32)
+        cosines = {n * 256: first_half[:, n] for n in range(2)}
+        parts = [
+            (first_half[:, :, t, :], diffs[0][:, t, :].rearrange("p (n c) -> p n c", n=2)) for t in range(2)
+        ]
+        parts.extend((first_half[:, n, 2:SLOTS, :], diffs[0][:, 2:SLOTS, n * 256 : (n + 1) * 256]) for n in range(2))
+        for at in range(0, HALF, P):
+            cosines[HALF + at] = held("cosine_%d" % at, [P, SLOTS, P], F32)[:]
+            parts.append((cosines[HALF + at], diffs[1][:, :, at : at + P]))
 
-        cos_of = {0: held("cosine0", [P, SLOTS, HALF], F32)}
-        for low, high in ((0, 1), (1, 2), (2, 4)):
-            cosines(cos_of[0][:, low:high, :], diffs[0][:, low:high, :])
-        for first, width in PIECES:
-            cos_of[HALF + first] = held("cosine1_%d" % first, [P, SLOTS, width], F32)
-            cosines(cos_of[HALF + first][:], diffs[1][:, :, first : first + width])
+        def size_of(n):
+            size = held("size%d" % n, list(parts[n][1].shape), F32)
+            nc.scalar.activation(size[:], parts[n][1], ACT.Abs)
+            return size
 
-        w2_grouped = held("w2_bf16", [P, SLOTS * N], BF16, after="depot1_2")
-        nc.vector.tensor_copy(
-            w2_grouped[:].rearrange("p (n i t) -> p n t i", t=SLOTS, i=2),
-            w2_raw[:].rearrange("p t (n i) -> p n t i", i=2),
-        )
+        for first in range(0, len(parts), 2):
+            sizes = [size_of(n) for n in (first, first + 1)]
+            for n, size in zip((first, first + 1), sizes):
+                nc.scalar.activation(parts[n][0], size[:], ACT.Sin, bias=math.pi / 2, scale=-1.0)
 
-        def products(at, width):
-            h_grouped = held("h_bf16_%d" % at, [P, SLOTS * width], BF16)
+        h_grouped = [held("h_bf16_%d" % at, [P, SLOTS * width], BF16) for at, width in PIECES]
+
+        def products(n, at):
+            width = cosines[at].shape[2]
+            first = SLOTS * (at - PIECES[n][0])
             nc.vector.tensor_tensor(
-                h_grouped[:].rearrange("p (c i t) -> p c t i", t=SLOTS, i=2),
-                cos_of[at][:].rearrange("p t (c i) -> p c t i", i=2),
+                h_grouped[n][:, first : first + SLOTS * width].rearrange("p (c i t) -> p c t i", t=SLOTS, i=2),
+                cosines[at].rearrange("p t (c i) -> p c t i", i=2),
                 scaled[:, :, at : at + width].rearrange("p t (c i) -> p c t i", i=2),
                 ALU.mult,
             )
-            return h_grouped
 
         def quantise_h(at, width, h_grouped):
             h_codes = held("h_codes_%d" % at, [P, width], U32)
@@ -287,18 +319,20 @@ def tile_list_coldchain_spoilage_scores_kernel(
                     nc.vector.tensor_scalar_add(result[:, c, :], scores[:, 0:width], shifts[:, c : c + 1])
                 else:
                     nc.scalar.activation(result[:, c, :], scores[:, 0:width], ACT.Identity, bias=shifts[:, c : c + 1])
-            nc.sync.dma_start(out_view[:, :, at : at + width], result[:])
+                if width == HALF:
+                    nc.sync.dma_start(out_view[:, c, at : at + width], result[:, c, :])
+            if width < HALF:
+                nc.sync.dma_start(out_view[:, :, at : at + width], result[:])
 
-        steps = [(0, HALF)] + [(HALF + first, width) for first, width in PIECES]
-        h_grouped = products(*steps[0])
-        w2_codes = held("w2_codes", [P, N], U32)
+        w2_codes = held("w2_codes", [P, N], U32, after="depot0")
         w2_scales = held("w2_scales", [P, N], U8)
         nc.vector.quantize_mx(out=w2_codes[:].bitcast(FP8X4), scales=w2_scales[:], in_=w2_grouped[:])
-        h_of = [quantise_h(0, HALF, h_grouped)]
-        h_grouped = products(*steps[1])
-        for n in range(1, len(steps)):
-            later = products(*steps[n + 1]) if n + 1 < len(steps) else None
-            h_of.append(quantise_h(steps[n][0], steps[n][1], h_grouped))
-            h_grouped = later
-        for n, (at, width) in enumerate(steps):
-            scores_of(at, width, h_of[n], (2 * n, 2 * n + 1), (1,) if n + 1 == len(steps) else ())
+        h_of = []
+        for n, (first, width) in enumerate(PIECES):
+            for m, at in enumerate(at for at in cosines if first <= at < first + width):
+                products(n, at)
+                if m == 0 and n > 0:
+                    h_of.append(quantise_h(*PIECES[n - 1], h_grouped[n - 1]))
+        h_of.append(quantise_h(*PIECES[-1], h_grouped[-1]))
+        for n, (at, width) in enumerate(PIECES):
+            scores_of(at, width, h_of[n], (2 * n, 2 * n + 1), (1,) if n + 2 >= len(PIECES) else ())

@@ -25,7 +25,7 @@ SLOTS = 4
 GROUP = 16
 TAB2_ROW = 4
 W8_ROW = 8
-EARLY_TOTALS = 4
+WD_FIRST = 6
 EARLY_ROUTES = 2
 PIECES = ((0, 512), (512, 256), (768, 128), (896, 128))
 FLOPS = 2 * S * (2 * (1024 + 512) * H + H * N)
@@ -56,11 +56,10 @@ def tile_list_coldchain_spoilage_scores_kernel(
         w4_rows = held("w4_rows", [P, 2, H], U8)
         w8_rows = held("w8_rows", [P, H], U8)
         planes = held("planes", [P, 2, S], U8)
-        nc.gpsimd.memset(tab_rows[:, 0 : T // 2].bitcast(I32), 0)
-        nc.vector.memset(tab_rows[:, T // 2 : T].bitcast(I32), 0)
         nc.vector.memset(tab2_rows[:].bitcast(I32), 0)
+        nc.vector.memset(tab_rows[:].bitcast(I32), 0)
         nc.vector.memset(w8_rows[:].bitcast(I32), 0)
-        nc.gpsimd.memset(w4_rows[:].rearrange("p a c -> p (a c)").bitcast(I32), 0)
+        nc.vector.memset(w4_rows[:].rearrange("p a c -> p (a c)").bitcast(I32), 0)
         nc.vector.memset(planes[:].rearrange("p a c -> p (a c)").bitcast(I32), 0)
         zeros = held("zeros", [P, 8], F32)
         nc.vector.memset(zeros[:], 0.0)
@@ -111,28 +110,48 @@ def tile_list_coldchain_spoilage_scores_kernel(
             for n, t in enumerate(slots):
                 made[name, t] = (codes[:, n * P : (n + 1) * P].bitcast(FP8X4), scales[:, n * P : (n + 1) * P])
 
-        nc.sync.dma_start(lists[:], offs)
         nc.sync.dma_start(list2[:], offs2)
-        nc.sync.dma_start(tab_rows[0:P:4, :].bitcast(I32), tab_scales.bitcast(I32).rearrange("a q t -> q a t"))
-        wd_raw = load_rows("wd_raw", wd)
-        load_plane(nc.sync, tab2_rows, tab2_scales[0], TAB2_ROW)
         w8_raw = load_words("w8_raw", w8_words[0])
+        load_plane(nc.sync, tab2_rows, tab2_scales[0], TAB2_ROW)
+        nc.sync.dma_start(lists[:], offs)
         tab2_tile = load_words("tab2_tile", tab2_words[0])
+        nc.sync.dma_start(tab_rows[0:P:4, :].bitcast(I32), tab_scales.bitcast(I32).rearrange("a q t -> q a t"))
         load_plane(nc.sync, w8_rows, w8_scales[0], W8_ROW)
-        for r in range(4):
-            nc.gpsimd.dma_start(
-                w4_rows[r:P:32, :, :].bitcast(I32), w4_scales[:, r:16:4, :].bitcast(I32).rearrange("a q c -> q a c")
-            )
         w4_raw = held("w4_raw", [P, 2, H // 2], I32)
         nc.sync.dma_start(w4_raw[:], w4_words.bitcast(I32).rearrange("a p c -> p a c"))
+        wd_raw = load_rows("wd_raw", wd)
+        for r in range(4):
+            nc.sync.dma_start(
+                w4_rows[r:P:32, :, :].bitcast(I32), w4_scales[:, r:16:4, :].bitcast(I32).rearrange("a q c -> q a c")
+            )
         tab0_tile = load_words("tab0_tile", tab_words[0])
+        tab1_tile = load_words("tab1_tile", tab_words[1])
+
+        tab2_plane = held("tab2_plane", [P, S], U8)
+        nc.vector.tensor_copy(tab2_plane[:], tab2_rows[:].indirect(list2[:]))
+        w8_codes = held("w8_codes", [P, H], I32)
+        by_slot(w8_codes[:], w8_raw[:], 8)
+        w8_plane = held("w8_plane", [P, H], U8)
+        by_slot(w8_plane[:], w8_rows[:], 2)
+        w4_codes = held("w4_codes", [P, H], I32)
+        by_slot(w4_codes[:], w4_raw[:].rearrange("p a c -> p (a c)"), 4)
+        v2 = [held("v2_0", [P, HALF], U32), held("v2_1", [P, HALF], U32)]
+
+        def pick_depots(first, width):
+            nc.vector.tensor_copy(
+                v2[first // HALF][:, first % HALF : first % HALF + width],
+                tab2_tile[:].bitcast(U32).indirect(list2[:, first // GROUP : (first + width) // GROUP]),
+            )
+
+        pick_depots(0, QUARTER)
+        pick_depots(QUARTER, QUARTER)
+        pick_depots(HALF, HALF)
         tab_picked = held("tab_picked", [P, S], U8)
         nc.vector.tensor_copy(tab_picked[:], tab_rows[:].indirect(lists[:]))
         for d in range(4):
             nc.sync.dma_start(
                 planes[32 * d : 32 * d + 4, :, :].bitcast(I32), tab_picked[32 * d : 32 * d + 32 : 4, :].bitcast(I32)
             )
-        tab1_tile = load_words("tab1_tile", tab_words[1])
         wr0_raw = load_rows("wr0_raw", wr[0:512, :])
         wr1_raw = load_rows("wr1_raw", wr[512:1024, :])
         gains = held("gains", [P, SLOTS, 8], F32)
@@ -145,55 +164,43 @@ def tile_list_coldchain_spoilage_scores_kernel(
                 nc.sync.dma_start(gains[:, t, 0:1], gain.rearrange("(q t i o) -> t q i o", t=SLOTS, i=8, o=1)[t])
             nc.sync.dma_start(shifts[:], shift.rearrange("(c p) -> p c", p=P))
 
-        tab2_plane = held("tab2_plane", [P, S], U8)
-        nc.vector.tensor_copy(tab2_plane[:], tab2_rows[:].indirect(list2[:]))
         pairs = ((0, 1), (2, 3))
-        wd_grouped = [round_weight("wd", wd_raw, slots, nc.scalar.copy) for slots in pairs]
-        quantise_weight("wd", wd_grouped[0], pairs[0], after="tab2_rows")
-        quantise_weight("wd", wd_grouped[1], pairs[1], after="wd_bf16_0")
-        v2 = [held("v2_%d" % half, [P, HALF], U32) for half in range(2)]
-        for first, width in ((0, QUARTER), (QUARTER, QUARTER), (HALF, HALF)):
-            nc.vector.tensor_copy(
-                v2[first // HALF][:, first % HALF : first % HALF + width],
-                tab2_tile[:].bitcast(U32).indirect(list2[:, first // GROUP : (first + width) // GROUP]),
-            )
-        w8_codes = held("w8_codes", [P, H], I32)
-        by_slot(w8_codes[:], w8_raw[:], 8)
-        w8_plane = held("w8_plane", [P, H], U8)
-        by_slot(w8_plane[:], w8_rows[:], 2)
-        w4_codes = held("w4_codes", [P, H], I32)
-        by_slot(w4_codes[:], w4_raw[:].rearrange("p a c -> p (a c)"), 4)
-
         units = [(half, t) for half in range(2) for t in range(SLOTS)]
-        depot_sums = [bank(n) for n in range(len(units))]
-        depot = [held("depot%d" % half, [P, SLOTS, HALF], F32) for half in range(2)]
+        depot_sums = {unit: bank(n) for n, unit in enumerate(units)}
+        early_depots = held("early_depots", [P, 2, HALF], F32)
 
-        def depot_pass(target, t, first, width):
+        def depot_pass(t, first, width):
             cols = slice(t * P, (t + 1) * P)
+            inside = slice(first % HALF, first % HALF + width)
             nc.tensor.matmul_mx(
-                out=target, lhsT=w8_codes[:, cols].bitcast(FP8X4), lhsT_scale=w8_plane[W8_ROW:P, cols],
-                rhs=v2[first // HALF][:, first % HALF : first % HALF + width].bitcast(FP8X4),
+                out=depot_sums[first // HALF, t][:, inside], lhsT=w8_codes[:, cols].bitcast(FP8X4),
+                lhsT_scale=w8_plane[W8_ROW:P, cols], rhs=v2[first // HALF][:, inside].bitcast(FP8X4),
                 rhs_scale=tab2_plane[TAB2_ROW:P, first : first + width], start=True, stop=True,
             )
 
-        places = []
         for quarter in range(2):
-            for n, slots in enumerate(pairs):
-                for m, t in enumerate(slots):
-                    depot_pass(depot_sums[2 * quarter + n][:, m * QUARTER : (m + 1) * QUARTER], t, quarter * QUARTER, QUARTER)
-                places.append(depot[0][:, slots[0] : slots[0] + 2, quarter * QUARTER : (quarter + 1) * QUARTER])
-        for t in range(SLOTS):
-            depot_pass(depot_sums[SLOTS + t][:], t, HALF, HALF)
-            places.append(depot[1][:, t : t + 1, :])
+            for t in pairs[0]:
+                depot_pass(t, quarter * QUARTER, QUARTER)
+        for half, t in units[2:]:
+            depot_pass(t, half * HALF, HALF)
+        depot = {}
+        for n, unit in enumerate(units[:2]):
+            depot[unit] = early_depots[:, n, :]
+            nc.scalar.copy(depot[unit], depot_sums[unit][:])
+        wd_grouped = [round_weight("wd", wd_raw, slots, nc.scalar.copy) for slots in pairs]
+        quantise_weight("wd", wd_grouped[0], pairs[0])
+        quantise_weight("wd", wd_grouped[1], pairs[1])
+        late_depots = held("late_depots", [P, len(units) - 2, HALF], F32, after="wd_raw")
 
         def copy_depots(first, last):
             for n in range(first, last):
-                nc.scalar.copy(places[n], depot_sums[n][:].rearrange("p (m c) -> p m c", m=places[n].shape[1]))
+                depot[units[n]] = late_depots[:, n - 2, :]
+                nc.scalar.copy(depot[units[n]], depot_sums[units[n]][:])
 
-        copy_depots(0, 6)
-        w4_planes = held("w4_planes", [P, 2 * H], U8, after="w8_codes")
+        copy_depots(2, 4)
+        w4_planes = held("w4_planes", [P, 2 * H], U8, after="wd_bf16_0")
         by_slot(w4_planes[:], w4_rows[:].rearrange("p a c -> p (a c)"), 2)
-        copy_depots(6, len(units))
+        copy_depots(4, len(units))
         v = {(a, half): pick("v%d_%d" % (a, half), U32, (tab0_tile, tab1_tile)[a], lists, half)
              for a in range(2) for half in range(2)}
 
@@ -212,23 +219,21 @@ def tile_list_coldchain_spoilage_scores_kernel(
                 rhs_scale=tab2_plane[TAB2_ROW:P, span(half)], start=start, stop=stop,
             )
 
-        totals = {unit: bank(n) for n, unit in enumerate(units[:EARLY_TOTALS])}
-        for half, t in units[:EARLY_TOTALS]:
+        totals = {unit: bank(n) for n, unit in enumerate(units)}
+        for half, t in units[:WD_FIRST]:
             wd_pass(totals[half, t], half, t, True, False)
-        for half, t in units[:EARLY_TOTALS]:
-            w4_pass(totals[half, t], half, t, 0, False, False)
+        for t in range(SLOTS):
+            w4_pass(totals[0, t], 0, t, 0, False, False)
         sines = held("sines", [P, SLOTS, S], F32)
-        for half, t in units[:EARLY_TOTALS]:
+        for n, (half, t) in enumerate(units):
+            if half == 1:
+                w4_pass(totals[half, t], half, t, 0, n >= WD_FIRST, False)
+            if n >= WD_FIRST:
+                wd_pass(totals[half, t], half, t, False, False)
             w4_pass(totals[half, t], half, t, 1, False, True)
             nc.scalar.activation(sines[:, t, span(half)], totals[half, t][:], ACT.Sin)
-        for half, t in units[EARLY_TOTALS:]:
-            total = bank(SLOTS * half + t)
-            w4_pass(total, half, t, 1, True, False)
-            w4_pass(total, half, t, 0, False, False)
-            wd_pass(total, half, t, False, True)
-            nc.scalar.activation(sines[:, t, span(half)], total[:], ACT.Sin)
 
-        w2_grouped = held("w2_bf16", [P, SLOTS * N], BF16, after="wd_bf16_0")
+        w2_grouped = held("w2_bf16", [P, SLOTS * N], BF16, after="wd_bf16_2")
         nc.scalar.copy(
             w2_grouped[:].rearrange("p (n i t) -> p n t i", t=SLOTS, i=2),
             w2_raw[:].rearrange("p t (n i) -> p n t i", i=2),
@@ -260,7 +265,7 @@ def tile_list_coldchain_spoilage_scores_kernel(
                 routes[half, t] = bank(SLOTS * half + t)
                 route_pass(routes[half, t], half, t, 1, True)
                 route_pass(routes[half, t], half, t, 0, False)
-            nc.vector.tensor_tensor(diffs[half][:, t, :], routes[half, t][:], depot[half][:, t, :], ALU.subtract)
+            nc.vector.tensor_tensor(diffs[half][:, t, :], routes[half, t][:], depot[half, t], ALU.subtract)
 
         scaled = held("scaled", [P, SLOTS, S], F32, after="wr1_bf16_2")
         for t in range(SLOTS):
@@ -324,7 +329,7 @@ def tile_list_coldchain_spoilage_scores_kernel(
             if width < HALF:
                 nc.sync.dma_start(out_view[:, :, at : at + width], result[:])
 
-        w2_codes = held("w2_codes", [P, N], U32, after="depot0")
+        w2_codes = held("w2_codes", [P, N], U32, after="size2")
         w2_scales = held("w2_scales", [P, N], U8)
         nc.vector.quantize_mx(out=w2_codes[:].bitcast(FP8X4), scales=w2_scales[:], in_=w2_grouped[:])
         h_of = []

@@ -25,8 +25,7 @@ SLOTS = 4
 GROUP = 16
 TAB2_ROW = 4
 W8_ROW = 8
-WD_FIRST = 6
-EARLY_ROUTES = 2
+WARM_UPS = 4
 PIECES = ((0, 512), (512, 256), (768, 128), (896, 128))
 FLOPS = 2 * S * (2 * (1024 + 512) * H + H * N)
 
@@ -56,11 +55,11 @@ def tile_list_coldchain_spoilage_scores_kernel(
         w4_rows = held("w4_rows", [P, 2, H], U8)
         w8_rows = held("w8_rows", [P, H], U8)
         planes = held("planes", [P, 2, S], U8)
+        nc.gpsimd.memset(tab_rows[:].bitcast(I32), 0)
         nc.vector.memset(tab2_rows[:].bitcast(I32), 0)
-        nc.vector.memset(tab_rows[:].bitcast(I32), 0)
         nc.vector.memset(w8_rows[:].bitcast(I32), 0)
-        nc.vector.memset(w4_rows[:].rearrange("p a c -> p (a c)").bitcast(I32), 0)
         nc.vector.memset(planes[:].rearrange("p a c -> p (a c)").bitcast(I32), 0)
+        nc.vector.memset(w4_rows[:].rearrange("p a c -> p (a c)").bitcast(I32), 0)
         zeros = held("zeros", [P, 8], F32)
         nc.vector.memset(zeros[:], 0.0)
         preload = held("preload", [P, 8], F32)
@@ -76,9 +75,8 @@ def tile_list_coldchain_spoilage_scores_kernel(
             nc.sync.dma_start(tile[:], words.rearrange("p c b -> p (c b)").bitcast(I32))
             return tile
 
-        def load_plane(queue, rows, scales, first):
-            for r in range(4):
-                queue.dma_start(rows[first + r : P : 32, :].bitcast(I32), scales[r:16:4, :].bitcast(I32))
+        def load_row(rows, scales, first, r):
+            nc.sync.dma_start(rows[first + r : P : 32, :].bitcast(I32), scales[r:16:4, :].bitcast(I32))
 
         def by_slot(dst, src, words):
             nc.scalar.copy(
@@ -86,16 +84,10 @@ def tile_list_coldchain_spoilage_scores_kernel(
                 src.bitcast(U32).rearrange("p (a q t w) -> p a t q w", t=SLOTS, q=16, w=words),
             )
 
-        def pick(name, dtype, table, offsets, half):
-            picked = held(name, [P, HALF], dtype)
-            cols = slice(half * HALF // GROUP, (half + 1) * HALF // GROUP)
-            nc.vector.tensor_copy(picked[:], table[:].bitcast(dtype).indirect(offsets[:, cols]))
-            return picked
-
         made = {}
 
-        def round_weight(name, raw, slots, copy, after=None):
-            grouped = held("%s_bf16_%d" % (name, slots[0]), [P, len(slots) * HALF], BF16, after)
+        def round_weight(name, raw, slots, copy):
+            grouped = held("%s_bf16_%d" % (name, slots[0]), [P, len(slots) * HALF], BF16)
             for n, t in enumerate(slots):
                 copy(
                     grouped[:, n * HALF : (n + 1) * HALF].rearrange("p (q u i j) -> p q u j i", u=4, i=2, j=4),
@@ -110,48 +102,41 @@ def tile_list_coldchain_spoilage_scores_kernel(
             for n, t in enumerate(slots):
                 made[name, t] = (codes[:, n * P : (n + 1) * P].bitcast(FP8X4), scales[:, n * P : (n + 1) * P])
 
-        nc.sync.dma_start(list2[:], offs2)
-        w8_raw = load_words("w8_raw", w8_words[0])
-        load_plane(nc.sync, tab2_rows, tab2_scales[0], TAB2_ROW)
         nc.sync.dma_start(lists[:], offs)
-        tab2_tile = load_words("tab2_tile", tab2_words[0])
         nc.sync.dma_start(tab_rows[0:P:4, :].bitcast(I32), tab_scales.bitcast(I32).rearrange("a q t -> q a t"))
-        load_plane(nc.sync, w8_rows, w8_scales[0], W8_ROW)
-        w4_raw = held("w4_raw", [P, 2, H // 2], I32)
-        nc.sync.dma_start(w4_raw[:], w4_words.bitcast(I32).rearrange("a p c -> p a c"))
+        nc.sync.dma_start(list2[:], offs2)
         wd_raw = load_rows("wd_raw", wd)
         for r in range(4):
-            nc.sync.dma_start(
-                w4_rows[r:P:32, :, :].bitcast(I32), w4_scales[:, r:16:4, :].bitcast(I32).rearrange("a q c -> q a c")
-            )
-        tab0_tile = load_words("tab0_tile", tab_words[0])
-        tab1_tile = load_words("tab1_tile", tab_words[1])
+            load_row(tab2_rows, tab2_scales[0], TAB2_ROW, r)
+        w8_raw = load_words("w8_raw", w8_words[0])
+        tab2_tile = load_words("tab2_tile", tab2_words[0])
+        for r in range(4):
+            load_row(w8_rows, w8_scales[0], W8_ROW, r)
+        w4_raw = held("w4_raw", [P, 2, H // 2], I32)
+        nc.sync.dma_start(w4_raw[:], w4_words.bitcast(I32).rearrange("a p c -> p a c"))
 
-        tab2_plane = held("tab2_plane", [P, S], U8)
-        nc.vector.tensor_copy(tab2_plane[:], tab2_rows[:].indirect(list2[:]))
-        w8_codes = held("w8_codes", [P, H], I32)
-        by_slot(w8_codes[:], w8_raw[:], 8)
-        w8_plane = held("w8_plane", [P, H], U8)
-        by_slot(w8_plane[:], w8_rows[:], 2)
-        w4_codes = held("w4_codes", [P, H], I32)
-        by_slot(w4_codes[:], w4_raw[:].rearrange("p a c -> p (a c)"), 4)
-        v2 = [held("v2_0", [P, HALF], U32), held("v2_1", [P, HALF], U32)]
-
-        def pick_depots(first, width):
-            nc.vector.tensor_copy(
-                v2[first // HALF][:, first % HALF : first % HALF + width],
-                tab2_tile[:].bitcast(U32).indirect(list2[:, first // GROUP : (first + width) // GROUP]),
-            )
-
-        pick_depots(0, QUARTER)
-        pick_depots(QUARTER, QUARTER)
-        pick_depots(HALF, HALF)
         tab_picked = held("tab_picked", [P, S], U8)
         nc.vector.tensor_copy(tab_picked[:], tab_rows[:].indirect(lists[:]))
-        for d in range(4):
+        tab2_plane = held("tab2_plane", [P, S], U8)
+        nc.vector.tensor_copy(tab2_plane[:], tab2_rows[:].indirect(list2[:]))
+
+        def move(d):
             nc.sync.dma_start(
                 planes[32 * d : 32 * d + 4, :, :].bitcast(I32), tab_picked[32 * d : 32 * d + 32 : 4, :].bitcast(I32)
             )
+
+        def load_w4_row(r):
+            nc.sync.dma_start(
+                w4_rows[r:P:32, :, :].bitcast(I32), w4_scales[:, r:16:4, :].bitcast(I32).rearrange("a q c -> q a c")
+            )
+
+        load_w4_row(0)
+        tab0_tile = load_words("tab0_tile", tab_words[0])
+        for r in range(1, 4):
+            load_w4_row(r)
+        tab1_tile = load_words("tab1_tile", tab_words[1])
+        for d in range(4):
+            move(d)
         wr0_raw = load_rows("wr0_raw", wr[0:512, :])
         wr1_raw = load_rows("wr1_raw", wr[512:1024, :])
         gains = held("gains", [P, SLOTS, 8], F32)
@@ -164,108 +149,154 @@ def tile_list_coldchain_spoilage_scores_kernel(
                 nc.sync.dma_start(gains[:, t, 0:1], gain.rearrange("(q t i o) -> t q i o", t=SLOTS, i=8, o=1)[t])
             nc.sync.dma_start(shifts[:], shift.rearrange("(c p) -> p c", p=P))
 
+        every = tuple(range(SLOTS))
         pairs = ((0, 1), (2, 3))
-        units = [(half, t) for half in range(2) for t in range(SLOTS)]
-        depot_sums = {unit: bank(n) for n, unit in enumerate(units)}
-        early_depots = held("early_depots", [P, 2, HALF], F32)
+        wd_grouped = round_weight("wd", wd_raw, every, nc.scalar.copy)
+        w8_codes = held("w8_codes", [P, H], I32)
+        by_slot(w8_codes[:], w8_raw[:], 8)
+        w8_plane = held("w8_plane", [P, H], U8)
+        by_slot(w8_plane[:], w8_rows[:], 2)
 
-        def depot_pass(t, first, width):
+        for n in range(WARM_UPS):
+            nc.tensor.matmul_mx(
+                out=bank(SLOTS + n)[:], lhsT=w8_raw[:, 0:P].bitcast(FP8X4), lhsT_scale=tab_picked[:, 0:P],
+                rhs=w8_raw[:].bitcast(FP8X4), rhs_scale=tab_picked[:, 0:HALF], start=True, stop=True,
+            )
+
+        v2 = [held("v2_0", [P, HALF], U32), held("v2_1", [P, HALF], U32)]
+
+        def pick_depots(first, width):
+            nc.vector.tensor_copy(
+                v2[first // HALF][:, first % HALF : first % HALF + width],
+                tab2_tile[:].bitcast(U32).indirect(list2[:, first // GROUP : (first + width) // GROUP]),
+            )
+
+        pick_depots(0, QUARTER)
+        pick_depots(QUARTER, QUARTER)
+        pick_depots(HALF, HALF)
+        quantise_weight("wd", wd_grouped, every, after="w8_rows")
+
+        units = [(half, t) for half in range(2) for t in range(SLOTS)]
+        depots = held("depots", [P, 2, SLOTS, HALF], F32)
+
+        def depot_pass(sums, t, first, width):
             cols = slice(t * P, (t + 1) * P)
             inside = slice(first % HALF, first % HALF + width)
             nc.tensor.matmul_mx(
-                out=depot_sums[first // HALF, t][:, inside], lhsT=w8_codes[:, cols].bitcast(FP8X4),
+                out=sums, lhsT=w8_codes[:, cols].bitcast(FP8X4),
                 lhsT_scale=w8_plane[W8_ROW:P, cols], rhs=v2[first // HALF][:, inside].bitcast(FP8X4),
                 rhs_scale=tab2_plane[TAB2_ROW:P, first : first + width], start=True, stop=True,
             )
 
+        w4_codes = held("w4_codes", [P, H], I32)
+        by_slot(w4_codes[:], w4_raw[:].rearrange("p a c -> p (a c)"), 4)
         for quarter in range(2):
-            for t in pairs[0]:
-                depot_pass(t, quarter * QUARTER, QUARTER)
-        for half, t in units[2:]:
-            depot_pass(t, half * HALF, HALF)
-        depot = {}
-        for n, unit in enumerate(units[:2]):
-            depot[unit] = early_depots[:, n, :]
-            nc.scalar.copy(depot[unit], depot_sums[unit][:])
-        wd_grouped = [round_weight("wd", wd_raw, slots, nc.scalar.copy) for slots in pairs]
-        quantise_weight("wd", wd_grouped[0], pairs[0])
-        quantise_weight("wd", wd_grouped[1], pairs[1])
-        late_depots = held("late_depots", [P, len(units) - 2, HALF], F32, after="wd_raw")
-
-        def copy_depots(first, last):
-            for n in range(first, last):
-                depot[units[n]] = late_depots[:, n - 2, :]
-                nc.scalar.copy(depot[units[n]], depot_sums[units[n]][:])
-
-        copy_depots(2, 4)
-        w4_planes = held("w4_planes", [P, 2 * H], U8, after="wd_bf16_0")
+            for n, slots in enumerate(pairs):
+                sums = bank(2 * quarter + n)
+                for m, t in enumerate(slots):
+                    depot_pass(sums[:, m * QUARTER : (m + 1) * QUARTER], t, quarter * QUARTER, QUARTER)
+                nc.scalar.copy(
+                    depots[:, 0, slots[0] : slots[0] + 2, quarter * QUARTER : (quarter + 1) * QUARTER],
+                    sums[:].rearrange("p (m c) -> p m c", m=2),
+                )
+        w4_planes = held("w4_planes", [P, 2 * H], U8)
         by_slot(w4_planes[:], w4_rows[:].rearrange("p a c -> p (a c)"), 2)
-        copy_depots(4, len(units))
-        v = {(a, half): pick("v%d_%d" % (a, half), U32, (tab0_tile, tab1_tile)[a], lists, half)
-             for a in range(2) for half in range(2)}
+        for t in every:
+            sums = bank(SLOTS + t)
+            depot_pass(sums[:], t, HALF, HALF)
+            nc.scalar.copy(depots[:, 1, t, :], sums[:])
+        v = {(a, half): [] for a in range(2) for half in range(2)}
 
-        def w4_pass(total, half, t, a, start, stop):
-            at = a * H + t * P
-            nc.tensor.matmul_mx(
-                out=total[:], lhsT=w4_codes[:, at // 2 : (at + P) // 2].bitcast(FP4X4),
-                lhsT_scale=w4_planes[:, at : at + P], rhs=v[a, half][:].bitcast(FP8X4),
-                rhs_scale=planes[:, a, span(half)], start=start, stop=stop,
-            )
+        def pick_legs(a, first, width, after=None):
+            picked = held("v%d_%d" % (a, first), [P, width], U32, after)
+            cols = slice(first // GROUP, (first + width) // GROUP)
+            nc.vector.tensor_copy(picked[:], (tab0_tile, tab1_tile)[a][:].bitcast(U32).indirect(lists[:, cols]))
+            v[a, first // HALF].append((first, width, picked))
 
-        def wd_pass(total, half, t, start, stop):
-            codes, scales = made["wd", t]
-            nc.tensor.matmul_mx(
-                out=total[:], lhsT=codes, lhsT_scale=scales, rhs=v2[half][:].bitcast(FP8X4),
-                rhs_scale=tab2_plane[TAB2_ROW:P, span(half)], start=start, stop=stop,
-            )
+        pick_legs(0, 0, HALF)
+        pick_legs(0, HALF, QUARTER)
+        pick_legs(1, 0, QUARTER)
+        pick_legs(1, QUARTER, QUARTER)
+        pick_legs(1, HALF, HALF)
+        pick_legs(0, HALF + QUARTER, QUARTER, after="tab_picked")
 
-        totals = {unit: bank(n) for n, unit in enumerate(units)}
-        for half, t in units[:WD_FIRST]:
-            wd_pass(totals[half, t], half, t, True, False)
-        for t in range(SLOTS):
-            w4_pass(totals[0, t], 0, t, 0, False, False)
+        def leg_pass(sums, codes, scales, half, a, start, stop):
+            for n, (first, width, picked) in enumerate(v[a, half]):
+                nc.tensor.matmul_mx(
+                    out=sums[:, first % HALF : first % HALF + width], lhsT=codes, lhsT_scale=scales,
+                    rhs=picked[:].bitcast(FP8X4), rhs_scale=planes[:, a, first : first + width],
+                    start=start and n == 0, stop=stop and n + 1 == len(v[a, half]),
+                )
+
         sines = held("sines", [P, SLOTS, S], F32)
-        for n, (half, t) in enumerate(units):
-            if half == 1:
-                w4_pass(totals[half, t], half, t, 0, n >= WD_FIRST, False)
-            if n >= WD_FIRST:
-                wd_pass(totals[half, t], half, t, False, False)
-            w4_pass(totals[half, t], half, t, 1, False, True)
-            nc.scalar.activation(sines[:, t, span(half)], totals[half, t][:], ACT.Sin)
 
-        w2_grouped = held("w2_bf16", [P, SLOTS * N], BF16, after="wd_bf16_2")
+        def w4_operand(t, a):
+            at = a * H + t * P
+            return w4_codes[:, at // 2 : (at + P) // 2].bitcast(FP4X4), w4_planes[:, at : at + P]
+
+        def window_pass(sums, weight, moving, plane, first, width, start=False, stop=False):
+            nc.tensor.matmul_mx(
+                out=sums, lhsT=weight[0], lhsT_scale=weight[1], rhs=moving.bitcast(FP8X4),
+                rhs_scale=plane[:, first : first + width], start=start, stop=stop,
+            )
+
+        early = {(quarter, n): bank(2 * quarter + n) for quarter in range(2) for n in range(2)}
+        for (quarter, n), sums in early.items():
+            cols = slice(quarter * QUARTER, (quarter + 1) * QUARTER)
+            for m, t in enumerate(pairs[n]):
+                window_pass(sums[:, m * QUARTER : (m + 1) * QUARTER], made["wd", t], v2[0][:, cols],
+                            tab2_plane[TAB2_ROW:P, :], quarter * QUARTER, QUARTER, start=m == 0)
+        totals = [bank(SLOTS + t) for t in every]
+
+        def wd_pass(t, start):
+            window_pass(totals[t][:], made["wd", t], v2[1][:], tab2_plane[TAB2_ROW:P, :], HALF, HALF, start=start)
+
+        for t in pairs[0]:
+            wd_pass(t, True)
+        for (quarter, n), sums in early.items():
+            cols = slice(quarter * QUARTER, (quarter + 1) * QUARTER)
+            for a, moving in enumerate((v[0, 0][0][2][:, cols], v[1, 0][quarter][2][:])):
+                for m, t in enumerate(pairs[n]):
+                    window_pass(sums[:, m * QUARTER : (m + 1) * QUARTER], w4_operand(t, a), moving,
+                                planes[:, a, :], quarter * QUARTER, QUARTER, stop=a == 1 and m == 1)
+            nc.scalar.activation(
+                sines[:, pairs[n][0] : pairs[n][0] + 2, cols], sums[:].rearrange("p (m c) -> p m c", m=2), ACT.Sin
+            )
+        for t in every[:3]:
+            leg_pass(totals[t], *w4_operand(t, 1), 1, 1, t in pairs[1], False)
+        for t in every:
+            if t == 3:
+                leg_pass(totals[t], *w4_operand(t, 1), 1, 1, True, False)
+            if t in pairs[1]:
+                wd_pass(t, False)
+            leg_pass(totals[t], *w4_operand(t, 0), 1, 0, False, True)
+            nc.scalar.activation(sines[:, t, span(1)], totals[t][:], ACT.Sin)
+
+        w2_grouped = held("w2_bf16", [P, SLOTS * N], BF16)
         nc.scalar.copy(
             w2_grouped[:].rearrange("p (n i t) -> p n t i", t=SLOTS, i=2),
             w2_raw[:].rearrange("p t (n i) -> p n t i", i=2),
         )
 
-        grouped = [round_weight("wr0", wr0_raw, slots, nc.vector.tensor_copy) for slots in pairs]
-        for n, slots in enumerate(pairs):
-            quantise_weight("wr0", grouped[n], slots)
-        grouped = [round_weight("wr1", wr1_raw, slots, nc.vector.tensor_copy) for slots in pairs]
-        quantise_weight("wr1", grouped[0], pairs[0])
-        quantise_weight("wr1", grouped[1], pairs[1])
+        for name, raw in (("wr0", wr0_raw), ("wr1", wr1_raw)):
+            grouped = [round_weight(name, raw, slots, nc.vector.tensor_copy) for slots in pairs]
+            for n, slots in enumerate(pairs):
+                quantise_weight(name, grouped[n], slots)
 
-        def route_pass(route, half, t, a, start):
+        routes = {unit: bank(n) for n, unit in enumerate(units)}
+
+        opened = set()
+
+        def route_pass(half, t, a):
             codes, scales = made["wr%d" % a, t]
-            nc.tensor.matmul_mx(
-                out=route[:], lhsT=codes, lhsT_scale=scales, rhs=v[a, half][:].bitcast(FP8X4),
-                rhs_scale=planes[:, a, span(half)], start=start, stop=not start,
-            )
+            leg_pass(routes[half, t], codes, scales, half, a, (half, t) not in opened, (half, t) in opened)
+            opened.add((half, t))
 
         diffs = [held("diff%d" % half, [P, SLOTS, HALF], F32) for half in range(2)]
-        routes = {}
-        for half, t in units[:EARLY_ROUTES]:
-            routes[half, t] = bank(SLOTS * half + t)
-            route_pass(routes[half, t], half, t, 0, True)
         for half, t in units:
-            if (half, t) in routes:
-                route_pass(routes[half, t], half, t, 1, False)
-            else:
-                routes[half, t] = bank(SLOTS * half + t)
-                route_pass(routes[half, t], half, t, 1, True)
-                route_pass(routes[half, t], half, t, 0, False)
-            nc.vector.tensor_tensor(diffs[half][:, t, :], routes[half, t][:], depot[half, t], ALU.subtract)
+            route_pass(half, t, 1 if (half, t) in units[1:] else 0)
+            route_pass(half, t, 0 if (half, t) in units[1:] else 1)
+            nc.vector.tensor_tensor(diffs[half][:, t, :], routes[half, t][:], depots[:, half, t, :], ALU.subtract)
 
         scaled = held("scaled", [P, SLOTS, S], F32, after="wr1_bf16_2")
         for t in range(SLOTS):

@@ -40,7 +40,7 @@ def tile_list_coldchain_spoilage_scores_kernel(
         psum = ctx.enter_context(tc.psum_pool(name="psum", bufs=1))
 
         def held(name, shape, dtype, after=None):
-            return keep.tile(shape, dtype, name=name, tag=after or name, align_bytes=64)
+            return keep.tile(shape, dtype, name=name, tag=after or name, align_bytes=256)
 
         def bank(number):
             return psum.tile([P, HALF], F32, name="bank%d" % number)

@@ -55,9 +55,11 @@ def tile_list_coldchain_spoilage_scores_kernel(
         w4_rows = held("w4_rows", [P, 2, H], U8)
         w8_rows = held("w8_rows", [P, H], U8)
         planes = held("planes", [P, 2, S], U8)
-        nc.gpsimd.memset(tab_rows[:].bitcast(I32), 0)
-        nc.vector.memset(tab2_rows[:].bitcast(I32), 0)
+        tab2_plane = held("tab2_plane", [P, S], U8)
+        nc.gpsimd.memset(tab2_rows[:].bitcast(I32), 0)
+        nc.vector.memset(tab_rows[:].bitcast(I32), 0)
         nc.vector.memset(w8_rows[:].bitcast(I32), 0)
+        nc.vector.memset(tab2_plane[:].bitcast(I32), 0)
         nc.vector.memset(planes[:].rearrange("p a c -> p (a c)").bitcast(I32), 0)
         nc.vector.memset(w4_rows[:].rearrange("p a c -> p (a c)").bitcast(I32), 0)
         zeros = held("zeros", [P, 8], F32)
@@ -102,23 +104,26 @@ def tile_list_coldchain_spoilage_scores_kernel(
             for n, t in enumerate(slots):
                 made[name, t] = (codes[:, n * P : (n + 1) * P].bitcast(FP8X4), scales[:, n * P : (n + 1) * P])
 
-        nc.sync.dma_start(lists[:], offs)
-        nc.sync.dma_start(tab_rows[0:P:4, :].bitcast(I32), tab_scales.bitcast(I32).rearrange("a q t -> q a t"))
         nc.sync.dma_start(list2[:], offs2)
+        nc.sync.dma_start(tab2_rows[0:P:8, :].bitcast(I32), tab2_scales[0].bitcast(I32))
+        nc.sync.dma_start(lists[:], offs)
         wd_raw = load_rows("wd_raw", wd)
-        for r in range(4):
-            load_row(tab2_rows, tab2_scales[0], TAB2_ROW, r)
+        nc.sync.dma_start(tab_rows[0:P:4, :].bitcast(I32), tab_scales.bitcast(I32).rearrange("a q t -> q a t"))
         w8_raw = load_words("w8_raw", w8_words[0])
-        tab2_tile = load_words("tab2_tile", tab2_words[0])
         for r in range(4):
             load_row(w8_rows, w8_scales[0], W8_ROW, r)
+        tab2_tile = load_words("tab2_tile", tab2_words[0])
         w4_raw = held("w4_raw", [P, 2, H // 2], I32)
         nc.sync.dma_start(w4_raw[:], w4_words.bitcast(I32).rearrange("a p c -> p a c"))
 
+        tab2_picked = held("tab2_picked", [P, S], U8)
+        nc.vector.tensor_copy(tab2_picked[:], tab2_rows[:].indirect(list2[:]))
         tab_picked = held("tab_picked", [P, S], U8)
         nc.vector.tensor_copy(tab_picked[:], tab_rows[:].indirect(lists[:]))
-        tab2_plane = held("tab2_plane", [P, S], U8)
-        nc.vector.tensor_copy(tab2_plane[:], tab2_rows[:].indirect(list2[:]))
+        for r in range(4):
+            nc.sync.dma_start(
+                tab2_plane[TAB2_ROW + r : P : 32, :].bitcast(I32), tab2_picked[8 * r : P : 32, :].bitcast(I32)
+            )
 
         def move(d):
             nc.sync.dma_start(
@@ -130,12 +135,11 @@ def tile_list_coldchain_spoilage_scores_kernel(
                 w4_rows[r:P:32, :, :].bitcast(I32), w4_scales[:, r:16:4, :].bitcast(I32).rearrange("a q c -> q a c")
             )
 
-        load_w4_row(0)
         tab0_tile = load_words("tab0_tile", tab_words[0])
-        for r in range(1, 4):
+        for r in range(4):
             load_w4_row(r)
         tab1_tile = load_words("tab1_tile", tab_words[1])
-        for d in range(4):
+        for d in (0, 2, 1, 3):
             move(d)
         wr0_raw = load_rows("wr0_raw", wr[0:512, :])
         wr1_raw = load_rows("wr1_raw", wr[512:1024, :])
@@ -159,8 +163,8 @@ def tile_list_coldchain_spoilage_scores_kernel(
 
         for n in range(WARM_UPS):
             nc.tensor.matmul_mx(
-                out=bank(SLOTS + n)[:], lhsT=w8_raw[:, 0:P].bitcast(FP8X4), lhsT_scale=tab_picked[:, 0:P],
-                rhs=w8_raw[:].bitcast(FP8X4), rhs_scale=tab_picked[:, 0:HALF], start=True, stop=True,
+                out=bank(SLOTS + n)[:], lhsT=w8_raw[:, 0:P].bitcast(FP8X4), lhsT_scale=tab2_picked[:, 0:P],
+                rhs=w8_raw[:].bitcast(FP8X4), rhs_scale=tab2_picked[:, 0:HALF], start=True, stop=True,
             )
 
         v2 = [held("v2_0", [P, HALF], U32), held("v2_1", [P, HALF], U32)]
@@ -174,7 +178,7 @@ def tile_list_coldchain_spoilage_scores_kernel(
         pick_depots(0, QUARTER)
         pick_depots(QUARTER, QUARTER)
         pick_depots(HALF, HALF)
-        quantise_weight("wd", wd_grouped, every, after="w8_rows")
+        quantise_weight("wd", wd_grouped, every, after="tab2_picked")
 
         units = [(half, t) for half in range(2) for t in range(SLOTS)]
         depots = held("depots", [P, 2, SLOTS, HALF], F32)

@@ -105,11 +105,11 @@ def tile_list_coldchain_spoilage_scores_kernel(
                 made[name, t] = (codes[:, n * P : (n + 1) * P].bitcast(FP8X4), scales[:, n * P : (n + 1) * P])
 
         nc.sync.dma_start(list2[:], offs2)
-        nc.sync.dma_start(tab2_rows[0:P:8, :].bitcast(I32), tab2_scales[0].bitcast(I32))
-        nc.sync.dma_start(lists[:], offs)
-        wd_raw = load_rows("wd_raw", wd)
-        nc.sync.dma_start(tab_rows[0:P:4, :].bitcast(I32), tab_scales.bitcast(I32).rearrange("a q t -> q a t"))
+        nc.sync.dma_start(tab2_rows[4:P:8, :].bitcast(I32), tab2_scales[0].bitcast(I32))
         w8_raw = load_words("w8_raw", w8_words[0])
+        nc.sync.dma_start(lists[:], offs)
+        nc.sync.dma_start(tab_rows[0:P:4, :].bitcast(I32), tab_scales.bitcast(I32).rearrange("a q t -> q a t"))
+        wd_raw = load_rows("wd_raw", wd)
         for r in range(4):
             load_row(w8_rows, w8_scales[0], W8_ROW, r)
         tab2_tile = load_words("tab2_tile", tab2_words[0])
@@ -122,7 +122,7 @@ def tile_list_coldchain_spoilage_scores_kernel(
         nc.vector.tensor_copy(tab_picked[:], tab_rows[:].indirect(lists[:]))
         for r in range(4):
             nc.sync.dma_start(
-                tab2_plane[TAB2_ROW + r : P : 32, :].bitcast(I32), tab2_picked[8 * r : P : 32, :].bitcast(I32)
+                tab2_plane[TAB2_ROW + r : P : 32, :].bitcast(I32), tab2_picked[4 + 8 * r : P : 32, :].bitcast(I32)
             )
 
         def move(d):
@@ -155,16 +155,16 @@ def tile_list_coldchain_spoilage_scores_kernel(
 
         every = tuple(range(SLOTS))
         pairs = ((0, 1), (2, 3))
-        wd_grouped = round_weight("wd", wd_raw, every, nc.scalar.copy)
         w8_codes = held("w8_codes", [P, H], I32)
         by_slot(w8_codes[:], w8_raw[:], 8)
+        wd_grouped = round_weight("wd", wd_raw, every, nc.scalar.copy)
         w8_plane = held("w8_plane", [P, H], U8)
         by_slot(w8_plane[:], w8_rows[:], 2)
 
         for n in range(WARM_UPS):
             nc.tensor.matmul_mx(
-                out=bank(SLOTS + n)[:], lhsT=w8_raw[:, 0:P].bitcast(FP8X4), lhsT_scale=tab2_picked[:, 0:P],
-                rhs=w8_raw[:].bitcast(FP8X4), rhs_scale=tab2_picked[:, 0:HALF], start=True, stop=True,
+                out=bank(SLOTS + n)[:], lhsT=w8_raw[:, 0:P].bitcast(FP8X4), lhsT_scale=tab2_picked[TAB2_ROW:P, 0:P],
+                rhs=w8_raw[:].bitcast(FP8X4), rhs_scale=tab2_picked[TAB2_ROW:P, 0:HALF], start=True, stop=True,
             )
 
         v2 = [held("v2_0", [P, HALF], U32), held("v2_1", [P, HALF], U32)]

@@ -25,7 +25,6 @@ SLOTS = 4
 GROUP = 16
 TAB2_ROW = 4
 W8_ROW = 8
-WARM_UPS = 4
 PIECES = ((0, 512), (512, 256), (768, 128), (896, 128))
 FLOPS = 2 * S * (2 * (1024 + 512) * H + H * N)
 
@@ -160,12 +159,6 @@ def tile_list_coldchain_spoilage_scores_kernel(
         wd_grouped = round_weight("wd", wd_raw, every, nc.scalar.copy)
         w8_plane = held("w8_plane", [P, H], U8)
         by_slot(w8_plane[:], w8_rows[:], 2)
-
-        for n in range(WARM_UPS):
-            nc.tensor.matmul_mx(
-                out=bank(SLOTS + n)[:], lhsT=w8_raw[:, 0:P].bitcast(FP8X4), lhsT_scale=tab2_picked[TAB2_ROW:P, 0:P],
-                rhs=w8_raw[:].bitcast(FP8X4), rhs_scale=tab2_picked[TAB2_ROW:P, 0:HALF], start=True, stop=True,
-            )
 
         v2 = [held("v2_0", [P, HALF], U32), held("v2_1", [P, HALF], U32)]
 

@@ -61,10 +61,6 @@ def tile_list_coldchain_spoilage_scores_kernel(
         nc.vector.memset(tab2_plane[:].bitcast(I32), 0)
         nc.vector.memset(planes[:].rearrange("p a c -> p (a c)").bitcast(I32), 0)
         nc.vector.memset(w4_rows[:].rearrange("p a c -> p (a c)").bitcast(I32), 0)
-        zeros = held("zeros", [P, 8], F32)
-        nc.vector.memset(zeros[:], 0.0)
-        preload = held("preload", [P, 8], F32)
-        nc.scalar.activation(preload[:], zeros[:], ACT.Sin)
 
         def load_rows(name, rows):
             raw = held(name, [P, 4, H], F32)

@@ -120,10 +120,8 @@ def tile_list_coldchain_spoilage_scores_kernel(
                 tab2_plane[TAB2_ROW + r : P : 32, :].bitcast(I32), tab2_picked[4 + 8 * r : P : 32, :].bitcast(I32)
             )
 
-        def move(d):
-            nc.sync.dma_start(
-                planes[32 * d : 32 * d + 4, :, :].bitcast(I32), tab_picked[32 * d : 32 * d + 32 : 4, :].bitcast(I32)
-            )
+        def move(a, r):
+            nc.sync.dma_start(planes[r:P:32, a, :].bitcast(I32), tab_picked[8 * r + 4 * a : P : 32, :].bitcast(I32))
 
         def load_w4_row(r):
             nc.sync.dma_start(
@@ -133,9 +131,12 @@ def tile_list_coldchain_spoilage_scores_kernel(
         tab0_tile = load_words("tab0_tile", tab_words[0])
         for r in range(4):
             load_w4_row(r)
+        moves = [(a, r) for a in range(2) for r in range(4)]
+        for a, r in moves[:2]:
+            move(a, r)
         tab1_tile = load_words("tab1_tile", tab_words[1])
-        for d in (0, 2, 1, 3):
-            move(d)
+        for a, r in moves[2:]:
+            move(a, r)
         wr0_raw = load_rows("wr0_raw", wr[0:512, :])
         wr1_raw = load_rows("wr1_raw", wr[512:1024, :])
         gains = held("gains", [P, SLOTS, 8], F32)

@@ -311,10 +311,12 @@ def tile_list_coldchain_spoilage_scores_kernel(
             nc.scalar.activation(size[:], parts[n][1], ACT.Abs)
             return size
 
-        for first in range(0, len(parts), 2):
-            sizes = [size_of(n) for n in (first, first + 1)]
-            for n, size in zip((first, first + 1), sizes):
-                nc.scalar.activation(parts[n][0], size[:], ACT.Sin, bias=math.pi / 2, scale=-1.0)
+        sizes = []
+        for group in ((0, 1, 2), (3, 4), (5, 6, 7)):
+            for n in group:
+                while len(sizes) <= min(n + 1, group[-1]):
+                    sizes.append(size_of(len(sizes)))
+                nc.scalar.activation(parts[n][0], sizes[n][:], ACT.Sin, bias=math.pi / 2, scale=-1.0)
 
         h_grouped = [held("h_bf16_%d" % at, [P, SLOTS * width], BF16) for at, width in PIECES]
 

import math
from contextlib import ExitStack

from concourse import mybir

F32 = mybir.dt.float32
BF16 = mybir.dt.bfloat16
I32 = mybir.dt.int32
U32 = mybir.dt.uint32
U16 = mybir.dt.uint16
U8 = mybir.dt.uint8
FP8X4 = mybir.dt.float8_e4m3fn_x4
FP4X4 = mybir.dt.float4_e2m1fn_x4
ACT = mybir.ActivationFunctionType
ALU = mybir.AluOpType

P = 128
T = 2048
S = 1024
H = 512
N = 256
HALF = 512
QUARTER = 256
SLOTS = 4
GROUP = 16
TAB2_ROW = 4
W8_ROW = 8
PIECES = ((0, 512), (512, 256), (768, 128), (896, 128))
FLOPS = 2 * S * (2 * (1024 + 512) * H + H * N)


def tile_list_coldchain_spoilage_scores_kernel(
    tc, tab_words, tab_scales, tab2_words, tab2_scales, offs, offs2, w4_words, w4_scales, w8_words, w8_scales,
    wd, wr, gain, w2, shift, out,
):
    nc = tc.nc
    with ExitStack() as ctx:
        keep = ctx.enter_context(tc.tile_pool(name="keep", bufs=1))
        psum = ctx.enter_context(tc.psum_pool(name="psum", bufs=1))

        def held(name, shape, dtype, after=None):
            return keep.tile(shape, dtype, name=name, tag=after or name, align_bytes=256)

        def bank(number):
            return psum.tile([P, HALF], F32, name="bank%d" % number)

        def span(half):
            return slice(half * HALF, (half + 1) * HALF)

        lists = held("lists", [P, S // GROUP], U16)
        list2 = held("list2", [P, S // GROUP], U16)
        tab_rows = held("tab_rows", [P, T], U8)
        tab2_rows = held("tab2_rows", [P, T], U8)
        w4_rows = held("w4_rows", [P, 2, H], U8)
        w8_rows = held("w8_rows", [P, H], U8)
        planes = held("planes", [P, 2, S], U8)
        tab2_plane = held("tab2_plane", [P, S], U8)
        nc.gpsimd.memset(tab2_rows[:].bitcast(I32), 0)
        nc.vector.memset(tab_rows[:].bitcast(I32), 0)
        nc.vector.memset(w8_rows[:].bitcast(I32), 0)
        nc.vector.memset(tab2_plane[:].bitcast(I32), 0)
        nc.vector.memset(planes[:].rearrange("p a c -> p (a c)").bitcast(I32), 0)
        nc.vector.memset(w4_rows[:].rearrange("p a c -> p (a c)").bitcast(I32), 0)

        def load_rows(name, rows):
            raw = held(name, [P, 4, H], F32)
            nc.sync.dma_start(raw[:], rows.rearrange("(p j) c -> p j c", j=4))
            return raw

        def load_words(name, words):
            tile = held(name, [P, words.shape[1]], I32)
            nc.sync.dma_start(tile[:], words.rearrange("p c b -> p (c b)").bitcast(I32))
            return tile

        def load_row(rows, scales, first, r):
            nc.sync.dma_start(rows[first + r : P : 32, :].bitcast(I32), scales[r:16:4, :].bitcast(I32))

        def by_slot(dst, src, words):
            nc.scalar.copy(
                dst.bitcast(U32).rearrange("p (a t q w) -> p a t q w", t=SLOTS, q=16, w=words),
                src.bitcast(U32).rearrange("p (a q t w) -> p a t q w", t=SLOTS, q=16, w=words),
            )

        made = {}

        def round_weight(name, raw, slots, copy):
            grouped = held("%s_bf16_%d" % (name, slots[0]), [P, len(slots) * HALF], BF16)
            for n, t in enumerate(slots):
                copy(
                    grouped[:, n * HALF : (n + 1) * HALF].rearrange("p (q u i j) -> p q u j i", u=4, i=2, j=4),
                    raw[:].rearrange("p j (q t u i) -> p t q u j i", t=SLOTS, u=4, i=2)[:, t],
                )
            return grouped

        def quantise_weight(name, grouped, slots, after=None):
            codes = held("%s_codes_%d" % (name, slots[0]), [P, len(slots) * P], U32, after)
            scales = held("%s_scales_%d" % (name, slots[0]), [P, len(slots) * P], U8)
            nc.vector.quantize_mx(out=codes[:].bitcast(FP8X4), scales=scales[:], in_=grouped[:])
            for n, t in enumerate(slots):
                made[name, t] = (codes[:, n * P : (n + 1) * P].bitcast(FP8X4), scales[:, n * P : (n + 1) * P])

        nc.sync.dma_start(list2[:], offs2)
        nc.sync.dma_start(tab2_rows[4:P:8, :].bitcast(I32), tab2_scales[0].bitcast(I32))
        w8_raw = load_words("w8_raw", w8_words[0])
        nc.sync.dma_start(lists[:], offs)
        nc.sync.dma_start(tab_rows[0:P:4, :].bitcast(I32), tab_scales.bitcast(I32).rearrange("a q t -> q a t"))
        wd_raw = load_rows("wd_raw", wd)
        for r in range(4):
            load_row(w8_rows, w8_scales[0], W8_ROW, r)
        tab2_tile = load_words("tab2_tile", tab2_words[0])
        w4_raw = held("w4_raw", [P, 2, H // 2], I32)
        nc.sync.dma_start(w4_raw[:], w4_words.bitcast(I32).rearrange("a p c -> p a c"))

        tab2_picked = held("tab2_picked", [P, S], U8)
        nc.vector.tensor_copy(tab2_picked[:], tab2_rows[:].indirect(list2[:]))
        tab_picked = held("tab_picked", [P, S], U8)
        nc.vector.tensor_copy(tab_picked[:], tab_rows[:].indirect(lists[:]))
        for r in range(4):
            nc.sync.dma_start(
                tab2_plane[TAB2_ROW + r : P : 32, :].bitcast(I32), tab2_picked[4 + 8 * r : P : 32, :].bitcast(I32)
            )

        def move(a, r):
            nc.sync.dma_start(planes[r:P:32, a, :].bitcast(I32), tab_picked[8 * r + 4 * a : P : 32, :].bitcast(I32))

        def load_w4_row(r):
            nc.sync.dma_start(
                w4_rows[r:P:32, :, :].bitcast(I32), w4_scales[:, r:16:4, :].bitcast(I32).rearrange("a q c -> q a c")
            )

        tab0_tile = load_words("tab0_tile", tab_words[0])
        for r in range(4):
            load_w4_row(r)
        moves = [(a, r) for a in range(2) for r in range(4)]
        for a, r in moves[:2]:
            move(a, r)
        tab1_tile = load_words("tab1_tile", tab_words[1])
        for a, r in moves[2:]:
            move(a, r)
        wr0_raw = load_rows("wr0_raw", wr[0:512, :])
        wr1_raw = load_rows("wr1_raw", wr[512:1024, :])
        gains = held("gains", [P, SLOTS, 8], F32)
        shifts = held("shifts", [P, N // P], F32)
        w2_raw = held("w2_raw", [P, SLOTS, N], F32)
        with nc.allow_non_contiguous_dma(reason="one value a partition and slot"):
            for t in range(SLOTS):
                nc.sync.dma_start(w2_raw[:, t, :], w2.rearrange("(q t i) n -> t q i n", t=SLOTS, i=8)[t])
            for t in range(SLOTS):
                nc.sync.dma_start(gains[:, t, 0:1], gain.rearrange("(q t i o) -> t q i o", t=SLOTS, i=8, o=1)[t])
            nc.sync.dma_start(shifts[:], shift.rearrange("(c p) -> p c", p=P))

        every = tuple(range(SLOTS))
        pairs = ((0, 1), (2, 3))
        w8_codes = held("w8_codes", [P, H], I32)
        by_slot(w8_codes[:], w8_raw[:], 8)
        wd_grouped = round_weight("wd", wd_raw, every, nc.scalar.copy)
        w8_plane = held("w8_plane", [P, H], U8)
        by_slot(w8_plane[:], w8_rows[:], 2)

        v2 = [held("v2_0", [P, HALF], U32), held("v2_1", [P, HALF], U32)]

        def pick_depots(first, width):
            nc.vector.tensor_copy(
                v2[first // HALF][:, first % HALF : first % HALF + width],
                tab2_tile[:].bitcast(U32).indirect(list2[:, first // GROUP : (first + width) // GROUP]),
            )

        pick_depots(0, QUARTER)
        pick_depots(QUARTER, QUARTER)
        pick_depots(HALF, HALF)
        quantise_weight("wd", wd_grouped, every, after="tab2_picked")

        units = [(half, t) for half in range(2) for t in range(SLOTS)]
        depots = held("depots", [P, 2, SLOTS, HALF], F32)

        def depot_pass(sums, t, first, width):
            cols = slice(t * P, (t + 1) * P)
            inside = slice(first % HALF, first % HALF + width)
            nc.tensor.matmul_mx(
                out=sums, lhsT=w8_codes[:, cols].bitcast(FP8X4),
                lhsT_scale=w8_plane[W8_ROW:P, cols], rhs=v2[first // HALF][:, inside].bitcast(FP8X4),
                rhs_scale=tab2_plane[TAB2_ROW:P, first : first + width], start=True, stop=True,
            )

        w4_codes = held("w4_codes", [P, H], I32)
        by_slot(w4_codes[:], w4_raw[:].rearrange("p a c -> p (a c)"), 4)
        for quarter in range(2):
            for n, slots in enumerate(pairs):
                sums = bank(2 * quarter + n)
                for m, t in enumerate(slots):
                    depot_pass(sums[:, m * QUARTER : (m + 1) * QUARTER], t, quarter * QUARTER, QUARTER)
                nc.scalar.copy(
                    depots[:, 0, slots[0] : slots[0] + 2, quarter * QUARTER : (quarter + 1) * QUARTER],
                    sums[:].rearrange("p (m c) -> p m c", m=2),
                )
        w4_planes = held("w4_planes", [P, 2 * H], U8)
        by_slot(w4_planes[:], w4_rows[:].rearrange("p a c -> p (a c)"), 2)
        for t in every:
            sums = bank(SLOTS + t)
            depot_pass(sums[:], t, HALF, HALF)
            nc.scalar.copy(depots[:, 1, t, :], sums[:])
        v = {(a, half): [] for a in range(2) for half in range(2)}

        def pick_legs(a, first, width, after=None):
            picked = held("v%d_%d" % (a, first), [P, width], U32, after)
            cols = slice(first // GROUP, (first + width) // GROUP)
            nc.vector.tensor_copy(picked[:], (tab0_tile, tab1_tile)[a][:].bitcast(U32).indirect(lists[:, cols]))
            v[a, first // HALF].append((first, width, picked))

        pick_legs(0, 0, HALF)
        pick_legs(0, HALF, QUARTER)
        pick_legs(1, 0, QUARTER)
        pick_legs(1, QUARTER, QUARTER)
        pick_legs(1, HALF, HALF)
        pick_legs(0, HALF + QUARTER, QUARTER, after="tab_picked")

        def leg_pass(sums, codes, scales, half, a, start, stop):
            for n, (first, width, picked) in enumerate(v[a, half]):
                nc.tensor.matmul_mx(
                    out=sums[:, first % HALF : first % HALF + width], lhsT=codes, lhsT_scale=scales,
                    rhs=picked[:].bitcast(FP8X4), rhs_scale=planes[:, a, first : first + width],
                    start=start and n == 0, stop=stop and n + 1 == len(v[a, half]),
                )

        sines = held("sines", [P, SLOTS, S], F32)

        def w4_operand(t, a):
            at = a * H + t * P
            return w4_codes[:, at // 2 : (at + P) // 2].bitcast(FP4X4), w4_planes[:, at : at + P]

        def window_pass(sums, weight, moving, plane, first, width, start=False, stop=False):
            nc.tensor.matmul_mx(
                out=sums, lhsT=weight[0], lhsT_scale=weight[1], rhs=moving.bitcast(FP8X4),
                rhs_scale=plane[:, first : first + width], start=start, stop=stop,
            )

        early = {(quarter, n): bank(2 * quarter + n) for quarter in range(2) for n in range(2)}
        for (quarter, n), sums in early.items():
            cols = slice(quarter * QUARTER, (quarter + 1) * QUARTER)
            for m, t in enumerate(pairs[n]):
                window_pass(sums[:, m * QUARTER : (m + 1) * QUARTER], made["wd", t], v2[0][:, cols],
                            tab2_plane[TAB2_ROW:P, :], quarter * QUARTER, QUARTER, start=m == 0)
        totals = [bank(SLOTS + t) for t in every]

        def wd_pass(t, start):
            window_pass(totals[t][:], made["wd", t], v2[1][:], tab2_plane[TAB2_ROW:P, :], HALF, HALF, start=start)

        for t in pairs[0]:
            wd_pass(t, True)
        for (quarter, n), sums in early.items():
            cols = slice(quarter * QUARTER, (quarter + 1) * QUARTER)
            for a, moving in enumerate((v[0, 0][0][2][:, cols], v[1, 0][quarter][2][:])):
                for m, t in enumerate(pairs[n]):
                    window_pass(sums[:, m * QUARTER : (m + 1) * QUARTER], w4_operand(t, a), moving,
                                planes[:, a, :], quarter * QUARTER, QUARTER, stop=a == 1 and m == 1)
            nc.scalar.activation(
                sines[:, pairs[n][0] : pairs[n][0] + 2, cols], sums[:].rearrange("p (m c) -> p m c", m=2), ACT.Sin
            )
        for t in every[:3]:
            leg_pass(totals[t], *w4_operand(t, 1), 1, 1, t in pairs[1], False)
        for t in every:
            if t == 3:
                leg_pass(totals[t], *w4_operand(t, 1), 1, 1, True, False)
            if t in pairs[1]:
                wd_pass(t, False)
            leg_pass(totals[t], *w4_operand(t, 0), 1, 0, False, True)
            nc.scalar.activation(sines[:, t, span(1)], totals[t][:], ACT.Sin)

        w2_grouped = held("w2_bf16", [P, SLOTS * N], BF16)
        nc.scalar.copy(
            w2_grouped[:].rearrange("p (n i t) -> p n t i", t=SLOTS, i=2),
            w2_raw[:].rearrange("p t (n i) -> p n t i", i=2),
        )

        for name, raw in (("wr0", wr0_raw), ("wr1", wr1_raw)):
            grouped = [round_weight(name, raw, slots, nc.vector.tensor_copy) for slots in pairs]
            for n, slots in enumerate(pairs):
                quantise_weight(name, grouped[n], slots)

        routes = {unit: bank(n) for n, unit in enumerate(units)}

        opened = set()

        def route_pass(half, t, a):
            codes, scales = made["wr%d" % a, t]
            leg_pass(routes[half, t], codes, scales, half, a, (half, t) not in opened, (half, t) in opened)
            opened.add((half, t))

        diffs = [held("diff%d" % half, [P, SLOTS, HALF], F32) for half in range(2)]
        for half, t in units:
            route_pass(half, t, 1 if (half, t) in units[1:] else 0)
            route_pass(half, t, 0 if (half, t) in units[1:] else 1)
            nc.vector.tensor_tensor(diffs[half][:, t, :], routes[half, t][:], depots[:, half, t, :], ALU.subtract)

        scaled = held("scaled", [P, SLOTS, S], F32, after="wr1_bf16_2")
        for t in range(SLOTS):
            nc.gpsimd.tensor_scalar(scaled[:, t, :], sines[:, t, :], gains[:, t, 0:1], 0.0, ALU.mult, ALU.add)

        first_half = held("cosine0", [P, 2, SLOTS, HALF // 2], F32)
        cosines = {n * 256: first_half[:, n] for n in range(2)}
        parts = [
            (first_half[:, :, t, :], diffs[0][:, t, :].rearrange("p (n c) -> p n c", n=2)) for t in range(2)
        ]
        parts.extend((first_half[:, n, 2:SLOTS, :], diffs[0][:, 2:SLOTS, n * 256 : (n + 1) * 256]) for n in range(2))
        for at in range(0, HALF, P):
            cosines[HALF + at] = held("cosine_%d" % at, [P, SLOTS, P], F32)[:]
            parts.append((cosines[HALF + at], diffs[1][:, :, at : at + P]))

        def size_of(n):
            size = held("size%d" % n, list(parts[n][1].shape), F32)
            nc.scalar.activation(size[:], parts[n][1], ACT.Abs)
            return size

        sizes = []
        for group in ((0, 1, 2), (3, 4), (5, 6, 7)):
            for n in group:
                while len(sizes) <= min(n + 1, group[-1]):
                    sizes.append(size_of(len(sizes)))
                nc.scalar.activation(parts[n][0], sizes[n][:], ACT.Sin, bias=math.pi / 2, scale=-1.0)

        h_grouped = [held("h_bf16_%d" % at, [P, SLOTS * width], BF16) for at, width in PIECES]

        def products(n, at):
            width = cosines[at].shape[2]
            first = SLOTS * (at - PIECES[n][0])
            nc.vector.tensor_tensor(
                h_grouped[n][:, first : first + SLOTS * width].rearrange("p (c i t) -> p c t i", t=SLOTS, i=2),
                cosines[at].rearrange("p t (c i) -> p c t i", i=2),
                scaled[:, :, at : at + width].rearrange("p t (c i) -> p c t i", i=2),
                ALU.mult,
            )

        def quantise_h(at, width, h_grouped):
            h_codes = held("h_codes_%d" % at, [P, width], U32)
            h_scales = held("h_scales_%d" % at, [P, width], U8)
            nc.vector.quantize_mx(out=h_codes[:].bitcast(FP8X4), scales=h_scales[:], in_=h_grouped[:])
            return h_codes, h_scales

        out_view = out.rearrange("(c p) j -> p c j", p=P)

        def scores_of(at, width, h, numbers, on_vector_rows):
            result = held("result_%d" % at, [P, N // P, width], F32)
            for c in range(N // P):
                rows = slice(c * P, (c + 1) * P)
                scores = bank(numbers[c])
                nc.tensor.matmul_mx(
                    out=scores[:, 0:width], lhsT=w2_codes[:, rows].bitcast(FP8X4), lhsT_scale=w2_scales[:, rows],
                    rhs=h[0][:].bitcast(FP8X4), rhs_scale=h[1][:], start=True, stop=True,
                )
                if c in on_vector_rows:
                    nc.vector.tensor_scalar_add(result[:, c, :], scores[:, 0:width], shifts[:, c : c + 1])
                else:
                    nc.scalar.activation(result[:, c, :], scores[:, 0:width], ACT.Identity, bias=shifts[:, c : c + 1])
                if width == HALF:
                    nc.sync.dma_start(out_view[:, c, at : at + width], result[:, c, :])
            if width < HALF:
                nc.sync.dma_start(out_view[:, :, at : at + width], result[:])

        w2_codes = held("w2_codes", [P, N], U32, after="size2")
        w2_scales = held("w2_scales", [P, N], U8)
        nc.vector.quantize_mx(out=w2_codes[:].bitcast(FP8X4), scales=w2_scales[:], in_=w2_grouped[:])
        h_of = []
        for n, (first, width) in enumerate(PIECES):
            for m, at in enumerate(at for at in cosines if first <= at < first + width):
                products(n, at)
                if m == 0 and n > 0:
                    h_of.append(quantise_h(*PIECES[n - 1], h_grouped[n - 1]))
        h_of.append(quantise_h(*PIECES[-1], h_grouped[-1]))
        for n, (at, width) in enumerate(PIECES):
            scores_of(at, width, h_of[n], (2 * n, 2 * n + 1), (1,) if n + 2 >= len(PIECES) else ())
